import numpy as np, ml_dtypes
CORES = [6,15,38,47]
N = 4
import mx_ref
BF = ml_dtypes.bfloat16
def gentries(a):
    return np.ascontiguousarray(a.reshape(8, 16, -1).transpose(0, 2, 1)).reshape(8, -1)
def gtable(e):
    e = np.asarray(e); return np.ascontiguousarray(e.reshape(8, -1, 16).transpose(0, 2, 1)).reshape(128, -1).astype(np.int32)
def gcols(t, e):
    v = np.concatenate([t.reshape(8, 16, -1, 4), np.zeros((8, 16, 1, 4), BF)], axis=2)
    return np.ascontiguousarray(np.stack([v[g][:, e[g]] for g in range(8)])).reshape(128, -1)
def tile(rs):
    return np.stack(rs, axis=2).reshape(128, -1).astype(BF)
def pick(q, e):
    c = np.concatenate([q[0].reshape(128, -1, 4), np.zeros((128, 1, 4), np.uint8)], axis=1); s = np.concatenate([q[1], np.ones((16, 1), np.uint8)], axis=1)
    return (np.ascontiguousarray(c[:, e].reshape(128, -1)), np.ascontiguousarray(s[:, e]))
def join(*qs):
    return (np.concatenate([q[0] for q in qs], axis=1), np.concatenate([q[1] for q in qs], axis=1))
def put(q, e, v):
    c, s = q[0].reshape(128, -1, 4).copy(), q[1].copy(); c[:, e] = v[0].reshape(128, -1, 4); s[:, e] = v[1]
    return (c.reshape(128, -1), s)
def pk(c, s):
    return (np.ascontiguousarray(c), mx_ref.live(s))
def emit(q):
    return q[0], q[1]
def packed(v, rng):
    q = [mx_ref.quantize(np.ascontiguousarray(v[r])) for r in range(N)]
    return np.stack([a for a, b in q]), np.stack([mx_ref.plane(b, rng) for a, b in q])
def values_of_codes():
    e, c = np.zeros((128, 128, 4), np.float32), np.zeros((128, 2, 4), np.uint8)
    e[np.arange(128), np.arange(128), 0] = 1
    c[:127, :, 0] = np.arange(256).reshape(2, 128).T[:127]
    return mx_ref.matmul(mx_ref.quantize(e.reshape(128, 512).astype(BF)), (c.reshape(128, 8), np.full((16, 2), 127, np.uint8))).T.reshape(-1).astype(np.float64)
CODE_VALUE, SCALE_VALUE = values_of_codes(), 2.0 ** (np.arange(256) - 127.0)
def decode(q):
    return (CODE_VALUE[q[0]].reshape(16, 8, -1, 4) * SCALE_VALUE[q[1]][:, None, :, None] + 0.0).reshape(128, -1).astype(np.float32)
def f(rng, *shape):
    return mx_ref.flush((rng.standard_normal(shape, dtype=np.float32) * np.exp2(rng.integers(-2, 3, shape[:-1] + (1,)))).astype(BF))
def wide(rng, *shape, cols=0):
    v = rng.standard_normal(shape, dtype=np.float32) * np.exp2(rng.integers(-12, 13, shape)).astype(np.float32)
    if cols: v *= np.repeat(np.exp2(rng.integers(-cols, cols + 1, shape[:-2] + (1, shape[-1] // 4))) * (rng.random(shape[:-2] + (1, shape[-1] // 4)) > 0.0625), 4, axis=-1).astype(np.float32)
    return mx_ref.flush(v.astype(BF))
C, J = 320, 128
STEP = [1, 2, 3]
def big(v):
    v = v.astype(np.float32)
    v[np.abs(v) < np.float32(2.0 ** -12)] = 0
    return v.astype(BF)
def numbers_of(rng):
    return {"x": big(f(rng, N, 128, 4 * C)), "u": np.array(f(rng, N, 128, 512)), "v": np.array(f(rng, N, 128, 512))}
def maps_of(rng):
    return rng.permuted(np.tile(np.arange(C), (N, 8, 1)), axis=2)
def arrivals(rng, m, right=0.75):
    return np.where(rng.random((N, 8, 4, C)) < right, m[:, :, None], rng.integers(0, C, (N, 8, 4, C)))
def lists(m, a):
    return {"mp": np.stack([gtable(m[r]) for r in range(N)]), "ar": np.stack([gtable(a[r].reshape(8, 4 * C)) for r in range(N)])}
def layers(rng):
    return big(f(rng, N, 128, 2048)).reshape(N, 128, 4, 128, 4)
def weights(rng, w):
    c, s = packed(np.ascontiguousarray(w).reshape(N, 128, 2048), rng)
    return {"wc": c, "ws": s}
def setup_inputs(rng):
    m = maps_of(rng)
    return {**numbers_of(rng), **lists(m, arrivals(rng, m)), **weights(rng, layers(rng))}
def setup_inputs_ties(rng):
    d = numbers_of(rng)
    o = rng.permutation(N)
    x = d["x"].reshape(N, 128, C, 4)
    x[:, :8, :, :2] = rng.integers(0, 3, (N, 8, C, 2)).astype(np.float32).astype(BF)
    x[:, 8:16, :, :2] = 1
    x[o[0], :16, :, :2] = 0
    u = d["u"].reshape(N, 128, 128, 4)
    u[:, :, ::16] = 0
    u[:, :, 1::16] = 0
    w = layers(rng)
    for e in range(2):
        for p in range(16):
            w[:, :, e, p] = 0
            w[:, p, e, p, e] = 32
        for g in range(8):
            for h in range(0, 16, 8):
                w[:, :, e, 16 * g + h] = 0
                w[:, g + h, e, 16 * g + h, e] = 32
                u[:, 16 * g + h, 16 * g + e, e] = 1.0 if h == 0 else -1.0
    m = maps_of(rng)
    for r in range(N): m[r, 1:] = rng.permutation(C)[:8][rng.integers(0, 8, (7, C))]
    one = int(o[1])
    goal = int(m[one, 1, 0])
    m[one, 1] = goal
    right = np.array([1.0, 0.75] + [0.25] * 6)[:, None, None]
    a = arrivals(rng, m, right)
    a[one, 1] = m[one, 1]
    a[one, 2, :, goal] = (m[one, 2, goal] + 1 + np.arange(4)) % C
    x[one, 2, m[one, 0, :J], :2] = 0
    x[one, 2, m[one, 0, 0], :2] = 2
    return {"x": x.reshape(N, 128, 4 * C), "u": u.reshape(N, 128, 512), "v": d["v"], **lists(m, a), **weights(rng, w)}
def setup_inputs_near(rng):
    d = numbers_of(rng)
    x = d["x"].reshape(N, 128, C, 4)
    x.reshape(N, 8, 16, C, 4)[:, :, 8:] = 1
    u = d["u"].reshape(N, 128, 128, 4)
    u[:, :, ::16] = 0
    u[:, :, 1::16] = 0
    o = rng.permutation(N) % 4
    m = maps_of(rng)
    for r in range(N):
        t = np.array([[9.0, 8.0], [11.0, 10.0], [10.0, 9.0]])[rng.integers(0, 3, (8, C, 2))].reshape(8, C, 4) * 0.125
        far = m[r, 0, rng.permutation(J)[:12]]
        if o[r] % 2 == 0: t = t * 2.0 ** -12
        if o[r] < 2:
            t[:, far[:8]] *= 2.0 ** 25 if o[r] == 0 else 2.0 ** 13
            x[r, 15] = 0
            x[r, 15, far[8:], 0] = 1
        x[r, :8] = t.astype(np.float32).astype(BF)
        k = 2.0 ** -30 if o[r] % 2 == 0 else 1.0
        for h in range(0, 128, 16):
            for b in range(2):
                u[r, h + 8 + 2 * b, h + b, 0] = 1.125 * k
                u[r, h + 9 + 2 * b, h + b, 0] = -1.25 * k
                if o[r] < 2: u[r, 16, h + b, 0] = 2.0 ** 30
    w = layers(rng)
    w.reshape(N, 128, 4, 8, 16, 4)[:, :, :, :, 8:] = 0
    w[:, :, :, :8] = 0
    w[:, :, 0, 16] = 0
    w[:, 15, 0, 16, 0] = 32
    for g in range(8):
        for i in range(4):
            w[:, g, i, g, i] = 32
            w[:, g, 0, 16 * g + 8 + i, i] = 2.0 ** -13
    return {"x": x.reshape(N, 128, 4 * C), "u": u.reshape(N, 128, 512), "v": d["v"], **lists(m, arrivals(rng, m)), **weights(rng, w)}
def setup_inputs_ends(rng):
    o = rng.permutation(N) % 4
    x = rng.choice([-1.0, 1.0], (N, 128, 4 * C))
    u = rng.choice([-1.0, 1.0], (N, 128, 128, 4))
    v = rng.choice([-1.0, 1.0], (N, 128, 512))
    m, a = np.zeros((N, 8, C), int), np.full((N, 8, 4, C), C - 1)
    for r in range(N):
        if o[r] == 0:
            x[r] = 1.0
            u[r] = u[r, :1, :, :1].copy()
        if o[r] % 2 == 0: m[r] = C - 1
        if o[r] == 2: a[r, :, ::3] = 0
        if o[r] == 3:
            x[r] = -1.0
            m[r] = np.arange(C)
            a[r] = np.arange(C)[::-1]
        x[r] *= 2.0 ** -12 if o[r] == 2 else 2.0 ** 14
        u[r] *= 2.0 ** -30 if o[r] == 2 else 2.0 ** 30
        v[r] *= 2.0 ** -30 if o[r] == 2 else 2.0 ** 30
    w = np.full((N, 128, 4, 128, 4), 4.0)
    w[:, :, :3, :, :2] = 8.0
    w[:, :, :3, :, 2:] = 0.0
    w[:, :, 3] *= rng.choice([-1.0, 1.0], (N, 128, 128, 4))
    return {"x": x.astype(BF), "u": u.reshape(N, 128, 512).astype(BF), "v": v.astype(BF), **lists(m, a), **weights(rng, w.astype(BF))}
def setup_inputs_blocks(rng):
    d = numbers_of(rng)
    s = (1.0 + (2 * rng.integers(0, 64, (N, 16, 8, C, 4)) + 1) * 2.0 ** -7) * np.exp2(-rng.integers(8, 15, (N, 16, 8, C, 4)).astype(np.float64))
    top = np.arange(32).reshape(8, 1, 4) == rng.integers(0, 32, (N, 16, C))[:, :, None, :, None]
    x = np.where(top, 1.96875, s) * rng.choice([-1.0, 1.0], (N, 16, 8, C, 4)) * np.exp2(rng.integers(2, 8, (N, 16, 1, C, 1)).astype(np.float64))
    m = maps_of(rng)
    return {"x": x.reshape(N, 128, 4 * C).astype(np.float32).astype(BF), "u": d["u"], "v": d["v"], **lists(m, arrivals(rng, m)), **weights(rng, layers(rng))}
def setup_inputs_spread(rng):
    d = setup_inputs(rng)
    d["x"] = big(wide(rng, N, 128, 4 * C, cols=4).astype(np.float32) * np.float32(2.0 ** -5))
    return d
def check_inputs(d):
    b = []
    for k, lo, hi in (("x", 2.0 ** -12, 2.0 ** 14), ("u", 2.0 ** -30, 2.0 ** 30), ("v", 2.0 ** -30, 2.0 ** 30)):
        a = np.abs(d[k].astype(np.float32))
        if not (np.isfinite(a).all() and ((a == 0) | (a >= lo) & (a <= hi)).all()): b.append("a value of " + k)
    for k in ("mp", "ar"):
        if not ((d[k] >= 0) & (d[k] < C)).all(): b.append("an entry of " + k)
    none, least, most = [emit(mx_ref.quantize(np.full((128, 16), k, np.float32).astype(BF)))[1][0, 0] for k in (0.0, 2.0 ** -30, 2.0 ** 30)]
    for r in range(N):
        if ((d["wc"][r] == 0x7F) | (d["wc"][r] == 0xFF)).any(): b.append("wc: a code that is no number")
        s = mx_ref.live(d["ws"][r])
        if ((s != none) & ((s < least) | (s > most))).any(): b.append("ws: a scale out of range")
        else:
            a = np.abs(decode(pk(d["wc"][r], d["ws"][r]))).reshape(128, 512, 4)
            if (np.sum(a, axis=(0, 2), dtype=np.float64) > 2048).any(): b.append("a column of W")
    return b
def chains(m):
    e = [np.arange(J)]
    for g in range(8): e.append(m[g, e[g]])
    return np.stack(e[:8]), np.stack(e[1:])
def reference(x, u, v, mp, ar, wc, ws):
    qu = [mx_ref.quantize(u[r]) for r in range(N)]
    lay = [pk(wc[r], ws[r]) for r in range(N)]
    now = [x[r] for r in range(N)]
    maps = np.stack([gentries(mp[r]) for r in range(N)])
    cand = np.stack([gentries(ar[r]).reshape(8, 4, C) for r in range(N)])
    grp = np.arange(8)
    for h in STEP:
        for r in range(N):
            donor = (r + h) % N
            old = decode(mx_ref.quantize(now[r])).astype(BF)
            e, l = chains(maps[r])
            m = mx_ref.quantize(gcols(old, l))
            q = mx_ref.quantize(tile([np.maximum(mx_ref.matmul(pick(lay[donor], np.arange(128 * b, 128 * b + 128)), m), np.float32(0.0)) * np.float32(0.03125) for b in range(4)]))
            s = mx_ref.matmul(qu[r], q)
            a = cand[r][grp[:, None], 2 * (s[::16] > 0) + (s[1::16] > 0), e]
            wrong = a != l
            first = np.argmax(wrong, axis=0)
            for j in range(J - 1, -1, -1):
                g = first[j]
                if wrong[g, j]: maps[r, g, e[g, j]] = a[g, j]
            l = chains(maps[r])[1]
            n = np.tile(J + np.arange(C), (8, 1))
            for j in range(J - 1, -1, -1): n[grp, l[:, j]] = j
            other = gcols(np.concatenate([decode(q).astype(BF), old], axis=1), n)
            now[r] = ((old.astype(np.float32) + other.astype(np.float32)) * np.float32(0.5)).astype(BF)
    y, fo = np.zeros((N, 128, C), np.float32), np.zeros((N, 8, C), np.float32)
    oc, osc = np.zeros((N, 128, 4 * C), np.uint8), np.zeros((N, 16, C), np.uint8)
    for r in range(N):
        q = mx_ref.quantize(now[r])
        y[r] = mx_ref.matmul(mx_ref.quantize(v[r]), q)
        fo[r] = maps[r]
        oc[r], osc[r] = emit(q)
    return {"y": y, "fo": fo, "oc": oc, "osc": osc}

@@ -1,0 +1,463 @@
+from concourse.mybir import dt, AluOpType as Op, AxisListType, ActivationFunctionType as Act
+
+F32, BF, I32, U16, MXC, U8 = "float32", "bfloat16", "int32", "uint16", "float8_e4m3fn_x4", "uint8"
+SCRATCH = {}
+for _n, _w, _t in (
+        ("xi", 1280, BF), ("ui", 512, BF), ("vi", 512, BF), ("mwi", 192, I32), ("mwf", 192, F32), ("cwi", 1280, I32), ("cwf", 1280, F32),
+        ("wcs", 512, MXC), ("wps", 512, U8), ("wdc", 512, MXC), ("wdp", 512, U8),
+        ("pi", 16, I32), ("pf", 32, F32), ("nat", 320, F32), ("nat512", 320, F32), ("ci", 160, I32), ("cj", 160, I32), ("cf", 192, F32), ("k20", 32, I32),
+        ("tril", 128, BF), ("idb", 128, BF), ("mod", 128, BF), ("m8", 8, BF),
+        ("l0", 4, U16), ("lr", 8, U16), ("lr7", 8, U16), ("ly", 20, U16), ("pk", 4, U16), ("la", 4, U16),
+        ("zt", 512, BF), ("ce", 2048, BF), ("ca", 1536, BF), ("cb", 1536, BF),
+        ("qe", 512, MXC), ("se", 512, U8), ("qa", 384, MXC), ("sa", 384, U8), ("qb", 384, MXC), ("sb", 384, U8),
+        ("qu", 128, MXC), ("su", 128, U8), ("qv", 128, MXC), ("sv", 128, U8), ("fs", 192, F32),
+        ("yb", 2560, F32), ("fw", 2880, F32), ("ox", 512, F32), ("o7", 128, F32), ("tt", 448, F32), ("of", 40, U16),
+        ("rl", 128, F32), ("tl", 256, F32), ("lw", 16, U16), ("rle", 128, F32), ("te", 128, F32), ("ew", 32, I32),
+        ("e1", 32, I32), ("e2", 32, I32), ("e3", 32, I32), ("ec", 32, I32), ("el", 8, U16), ("lc", 32, U16),
+        ("rf", 768, F32), ("cp", 48, F32), ("ne", 32, F32), ("sk", 32, F32), ("pp", 32, F32), ("kk", 128, F32), ("dd", 1024, F32), ("fl", 8, U16),
+        ("sg", 32, F32), ("xx", 32, F32), ("yy", 36, F32), ("qd", 8, I32), ("b1", 1536, BF), ("b2", 512, BF),
+        ("qk", 384, MXC), ("sk1", 384, U8), ("ql", 128, MXC), ("sl", 128, U8), ("kt", 128, F32), ("eq", 128, F32), ("ofs", 8, U16), ("va", 128, F32),
+        ("fh", 1280, BF), ("dh", 512, BF), ("fg", 512, F32), ("nt", 512, BF), ("qn", 128, MXC), ("sn", 128, U8), ("mt", 512, BF), ("ht", 512, BF),
+        ("xt", 1792, BF), ("qx", 320, MXC), ("sx", 320, U8), ("xl", 32, U16), ("yo", 320, F32),
+        ("qm0", 128, MXC), ("sm0", 128, U8), ("qm1", 128, MXC), ("sm1", 128, U8), ("qm2", 128, MXC), ("sm2", 128, U8),
+        ("qh0", 128, MXC), ("sh0", 128, U8), ("qh1", 128, MXC), ("sh1", 128, U8), ("qh2", 128, MXC), ("sh2", 128, U8),
+        ("mc0", 128, MXC), ("mp_0", 128, U8), ("mc1", 128, MXC), ("mp_1", 128, U8), ("hc0", 128, MXC), ("hp0", 128, U8), ("hc1", 128, MXC), ("hp1", 128, U8)):
+    SCRATCH[_n] = ("sbuf", [128, _w], _t)
+for _n in range(8):
+    SCRATCH["p%d" % _n] = ("psum", [128, 512], F32)
+SMALL = {n: 8 * k for k, n in enumerate(("jw", "jd", "sc", "nq", "dg", "kf", "lo", "kw", "dj", "t1", "t2", "rq", "fi", "wn", "xd", "nl", "xe"))}
+SEMAPHORES = ["v", "s", "t", "p", "dx", "du", "dv", "dw", "da", "dc", "do", "aw", "am0", "am1", "ah0", "ah1", "ls"] + ["dm%d" % _n for _n in range(8)]
+STEP = [1, 2, 3]
+ORDER_TEXT = """
+1 61 93 120 24 49 94 15 0 52 2 110 112 3-4 97 113 5-6 115 7 41 116 22 8 117-118 30 10 111 11-12 114 13-14 46 63 119 9 17-19 121 20-21 122 98 126
+23 26 35 28 141 123 25 32 124 27 34 130 29 36 128 31 38 125 131 37 42 134 39 44 127 16 48 234 33 50 135 47 54 136 57 56 51 60 53 62 55 58 95 59
+40 43 64 99 45 145 132 75 139 66 146 133 73 137 67 129 68-69 151 140 71-72 152 74 157 76 78-81 163 100 147 82 158 77 65 90 153 70 91 83-84 148
+164 85-87 149 88 159 89 92 101 150 169 154 170 155 165 156 175 160 176 102 161 171 162 181 166 182 167 177 168 96 187 172 188 183 106 105 173
+103 193 108 192 104 189 194 109 174 195 138 198 178 107 196 179-180 199 197 184-185 200 256 186 202 190 201 235 203 191 257 291 204 258 237 236*
+238* 239 268 240 259 293 241 233 294 242-243 292 260-265 269 266-267 142 272 270 273 227 223 271 211 205-206 208 279 209 274 210 275 213 277 144
+278 280-281 276 247 244 251* 245-246 248 249* 229 250 226 252 231 230 253 216 220 212 143 254-255 283 282 284-286 289 217 219 288 214 287 207
+225 215 290 221 232 218 228 222 224 295 340 296 337 297 344 338 298 339 341 299-300 343 301 342 302 316 303 322 315 313* 304-305* 311 306* 314*
+307 312 317 308-309 328 310 318 323 319-320 324 329 321* 330 325 332 326 331 327 333-336 345-364 368 365 369 366-367 370-371 392 372 389 390* 391
+379-380 377 442 373-374 381 378* 382 376 388 375* 387 384 383 386 385 393 403 405-406 404 407 432 411 409 395 415* 410 413* 408 414* 412* 416 433
+417 394 434 396 435-436 418 437 439 443 438 397 440 419 398 441 400 399 444 447* 445 446* 465 454 452 448 450 449 451 401 455 466 453 402 467-469
+421 420 425* 422 424 423 426 471 427 462 428 472 475 463 456 429 457 473 458-461 476 470 430 464 477* 479 431 474* 480-481* 478* 482 525 483 524
+484 529 526 485 527 530 486-487 528 488 531 489 503 490 509 502 493* 491-492* 498 501* 494 499-500* 495-496 504 497 515 505 510 506-507 511 516
+508* 517 512 519 513 518 514 520-523 532-551 555 552 613 553-554 614 556 615 557 617 616 623 619 559 577 620 558 578 618 621 564 567 624 566 565
+579 560-562 575-576 574 573 563* 572 568-571 622 580 625* 626 627* 628 590 629-630 591 632-634 592 635-636 631 593 582 594 583 581 598 597 584
+602* 595 601* 596 599-600* 585 603 586-587 605 646 604 609* 606-607 610* 608 637 611* 638-642 612 643-644 663 645 664-670 684 671 690 682 672*
+680* 673* 679 683* 681* 674* 685 675 686 696 687 647 676-678 688 691 697 689* 698 692 700 699 693 588 694 589 648 695 701-704 721 718 713-715 722
+716 723 717 719 724 720 725-727 649 728-734 650 735 651 736 652 737 655 738 653 739 656 654 740 744 705 741 658 742 706 745 657 743 708 746 712*
+765 748 707 747 766 711* 753 756 767 755 754 768 763 762 749 752* 751 764 750* 761 771 709 757 759-760 758 710 772 660* 662 770 769 661* 773 659
+774 779 775 780 783 776 781 784 777-778 785 782 786-789 791-793 790 794* 795
+"""
+
+
+def program(g, core, T, topo):
+    r = T.rank_of(core)
+    N = len(T.cores)
+    Q = {"v": g.vector, "s": g.scalar, "t": g.tensor, "p": g, "y": g.sync}
+    ops = []
+
+    def op(q, call, reads, writes, acc=False):
+        ops.append([q, call, reads, writes, "acc" if acc else "op", None, 0])
+
+    def dma(q, sem, out, in_, reads, writes, batch=0):
+        ops.append([q, lambda _: Q[q].dma_start(out, in_), reads, writes, "dma", sem, batch])
+
+    def send(pairs, dst, sem, reads):
+        rid, pid, _ = topo.addr(dst)
+        mask, n = topo.mask(core, dst), len(topo.engines(core, dst))
+        for out, in_ in pairs:
+            ops.append(["p", lambda _, out=out, in_=in_: g.remote_dma(out, in_, T.sem[sem], T.sem.ls, pid, rid, mask), reads, ["sent." + sem], "send", sem, n])
+
+    def arrives(sem, src, writes):
+        ops.append(["-", None, ["sent." + sem], writes, "arrival", sem, 2 * len(topo.engines(src, core))])
+
+    V, S = g.vector, g.scalar
+    B8 = dt.uint8
+
+    def ts(out, in0, s1, op0, reads, writes, s2=None, op1=None):
+        if op1 is None:
+            op("v", lambda _: V.tensor_scalar(out, in0, s1, None, op0), reads, writes)
+        else:
+            op("v", lambda _: V.tensor_scalar(out, in0, s1, s2, op0, op1), reads, writes)
+
+    def tt(out, a, b, o, reads, writes):
+        op("v", lambda _: V.tensor_tensor(out, a, b, o), reads, writes)
+
+    def cp(out, in_, reads, writes):
+        op("v", lambda _: V.tensor_copy(out, in_), reads, writes)
+
+    def tr(out, in_, reads, writes):
+        op("v", lambda _: V.transpose(out, in_), reads, writes)
+
+    def times(out, in_, reads, writes, scale, q="sv"):
+        op(q, lambda e: S.activation(out, in_, Act.Copy, scale=scale) if e == "s" else V.tensor_scalar(out, in_, scale, None, Op.mult), reads, writes)
+
+    def red(out, in_, o, reads, writes, **kw):
+        op("v", lambda _: V.tensor_reduce(out, in_, AxisListType.X, o, **kw), reads, writes)
+
+    def fill(ap, val, writes):
+        op("v", lambda _: V.memset(ap, val), [], writes)
+
+    def quant(q, s, t, reads, writes):
+        op("v", lambda _: V.quantize_mx(q, s, t), reads, writes)
+
+    def mm(out, l, ls, m, ms, reads, writes, start=True, stop=True):
+        op("t", lambda _: g.tensor.matmul_mx(out, l, ls, m, ms, start, stop), reads, writes, acc=not start)
+
+    def iota(out, pattern, base, cm, writes, flt):
+        if flt:
+            op("p", lambda _: g.iota(out, pattern, base, cm, allow_small_or_imprecise_dtypes=True), [], writes)
+        else:
+            op("p", lambda _: g.iota(out, pattern, base, cm), [], writes)
+
+    def select(out, in_, pattern, cmp, fill_, base, cm, reads, writes):
+        op("p", lambda _: g.affine_select(out, in_, pattern, cmp, fill_, base, cm), reads, writes)
+
+    def col(name, k, n=1):
+        return T[name][:, k:k + n]
+
+    def sm(name, n=8):
+        return T.fs[:, SMALL[name]:SMALL[name] + n]
+
+    def sm1(name, k):
+        return T.fs[:, SMALL[name] + k:SMALL[name] + k + 1]
+
+    def blk(name, t, w=128):
+        return T[name][:, w * t:w * t + w]
+
+    PS = [T["p%d" % k] for k in range(8)]
+    M4, H4, N4, X4 = [["%s%d" % (n, t) for t in range(4)] for n in "MHNX"]
+    OX = ["ox%d" % k for k in range(8)]
+    FWALL = ["fw%d" % s for s in range(8)]
+    pf = lambda k: T.pf[:, k:k + 1]
+
+    for m in range(8):
+        for q in range(8):
+            dma("ys"[q % 2], "dm%d" % m, T.mwi[16 * q:16 * q + 16, 24 * m:24 * m + 20], T.mp[16 * m:16 * m + 16, :], [], ["mwi%d.%d" % (m, q)])
+        if m == 1:
+            dma("y", "dx", T.xi[:], T.x[:], [], ["xi"])
+    dma("y", "dw", T.wcs[:].bitcast(B8), T.wc[:], [], ["wcs"])
+    dma("y", "dw", T.wps[:], T.ws[:], [], ["wps"])
+    for i in range(16):
+        dma("y", "da", T.cwi[i:128:16, :], T.ar[:], [], ["cwi%d" % i])
+    for m in range(8):
+        dma("y", "du", T.ui[:, 8 * m:8 * m + 8], T.u[:, 64 * m:64 * m + 8], [], ["ui%d" % m])
+    dma("y", "du", T.ui[:, 64:512], T.u[:, 0:448], [], ["ui8"])
+    dma("y", "dv", T.vi[:], T.v[:], [], ["vi"])
+
+    iota(col("pi", 9), [[0, 1]], 0, 1, ["pi9"], False)
+    iota(col("cf", 0, 20), [[2, 10], [0, 2]], 0, 0, ["cf0"], True)
+    iota(col("cf", 32, 8), [[16, 4], [64, 2]], 0, 0, ["cf1"], True)
+    iota(col("cf", 64, 64), [[32, 2], [64, 2], [1, 16]], 0, 0, ["cf4"], True)
+    iota(T.nat[:], [[1, 320]], 0, 0, ["nat"], True)
+    iota(T.zt[:], [[0, 512]], 0, 0, ["zt"], True)
+    for b in range(4):
+        select(blk("ce", b, 512), T.zt[:], [[-1, 512]], Op.not_equal, 1.0, b, 4, ["zt"], ["ce%d" % b])
+    iota(col("ci", 0, 128), [[-1, 128]], 128, 1, ["cia"], False)
+    iota(col("ci", 128, 8), [[-16, 8]], 0, 1, ["cib"], False)
+    iota(col("cf", 56, 2), [[-16, 2]], 16, 0, ["cf3"], True)
+    iota(T.k20[:], [[20, 4], [0, 8]], 0, 0, ["k20"], False)
+    iota(T.nat512[:], [[512, 320]], 0, 0, ["nat512"], True)
+    select(T.idb[:], blk("zt", 0), [[-1, 128]], Op.not_equal, 1.0, 0, 1, ["zt"], ["idb"])
+    select(T.tril[:], blk("zt", 0), [[1, 128]], Op.is_ge, 1.0, 0, -1, ["zt"], ["tril"])
+    for k, sh, an in ((0, 0, 15), (1, 4, 1), (2, 5, 3), (4, 0, 1), (5, 1, 1), (6, 2, 1), (7, 0, 7), (8, 3, 1)):
+        ts(col("pi", k), col("pi", 9), sh, Op.logical_shift_right, ["pi9"], ["pi%d" % k], an, Op.bitwise_and)
+    ts(col("pi", 3), col("pi", 9), 4, Op.logical_shift_right, ["pi9"], ["pi3"])
+    cp(col("pf", 0, 10), col("pi", 0, 10), ["pi%d" % k for k in range(10)], ["pf"])
+    fill(T.b2[:], 0.0, ["b2"])
+    ts(T.ly[:], col("cf", 0, 20), pf(1), Op.add, ["cf0", "pf"], ["ly"])
+    ts(pf(10), pf(1), 64.0, Op.mult, ["pf"], ["pf10"], pf(0), Op.add)
+    ts(pf(11), pf(1), 16.0, Op.mult, ["pf"], ["pf11"])
+    ts(pf(12), pf(2), 128.0, Op.mult, ["pf"], ["pf12"], pf(0), Op.add)
+    tt(pf(13), pf(6), pf(4), Op.subtract, ["pf"], ["pf13"])
+    ts(pf(15), pf(5), 4.0, Op.mult, ["pf"], ["pf15"], pf(4), Op.add)
+    tt(pf(14), pf(13), pf(1), Op.mult, ["pf13", "pf"], ["pf14"])
+    tt(pf(16), pf(15), pf(6), Op.add, ["pf15", "pf"], ["pf16"])
+    ts(T.lr[:], col("cf", 32, 8), pf(12), Op.add, ["cf1", "pf12"], ["lr"])
+    ts(pf(24), pf(2), 3.0, Op.is_lt, ["pf"], ["pf24"], 64.0, Op.mult)
+    ts(pf(25), pf(24), pf(12), Op.add, ["pf24", "pf12"], ["pf25"])
+    ts(T.lr7[:, 0:8:2], T.cf[:, 32:40:2], pf(12), Op.add, ["cf1", "pf12"], ["lr7_"])
+    ts(T.lr7[:, 1:8:2], T.cf[:, 32:40:2], pf(25), Op.add, ["cf1", "pf25", "lr7_"], ["lr7"])
+    ts(pf(26), pf(3), 7.0, Op.is_equal, ["pf"], ["pf26"], 128.0, Op.mult)
+    ts(pf(17), pf(16), pf(4), Op.add, ["pf16", "pf14", "pf"], ["pf17"], pf(14), Op.add)
+    ts(pf(23), pf(16), pf(6), Op.add, ["pf16", "pf14", "pf"], ["pf23"], pf(14), Op.subtract)
+    ts(pf(18), pf(23), 16.0, Op.mult, ["pf23"], ["pf18"])
+    ts(col("ox", 0, 64), col("cf", 64, 64), pf(11), Op.add, ["cf4", "pf11"], ["ox0"])
+    ts(col("pk", 0), pf(17), 16.0, Op.mult, ["pf17", "pf26"], ["pk0"], pf(26), Op.add)
+    ts(col("pk", 2, 2), col("cf", 0, 2), 0.0, Op.mult, ["cf0", "pf18"], ["pk1"], pf(18), Op.add)
+    ts(T.l0[:], col("nat", 0, 4), 16.0, Op.mult, ["nat", "pf10"], ["l0"], pf(10), Op.add)
+    fill(T.b1[:], 0.0, ["b1"])
+    fill(T.ca[:], 0.0, ["ca"])
+    fill(T.cb[:], 0.0, ["cb"])
+
+    def step(s):
+        if s == 7:
+            cp(T.o7[:], col("fw", 320, 320).indirect(col("of", 24, 8)), ["fw7", "of6"], ["o7"])
+            tr(col("tl", 128, 128), T.o7[:], ["o7"], ["tl7"])
+            return
+        lst, key = (T.l0[:], "l0") if s == 0 else (blk("of", s - 1, 4), "of%d" % (s - 1))
+        cp(blk("ox", s + 1, 64), blk("fw", 8 - s, 320).indirect(lst), ["fw%d" % s, key], [OX[s + 1]])
+        tr(blk("tt", s, 64), blk("ox", s + 1, 64), [OX[s + 1]], ["tt%d" % s])
+        cp(col("of", 24, 8) if s == 6 else blk("of", s, 4), T.tt[:, 64 * s:64 * s + 64:8 if s == 6 else 16], ["tt%d" % s], ["of%d" % s])
+
+    def places():
+        cp(T.rl[:], col("ox", 64, 448).indirect(T.lr7[:]), OX[1:] + ["lr7"], ["rl"])
+        tr(col("tl", 0, 128), T.rl[:], ["rl"], ["tl"])
+        cp(T.lw[:], T.tl[:].indirect(col("pk", 0)), ["tl", "tl7", "pk0"], ["lw"])
+
+    def decode(name, keys, w, q, s, key, scale, view=None):
+        for t in range(4):
+            mm(PS[t][:, 0:w], blk("qe", t), blk("se", t), q, s, ["qe", key], ["#%d" % t])
+        for t in range(4):
+            times(T[name][:, t:4 * w:4] if view else blk(name, t, w), PS[t][:, 0:w], ["#%d" % t], [keys[t]], scale)
+
+    FH4, DH4 = ["fh%d" % t for t in range(4)], ["dh%d" % t for t in range(4)]
+    LW = col("lw", 0, 8)
+
+    for m in range(8):
+        cp(col("mwf", 24 * m, 20), col("mwi", 24 * m, 20), ["mwi%d.%d" % (m, q) for q in range(8)], ["mwf%d" % m])
+        times(blk("yb", m, 320), col("mwf", 24 * m, 20).indirect(T.ly[:]), ["mwf%d" % m, "ly"], ["yb%d" % m], 1.0)
+        tr(blk("fw", 8 - m, 320), blk("yb", m, 320), ["yb%d" % m], ["fw%d" % m])
+        step(m)
+    quant(T.qx[:], T.sx[:], T.xi[:], ["xi"], ["qx"])
+    quant(T.qe[:], T.se[:], T.ce[:], ["ce%d" % t for t in range(4)], ["qe"])
+    decode("fh", FH4, 320, T.qx[:], T.sx[:], "qx", 0.5)
+    places()
+
+    for t in range(5):
+        fill(sm1("sc", t), 32.0 ** -t, ["sc%d" % t])
+    fill(sm1("sc", 5), 0.0, ["sc5"])
+    ts(col("cj", 0, 128), col("ci", 0, 128), 15, Op.bitwise_and, ["cia"], ["cja"])
+    ts(col("cj", 128, 8), col("ci", 128, 8), 4, Op.arith_shift_right, ["cib"], ["cjb"])
+    ts(T.mod[:], col("cj", 0, 128), 0.0, Op.is_equal, ["cja"], ["mod"])
+    ts(T.m8[:], col("cj", 128, 8), 0.0, Op.is_equal, ["cjb"], ["m8"])
+    for t in range(3):
+        ts(T.ca[:, 512 * t + t:512 * t + 512:4], T.mod[:], 0.0, Op.mult, ["mod", "ca"], ["ca.%d" % t], 32.0 ** t, Op.add)
+        ts(T.cb[:, 512 * t + t:512 * t + 512:4], T.mod[:], 32.0 ** t, Op.mult, ["mod", "cb"], ["cb.%d" % t])
+    quant(T.qa[:], T.sa[:], T.ca[:], ["ca"] + ["ca.%d" % t for t in range(3)], ["qa"])
+    quant(T.qb[:], T.sb[:], T.cb[:], ["cb"] + ["cb.%d" % t for t in range(3)], ["qb"])
+    quant(T.qu[:], T.su[:], T.ui[:], ["ui%d" % m for m in range(9)], ["qu"])
+    quant(T.qv[:], T.sv[:], T.vi[:], ["vi"], ["qv"])
+    ts(sm("jw"), col("nat", 0, 8), 16.0, Op.mult, ["nat", "pf"], ["jw"], pf(0), Op.add)
+    ts(pf(19), pf(7), 2.0, Op.mult, ["pf"], ["pf19"])
+    ts(pf(20), pf(8), -16.0, Op.mult, ["pf"], ["pf20"], 17.0, Op.add)
+    ts(sm("jd"), sm("jw"), 4.0, Op.mult, ["jw"], ["jd"], 1280.0, Op.add)
+    ts(col("yy", 32), pf(9), 1024.0, Op.mult, ["pf"], ["yyc"])
+    ts(col("la", 0, 2), col("cf", 56, 2), pf(19), Op.add, ["cf3", "pf19"], ["la0"])
+    tt(pf(21), pf(20), pf(19), Op.add, ["pf20", "pf19"], ["pf21"])
+    ts(col("la", 2, 2), col("nat", 0, 2), 0.0, Op.mult, ["nat", "pf21"], ["la1"], pf(21), Op.add)
+    cp(T.cwf[:], T.cwi[:], ["cwi%d" % i for i in range(16)], ["cwf"])
+    ts(pf(22), pf(3), -327680.0, Op.mult, ["pf"], ["pf22"], 2621440.0, Op.add)
+
+    heir = T.cores[(r - STEP[2]) % N]
+    send([(T.wdp[:], T.wps[:])], heir, "aw", ["wps"])
+    for k in range(3):
+        donor, client = T.cores[(r + STEP[k]) % N], T.cores[(r - STEP[k]) % N]
+        qm, sp, qh, sh = [T["%s%d" % (n, k)] for n in ("qm", "sm", "qh", "sh")]
+        if k == 0:
+            for t in range(4):
+                times(T.mt[:, t:512:4], blk("fh", t, 320).indirect(LW), [FH4[t], "lw"], [M4[t]], 2.0)
+        else:
+            quant(T.qn[:], T.sn[:], T.nt[:], N4, ["qn"])
+            decode("mt", M4, 128, T.qn[:], T.sn[:], "qn", 1.0, True)
+        quant(qm[:], sp[:], T.mt[:], M4, ["qm%d" % k])
+        mc, mp, mkey, wc, wp, wkeys = qm, sp, "qm%d" % k, T.wdc, T.wdp, ["wd"]
+        hc, hp, hkey = qh, sh, "qh%d" % k
+        if k < 2:
+            send([(T["mc%d" % k][:].bitcast(B8), qm[:].bitcast(B8)), (T["mp_%d" % k][:], sp[:])], donor, "am%d" % k, ["qm%d" % k])
+            mc, mp, mkey, wc, wp, wkeys = T["mc%d" % k], T["mp_%d" % k], "mc%d" % k, T.wcs, T.wps, ["wcs", "wps"]
+            arrives("am%d" % k, client, [mkey])
+        for b in range(4):
+            mm(PS[b][:, 0:128], wc[:, 128 * b:128 * b + 128], wp[:, 128 * b:128 * b + 128], mc[:], mp[:], wkeys + [mkey], ["#%d" % b])
+        for b in range(4):
+            o, i = T.ht[:, b:512:4], PS[b][:, 0:128]
+            op("vs", lambda e, o=o, i=i: V.tensor_scalar(o, i, 0.0, 0.03125, Op.max, Op.mult) if e == "v" else S.activation(o, i, Act.Relu, scale=0.03125), ["#%d" % b], [H4[b]])
+        quant(qh[:], sh[:], T.ht[:], H4, ["qh%d" % k])
+        if k < 2:
+            send([(T["hc%d" % k][:].bitcast(B8), qh[:].bitcast(B8)), (T["hp%d" % k][:], sh[:])], client, "ah%d" % k, ["qh%d" % k])
+            hc, hp, hkey = T["hc%d" % k], T["hp%d" % k], "hc%d" % k
+            arrives("ah%d" % k, donor, [hkey])
+            if k == 0:
+                send([(T.wdc[:].bitcast(B8), T.wcs[:].bitcast(B8))], heir, "aw", ["wcs"])
+                arrives("aw", T.cores[(r + STEP[2]) % N], ["wd"])
+        cp(T.rle[:], T.ox[:].indirect(T.lr[:]), OX + ["lr"], ["rle"])
+        tr(T.te[:], T.rle[:], ["rle"], ["te"])
+        cp(T.ew[:], T.te[:].indirect(col("pk", 2, 2)), ["te", "pk1"], ["ew"])
+        ts(T.e1[:], T.ew[:], 15, Op.bitwise_and, ["ew"], ["e1"])
+        ts(T.e2[:], T.ew[:], 4, Op.logical_shift_right, ["ew"], ["e2"])
+        cp(T.el[:], col("ew", 0, 8), ["ew"], ["el"])
+        ts(T.e3[:], T.e1[:], 80.0, Op.mult, ["e1"], ["e3"])
+        tt(T.ec[:], T.e2[:], T.k20[:], Op.add, ["e2", "k20"], ["ec"])
+        tt(T.e1[:], T.e3[:], T.ec[:], Op.add, ["e3", "ec"], ["e1"])
+        cp(T.lc[:], T.e1[:], ["e1"], ["lc"])
+        times(T.rf[:, 4:768:6], T.nat[:].indirect(LW), ["nat", "lw"], ["rf4"], 1.0)
+        op("s", lambda _: S.activation(T.rf[:, 5:768:6], T.nat[:].indirect(T.el[:]), Act.Identity, scale=1024.0, bias=pf(22)), ["nat", "el", "pf22"], ["rf5"])
+        for q in range(4):
+            times(T.rf[:, q:768:6], T.cwf[:].indirect(blk("lc", q, 8)), ["cwf", "lc"], ["rf%d" % q], 1.0)
+        for m in range(8):
+            dma("y", "dc", blk("cp", m, 6), T.rf[16 * m:16 * m + 1, 0:768], ["rf%d" % q for q in range(6)], ["cp%d" % m], k)
+        C = ["cp%d" % m for m in range(8)]
+        for q in range(4):
+            tt(blk("ne", q, 8), T.cp[:, q:48:6], T.cp[:, 4:48:6], Op.not_equal, C, ["ne%d" % q])
+            tt(blk("sk", q, 8), T.cp[:, q:48:6], T.cp[:, 5:48:6], Op.add, C, ["sk%d" % q])
+        tt(T.pp[:], T.ne[:], T.sk[:], Op.mult, ["ne%d" % q for q in range(4)] + ["sk%d" % q for q in range(4)], ["pp"])
+        if k:
+            for t in range(4):
+                cp(T.xt[:].indirect(blk("xl", t, 8)), T.nt[:, t:512:4], ["xl%d" % t, N4[t]], X4)
+            quant(T.qx[:], T.sx[:], col("xt", 0, 1280), X4, ["qx"])
+            decode("fh", FH4, 320, T.qx[:], T.sx[:], "qx", 0.5)
+        for t in range(4):
+            times(T.xt[:, t:1280:4], blk("fh", t, 320), [FH4[t]], [X4[t]], 2.0)
+        mm(PS[4][:, 0:128], hc[:], hp[:], T.qu[:], T.su[:], [hkey, "qu"], ["#4"])
+        ts(col("sg", 0, 16), PS[4][:, 0:16], 0.0, Op.is_gt, ["#4"], ["sg0"])
+        ts(col("sg", 16, 16), PS[4][:, 0:16], 0.0, Op.is_le, ["#4"], ["sg1"])
+        tt(T.xx[:], T.sg[:].indirect(col("la", 0, 2)), T.pp[:], Op.mult, ["sg0", "sg1", "la0", "pp"], ["xx"])
+        tt(col("yy", 0, 32), T.sg[:].indirect(col("la", 2, 2)), T.xx[:], Op.mult, ["sg0", "sg1", "la1", "xx"], ["yy"])
+        red(sm("rq", 1), col("yy", 0, 33), Op.max, ["yy", "yyc"], ["rq"])
+        ts(col("qd", 0, 6), sm("sc", 6), sm("rq", 1), Op.mult, ["rq"] + ["sc%d" % t for t in range(6)], ["qd"])
+        ts(sm("nq", 5), col("qd", 1, 5), -32.0, Op.mult, ["qd"], ["nq"])
+        tt(sm("dg", 5), sm("nq", 5), col("qd", 0, 5), Op.add, ["nq", "qd"], ["dg"])
+        for t in range(3):
+            times(T.b1[:, t:512:4], T.idb[:], ["idb", "dg", "b1"], ["ba%d" % t], sm1("dg", 2 + t))
+        quant(blk("qk", 0), blk("sk1", 0), col("b1", 0, 512), ["ba%d" % t for t in range(3)] + ["b1"], ["qk0"])
+        for t in range(3):
+            mm(PS[5][:, 0:128], blk("qa", t), blk("sa", t), blk("qk", 0), blk("sk1", 0), ["qa", "qk0"], ["#5"], t == 0, t == 2)
+        for t in range(2):
+            times(T.b1[:, 512 + t:1024:4], T.idb[:], ["idb", "dg", "b1"], ["bb%d" % t], sm1("dg", t))
+        for t in range(3):
+            times(T.b1[:, 1024 + t:1056:4], T.m8[:], ["m8", "dg", "b1"], ["bc%d" % t], sm1("dg", 2 + t))
+        ts(sm("kf", 1), col("qd", 2), 1.0, Op.add, ["qd"], ["kf"])
+        quant(blk("qk", 2), blk("sk1", 2), col("b1", 1024, 512), ["bc0", "bc1", "bc2", "b1"], ["qk2"])
+        for t in range(3):
+            mm(PS[7][:, 0:128], blk("qb", t), blk("sb", t), blk("qk", 2), blk("sk1", 2), ["qb", "qk2"], ["#7"], t == 0, t == 2)
+        times(sm("kw"), PS[7][:, 0:8], ["#7"], ["kw"], 1.0)
+        ts(T.kt[:], T.tril[:], sm("kf", 1), Op.mult, ["tril", "kf"], ["kt"], -1.0, Op.add)
+        tt(T.eq[:], PS[5][:, 0:128], T.kt[:], Op.is_equal, ["#5", "kt"], ["eq"])
+        red(sm("lo", 1), T.eq[:], Op.max, ["eq"], ["lo"])
+        ts(T.b2[:, 0:32:4], T.m8[:], sm("lo", 1), Op.mult, ["m8", "lo", "b2"], ["b2a"])
+        quant(T.ql[:], T.sl[:], T.b2[:], ["b2", "b2a"], ["ql"])
+        mm(PS[4][:, 0:128], blk("qb", 0), blk("sb", 0), T.ql[:], T.sl[:], ["qb", "ql"], ["#4"])
+        quant(blk("qk", 1), blk("sk1", 1), col("b1", 512, 512), ["bb0", "bb1", "b1"], ["qk1"])
+        for t in range(2):
+            mm(PS[6][:, 0:128], blk("qa", t), blk("sa", t), blk("qk", 1), blk("sk1", 1), ["qa", "qk1"], ["#6"], t == 0, t == 1)
+        times(T.va[:], PS[6][:, 0:128], ["#6"], ["va"], 1.0)
+        tt(sm("dj"), sm("jw"), sm("kw"), Op.subtract, ["jw", "kw"], ["dj"])
+        tt(sm("t1"), PS[4][:, 0:8], sm("dj"), Op.mult, ["#4", "dj"], ["t1"])
+        tt(sm("t2"), sm("t1"), sm("kw"), Op.add, ["t1", "kw"], ["t2"])
+        cp(T.ofs[:], sm("t2"), ["t2"], ["ofs"])
+        cp(T.fw[:].indirect(T.ofs[:]), T.va[:], ["ofs", "va"], FWALL)
+        decode("dh", DH4, 128, hc[:], hp[:], hkey, 0.5)
+        if k == 2:
+            for m in range(8):
+                dma("y", "do", T.fo[m:m + 1, :], T.fw[0:1, 320 * (8 - m):320 * (8 - m) + 320], ["fw%d" % m], [])
+        for s in range(8):
+            step(s)
+        places()
+        ts(sm("nl"), LW, -512.0, Op.mult, ["lw"], ["nl"])
+        tt(T.kk[:], T.nat512[:].indirect(LW), col("nat", 0, 128), Op.add, ["nat512", "lw", "nat"], ["kk"])
+        for c in range(8):
+            n = 16 * c + 16
+            d, b, i = col("dd", 128 * c, n), sm1("nl", c), col("kk", 0, n)
+            op("vs", lambda e, d=d, b=b, i=i: V.tensor_scalar(d, i, b, None, Op.add) if e == "v" else S.activation(d, i, Act.Identity, bias=b), ["kk", "nl"], ["dd%d" % c])
+        for c in range(8):
+            red(sm1("fi", c), col("dd", 128 * c, 16 * c + 16), Op.min, ["dd%d" % c], ["fi%d" % c], apply_absolute_value=True)
+        for t in range(4):
+            times(blk("fg", t), blk("fh", t, 320).indirect(LW), [FH4[t], "lw"], ["fg%d" % t], 1.0)
+        cp(T.fl[:], sm("fi"), ["fi%d" % c for c in range(8)], ["fl"])
+        tt(sm("wn"), sm("fi"), sm("jw"), Op.is_equal, ["fi%d" % c for c in range(8)] + ["jw"], ["wn"])
+        ts(sm("xd"), LW, 4.0, Op.mult, ["lw"], ["xd"])
+        tt(sm("xe"), sm("xd"), sm("jd"), Op.subtract, ["xd", "jd"], ["xe"])
+        tt(sm("xd"), sm("xe"), sm("wn"), Op.mult, ["xe", "wn"], ["xd"])
+        tt(sm("xe"), sm("xd"), sm("jd"), Op.add, ["xd", "jd"], ["xe"])
+        for t in range(4):
+            ts(blk("xl", t, 8), sm("xe"), float(t), Op.add, ["xe"], ["xl%d" % t])
+        for t in range(4):
+            tt(T.nt[:, t:512:4], blk("dh", t).indirect(T.fl[:]), blk("fg", t), Op.add, [DH4[t], "fl", "fg%d" % t], [N4[t]])
+    for t in range(4):
+        cp(T.xt[:].indirect(blk("xl", t, 8)), T.nt[:, t:512:4], ["xl%d" % t, N4[t]], X4)
+    quant(T.qx[:], T.sx[:], col("xt", 0, 1280), X4, ["qx"])
+    mm(PS[4][:, 0:320], T.qv[:], T.sv[:], T.qx[:], T.sx[:], ["qv", "qx"], ["#4"])
+    dma("y", "do", T.oc[:], T.qx[:].bitcast(B8), ["qx"], [])
+    for i in range(4):
+        dma("y", "do", T.osc[4 * i:4 * i + 4, :], T.sx[32 * i:32 * i + 4, :], ["qx"], [])
+    times(T.yo[:], PS[4][:, 0:320], ["#4"], ["yo"], 1.0)
+    dma("s", "do", T.y[:], T.yo[:], ["yo"], [])
+    return ops
+
+
+def orders(ops):
+    wr, rd, out = {}, {}, []
+    for i, (q, _, reads, writes, kind, _, _) in enumerate(ops):
+        p = set()
+        for k in reads:
+            p.update(wr.get(k, []))
+            if k[0] == "#":
+                p.update(j for j in rd.get(k, []) if len(q + ops[j][0]) > 2 or ops[j][0] != q)
+        for k in writes:
+            if kind != "send":
+                p.update(wr.get(k, []) + rd.get(k, []))
+        for k in reads:
+            rd.setdefault(k, []).append(i)
+        for k in writes:
+            wr[k] = wr[k] + [i] if kind == "send" and k in wr else [i]
+            rd[k] = []
+        out.append(p)
+    return out
+
+
+def listed(text, ops):
+    out = []
+    for w in text.split():
+        a, e = w.rstrip("*"), 1 if w[-1] == "*" else 0
+        lo, hi = (a.split("-") + [a])[:2] if "-" in a else (a, a)
+        out += [(k, ops[k][0][e]) for k in range(int(lo), int(hi) + 1)]
+    return out
+
+
+def rank_program(g, core, T, topo):
+    if T.rank_of(core) is None:
+        return
+    ops = program(g, core, T, topo)
+    before = orders(ops)
+    Q = {"v": g.vector, "s": g.scalar, "t": g.tensor, "p": g, "y": g.sync}
+    known, tot, end, token = {q: {} for q in Q}, {}, {}, {}
+    for q, _, _, _, kind, sem, batch in ops:
+        if kind == "dma":
+            tot[sem] = tot.get(sem, 0) + 16
+            end[sem, batch] = tot[sem]
+        elif kind == "arrival":
+            tot[sem] = batch
+        elif kind == "send":
+            tot["ls"] = tot.get("ls", 0) + batch
+    for i, e in listed(ORDER_TEXT, ops) or [(k, ops[k][0][0]) for k in range(len(ops))]:
+        q, call, reads, writes, kind, sem, batch = ops[i]
+        if kind == "arrival":
+            token[i] = (sem, batch, {})
+            continue
+        want = {}
+        for j in before[i]:
+            if j not in token or (kind == "acc" and ops[j][0] == "t" and set(ops[j][3]) & set(writes)):
+                continue
+            s, val, snap = token[j]
+            if val > want.get(s, (0, None))[0]:
+                want[s] = (val, snap)
+        for s in sorted(want, key=lambda m: (-len(want[m][1]), m)):
+            val, snap = want[s]
+            if known[e].get(s, 0) < val:
+                Q[e].wait_ge(T.sem[s], val)
+                known[e][s] = val
+                for a, b in snap.items():
+                    known[e][a] = max(known[e].get(a, 0), b)
+        ins = call(e)
+        if kind == "dma":
+            ins.then_inc(T.sem[sem], 16)
+            token[i] = (sem, end[sem, batch], dict(known[e]))
+        elif kind != "send":
+            tot[e] = tot.get(e, 0) + 1
+            ins.then_inc(T.sem[e], 1)
+            token[i] = (e, tot[e], dict(known[e]))
+    for sem in sorted(tot):
+        if known["p"].get(sem, 0) < tot[sem]:
+            g.wait_ge(T.sem[sem], tot[sem])

@@ -1,419 +1,454 @@
 from concourse.mybir import dt, AluOpType as Op, AxisListType, ActivationFunctionType as Act
 
 F32, BF, I32, U16, MXC, U8 = "float32", "bfloat16", "int32", "uint16", "float8_e4m3fn_x4", "uint8"
-SCRATCH = {}
+C, J = 320, 128
+SCRATCH = {"tb": ("dram", [6, 8 * C], I32), "raw": ("sbuf", [128, 8, C], I32)}
 for _n, _w, _t in (
-        ("xi", 1280, BF), ("ui", 512, BF), ("vi", 512, BF), ("mwi", 192, I32), ("mwf", 192, F32), ("cwi", 1280, I32), ("cwf", 1280, F32),
-        ("wcs", 512, MXC), ("wps", 512, U8), ("wdc", 512, MXC), ("wdp", 512, U8),
-        ("pi", 16, I32), ("pf", 32, F32), ("nat", 320, F32), ("nat512", 320, F32), ("ci", 160, I32), ("cj", 160, I32), ("cf", 192, F32), ("k20", 32, I32),
-        ("tril", 128, BF), ("idb", 128, BF), ("mod", 128, BF), ("m8", 8, BF),
-        ("l0", 4, U16), ("lr", 8, U16), ("lr7", 8, U16), ("ly", 20, U16), ("pk", 4, U16), ("la", 4, U16),
-        ("zt", 512, BF), ("ce", 2048, BF), ("ca", 1536, BF), ("cb", 1536, BF),
+        ("xi", 1280, BF), ("ui", 512, BF), ("vi", 512, BF), ("wcs", 512, MXC), ("wps", 512, U8), ("wdc", 512, MXC), ("wdp", 512, U8),
+        ("pi", 16, I32), ("pf", 48, F32), ("nat", 320, F32), ("dm", 128, F32), ("ci", 128, I32), ("cj", 128, I32), ("cf", 96, F32), ("kb", 32, F32),
+        ("tril", 128, BF), ("idb", 128, BF), ("mod", 128, BF), ("m8", 8, BF), ("stp", 576, BF), ("ls_", 24, U16),
+        ("ze", 516, BF), ("za", 516, BF), ("zb", 516, BF),
         ("qe", 512, MXC), ("se", 512, U8), ("qa", 384, MXC), ("sa", 384, U8), ("qb", 384, MXC), ("sb", 384, U8),
-        ("qu", 128, MXC), ("su", 128, U8), ("qv", 128, MXC), ("sv", 128, U8), ("fs", 192, F32),
-        ("yb", 2560, F32), ("fw", 2880, F32), ("ox", 512, F32), ("o7", 128, F32), ("tt", 448, F32), ("of", 40, U16),
-        ("rl", 128, F32), ("tl", 256, F32), ("lw", 16, U16), ("rle", 128, F32), ("te", 128, F32), ("ew", 32, I32),
-        ("e1", 32, I32), ("e2", 32, I32), ("e3", 32, I32), ("ec", 32, I32), ("el", 8, U16), ("lc", 32, U16),
-        ("rf", 768, F32), ("cp", 48, F32), ("ne", 32, F32), ("sk", 32, F32), ("pp", 32, F32), ("kk", 128, F32), ("dd", 1024, F32), ("fl", 8, U16),
-        ("sg", 32, F32), ("xx", 32, F32), ("yy", 36, F32), ("qd", 8, I32), ("b1", 1536, BF), ("b2", 512, BF),
-        ("qk", 384, MXC), ("sk1", 384, U8), ("ql", 128, MXC), ("sl", 128, U8), ("kt", 128, F32), ("eq", 128, F32), ("ofs", 8, U16), ("va", 128, F32),
-        ("fh", 1280, BF), ("dh", 512, BF), ("fg", 512, F32), ("nt", 512, BF), ("qn", 128, MXC), ("sn", 128, U8), ("mt", 512, BF), ("ht", 512, BF),
+        ("qu", 128, MXC), ("su", 128, U8), ("qv", 128, MXC), ("sv", 128, U8), ("fs", 320, F32),
+        ("fw", 2688, F32), ("ox", 448, U16), ("ot", 464, U16), ("oxf", 656, F32), ("wf", 1440, F32), ("lw", 16, U16),
+        ("pw", 224, F32), ("lrow", 128, F32), ("ne", 576, BF), ("so", 576, BF), ("fl", 16, U16),
+        ("sg", 32, F32), ("xx", 32, F32), ("yy", 36, F32), ("qd", 16, I32), ("ba", 544, BF), ("bb", 512, BF), ("b2", 512, BF),
+        ("qk", 136, MXC), ("sk", 136, U8), ("qw", 128, MXC), ("sw", 128, U8), ("ql", 128, MXC), ("sl", 128, U8),
+        ("kt", 128, F32), ("eq", 128, F32), ("kl", 8, U16), ("ofs", 8, U16), ("va", 128, F32), ("nv", 128, F32),
+        ("fh", 1280, BF), ("dh", 256, BF), ("fg", 256, BF), ("nt", 512, BF), ("qn", 128, MXC), ("sn", 128, U8), ("dn", 512, BF), ("mt", 512, BF), ("ht", 512, BF),
         ("xt", 1792, BF), ("qx", 320, MXC), ("sx", 320, U8), ("xl", 32, U16), ("yo", 320, F32),
         ("qm0", 128, MXC), ("sm0", 128, U8), ("qm1", 128, MXC), ("sm1", 128, U8), ("qm2", 128, MXC), ("sm2", 128, U8),
         ("qh0", 128, MXC), ("sh0", 128, U8), ("qh1", 128, MXC), ("sh1", 128, U8), ("qh2", 128, MXC), ("sh2", 128, U8),
-        ("mc0", 128, MXC), ("mp_0", 128, U8), ("mc1", 128, MXC), ("mp_1", 128, U8), ("hc0", 128, MXC), ("hp0", 128, U8), ("hc1", 128, MXC), ("hp1", 128, U8)):
+        ("mc1", 128, MXC), ("mp_1", 128, U8), ("mc2", 128, MXC), ("mp_2", 128, U8), ("hc1", 128, MXC), ("hp1", 128, U8), ("hc2", 128, MXC), ("hp2", 128, U8)):
     SCRATCH[_n] = ("sbuf", [128, _w], _t)
 for _n in range(8):
     SCRATCH["p%d" % _n] = ("psum", [128, 512], F32)
-SMALL = {n: 8 * k for k, n in enumerate(("jw", "jd", "sc", "nq", "dg", "kf", "lo", "kw", "dj", "t1", "t2", "rq", "fi", "wn", "xd", "nl", "xe"))}
-SEMAPHORES = ["v", "s", "t", "p", "dx", "du", "dv", "dw", "da", "dc", "do", "aw", "am0", "am1", "ah0", "ah1", "ls"] + ["dm%d" % _n for _n in range(8)]
+SMALL = {n: 16 * k for k, n in enumerate(("sc", "sd", "dg", "rq", "lo", "dk", "of", "jc", "nl", "jw", "xm", "xj", "xe", "wn", "wn_"))}
+SEMAPHORES = ["v", "s", "t", "p", "ls", "aw", "am1", "am2", "ah1", "ah2"] + ["d%d" % _n for _n in range(16)]
 STEP = [1, 2, 3]
-ORDER_TEXT = """
-1 61 93 120 24 49 94 15 0 52 2 110 112 3-4 97 113 5-6 115 7 41 116 22 8 117-118 30 10 111 11-12 114 13-14 46 63 119 9 17-19 121 20-21 122 98 126
-23 26 35 28 141 123 25 32 124 27 34 130 29 36 128 31 38 125 131 37 42 134 39 44 127 16 48 234 33 50 135 47 54 136 57 56 51 60 53 62 55 58 95 59
-40 43 64 99 45 145 132 75 139 66 146 133 73 137 67 129 68-69 151 140 71-72 152 74 157 76 78-81 163 100 147 82 158 77 65 90 153 70 91 83-84 148
-164 85-87 149 88 159 89 92 101 150 169 154 170 155 165 156 175 160 176 102 161 171 162 181 166 182 167 177 168 96 187 172 188 183 106 105 173
-103 193 108 192 104 189 194 109 174 195 138 198 178 107 196 179-180 199 197 184-185 200 256 186 202 190 201 235 203 191 257 291 204 258 237 236*
-238* 239 268 240 259 293 241 233 294 242-243 292 260-265 269 266-267 142 272 270 273 227 223 271 211 205-206 208 279 209 274 210 275 213 277 144
-278 280-281 276 247 244 251* 245-246 248 249* 229 250 226 252 231 230 253 216 220 212 143 254-255 283 282 284-286 289 217 219 288 214 287 207
-225 215 290 221 232 218 228 222 224 295 340 296 337 297 344 338 298 339 341 299-300 343 301 342 302 316 303 322 315 313* 304-305* 311 306* 314*
-307 312 317 308-309 328 310 318 323 319-320 324 329 321* 330 325 332 326 331 327 333-336 345-364 368 365 369 366-367 370-371 392 372 389 390* 391
-379-380 377 442 373-374 381 378* 382 376 388 375* 387 384 383 386 385 393 403 405-406 404 407 432 411 409 395 415* 410 413* 408 414* 412* 416 433
-417 394 434 396 435-436 418 437 439 443 438 397 440 419 398 441 400 399 444 447* 445 446* 465 454 452 448 450 449 451 401 455 466 453 402 467-469
-421 420 425* 422 424 423 426 471 427 462 428 472 475 463 456 429 457 473 458-461 476 470 430 464 477* 479 431 474* 480-481* 478* 482 525 483 524
-484 529 526 485 527 530 486-487 528 488 531 489 503 490 509 502 493* 491-492* 498 501* 494 499-500* 495-496 504 497 515 505 510 506-507 511 516
-508* 517 512 519 513 518 514 520-523 532-551 555 552 613 553-554 614 556 615 557 617 616 623 619 559 577 620 558 578 618 621 564 567 624 566 565
-579 560-562 575-576 574 573 563* 572 568-571 622 580 625* 626 627* 628 590 629-630 591 632-634 592 635-636 631 593 582 594 583 581 598 597 584
-602* 595 601* 596 599-600* 585 603 586-587 605 646 604 609* 606-607 610* 608 637 611* 638-642 612 643-644 663 645 664-670 684 671 690 682 672*
-680* 673* 679 683* 681* 674* 685 675 686 696 687 647 676-678 688 691 697 689* 698 692 700 699 693 588 694 589 648 695 701-704 721 718 713-715 722
-716 723 717 719 724 720 725-727 649 728-734 650 735 651 736 652 737 655 738 653 739 656 654 740 744 705 741 658 742 706 745 657 743 708 746 712*
-765 748 707 747 766 711* 753 756 767 755 754 768 763 762 749 752* 751 764 750* 761 771 709 757 759-760 758 710 772 660* 662 770 769 661* 773 659
-774 779 775 780 783 776 781 784 777-778 785 782 786-789 791-793 790 794* 795
-"""
+CYC, WAKE = 1.0, 130.0
 
 
 def program(g, core, T, topo):
     r = T.rank_of(core)
     N = len(T.cores)
-    Q = {"v": g.vector, "s": g.scalar, "t": g.tensor, "p": g, "y": g.sync}
+    V, S = g.vector, g.scalar
+    Q = {"s": S, "y": g.sync}
     ops = []
 
-    def op(q, call, reads, writes, acc=False):
-        ops.append([q, call, reads, writes, "acc" if acc else "op", None, 0])
+    def bits(a, b, st=1):
+        return sum(1 << c for c in range(a, b, st)) if st != 1 else (1 << b) - (1 << a)
 
-    def dma(q, sem, out, in_, reads, writes, batch=0):
-        ops.append([q, lambda _: Q[q].dma_start(out, in_), reads, writes, "dma", sem, batch])
+    def R(name, a=0, b=None, st=1):
+        b = T[name].shape[1] if b is None else b
+        return (T[name][:, a:b:st], [(name, bits(a, b, st))], len(range(a, b, st)), SCRATCH[name][2] in (BF, U16), False)
 
-    def send(pairs, dst, sem, reads):
+    def col(name, k, n=1):
+        return R(name, k, k + n)
+
+    def blk(name, t, w=128):
+        return R(name, w * t, w * t + w)
+
+    def by(win, off):
+        return (win[0].indirect(off[0]), win[1] + off[1], 16 * off[2], False, True)
+
+    def sm(name, a=0, b=16, st=1):
+        return R("fs", SMALL[name] + a, SMALL[name] + b, st)
+
+    def ps(k, a, b, st=1):
+        return (T["p%d" % k][:, a:b:st], [("#%d" % k, 1)], len(range(a, b, st)), False, False)
+
+    def u8(v):
+        return (v[0].bitcast(dt.uint8),) + v[1:]
+
+    def ap(x):
+        return x[0] if isinstance(x, tuple) else x
+
+    def op(q, f, out, ins, cost, kind="op", **kw):
+        ins = [x for x in ins if isinstance(x, tuple)]
+        w = [k for o in out for k in o[1][:1]]
+        rd = [k for x in ins for k in x[1]] + [k for o in out for k in o[1][1:]]
+        ops.append(dict(q=q, f=f, r=rd, w=w, hold=cost, done=kw.pop("done", cost), kind=kind, **kw))
+        return len(ops) - 1
+
+    def ew(out, in0, per=1.0):
+        if in0[4]:
+            return 55 + 1.55 * in0[2] * CYC
+        if out[4]:
+            return 55 + 3.8 * out[2] * CYC
+        return max(64, in0[2] * per) * CYC
+
+    def half(*a):
+        return 0.5 if all(x[3] for x in a) else 1.0
+
+    def ts(out, in0, s1, op0, s2=None, op1=None):
+        f = (lambda e: V.tensor_scalar(out[0], in0[0], ap(s1), None, op0)) if op1 is None else (lambda e: V.tensor_scalar(out[0], in0[0], ap(s1), ap(s2), op0, op1))
+        op("v", f, [out], [in0, s1, s2], ew(out, in0, half(out, in0)))
+
+    def tt(out, a, b, o):
+        op("v", lambda e: V.tensor_tensor(out[0], a[0], b[0], o), [out], [a, b], ew(out, a, 1.0 if "#" in a[1][0][0] + b[1][0][0] else 2.0))
+
+    def cp(out, in_):
+        op("v", lambda e: V.tensor_copy(out[0], in_[0]), [out], [in_], ew(out, in_, half(out, in_)))
+
+    def tr(out, in_):
+        op("v", lambda e: V.transpose(out[0], in_[0]), [out], [in_], ew(out, in_, half(in_)))
+
+    def either(out, in_, fv, fs, more=(), q="vs"):
+        op(q, lambda e: fv() if e == "v" else fs(), [out], [in_] + list(more), {"v": ew(out, in_, half(out, in_)), "s": ew(out, in_) + 10})
+
+    def times(out, in_, s, q="vs"):
+        either(out, in_, lambda: V.tensor_scalar(out[0], in_[0], ap(s), None, Op.mult), lambda: S.activation(out[0], in_[0], Act.Copy, scale=ap(s)), [s], q)
+
+    def fma(out, in_, s, b, q="vs"):
+        either(out, in_, lambda: V.tensor_scalar(out[0], in_[0], ap(s), ap(b), Op.mult, Op.add),
+               lambda: S.activation(out[0], in_[0], Act.Identity, bias=ap(b), scale=ap(s)), [s, b], q)
+
+    def scan(out, d0, d1, op0, op1):
+        op("v", lambda e: V.tensor_tensor_scan(out[0], d0[0], d1[0], 0.0, op0, op1), [out], [d0, d1], ew(out, d0, half(out, d0, d1)))
+
+    def red(out, in_, o, **kw):
+        op("v", lambda e: V.tensor_reduce(out[0], in_[0], AxisListType.X, o, **kw), [out], [in_], ew(out, in_))
+
+    def fill(out, val):
+        op("v", lambda e: V.memset(out[0], val), [out], [], ew(out, out, half(out)))
+
+    def quant(q, s, t):
+        op("v", lambda e: V.quantize_mx(q[0], s[0], t[0]), [q, s], [t], (15 + 0.27 * t[2]) * CYC)
+
+    def mm(out, l, ls, m, ms, start=True, stop=True):
+        op("t", lambda e: g.tensor.matmul_mx(out[0], l[0], ls[0], m[0], ms[0], start, stop), [out], [l, ls, m, ms], 0.6 * (m[2] + 16), "op" if start else "acc")
+
+    def iota(out, pattern, base, cm):
+        flt = SCRATCH[out[1][0][0]][2] != I32
+        f = (lambda e: g.iota(out[0], pattern, base, cm, allow_small_or_imprecise_dtypes=True)) if flt else (lambda e: g.iota(out[0], pattern, base, cm))
+        op("p", f, [out], [], 130 + 2 * out[2] * CYC)
+
+    def dma(q, sem, out, in_, done, after=()):
+        return op(q, lambda e: Q[e].dma_start(out[0], in_[0]), [out], [in_], 60, "dma", sem=sem, done=done, after=list(after))
+
+    def hbm(a, name="hbm"):
+        return (a, [(name, 0 if name == "hbm" else 1)], 0, False, False)
+
+    def send(pairs, dst, sem, done):
         rid, pid, _ = topo.addr(dst)
         mask, n = topo.mask(core, dst), len(topo.engines(core, dst))
         for out, in_ in pairs:
-            ops.append(["p", lambda _, out=out, in_=in_: g.remote_dma(out, in_, T.sem[sem], T.sem.ls, pid, rid, mask), reads, ["sent." + sem], "send", sem, n])
+            op("p", lambda e, out=out, in_=in_: g.remote_dma(out[0], in_[0], T.sem[sem], T.sem.ls, pid, rid, mask), [(0, [("sent" + sem, 1)])], [in_], 250, "send", sem=sem, n=n, done=done)
 
-    def arrives(sem, src, writes):
-        ops.append(["-", None, ["sent." + sem], writes, "arrival", sem, 2 * len(topo.engines(src, core))])
+    def arrives(sem, src, outs):
+        op("-", None, outs, [(0, [("sent" + sem, 1)])], 0, "arrival", sem=sem, n=len(outs) * len(topo.engines(src, core)))
 
-    V, S = g.vector, g.scalar
-    B8 = dt.uint8
-
-    def ts(out, in0, s1, op0, reads, writes, s2=None, op1=None):
-        if op1 is None:
-            op("v", lambda _: V.tensor_scalar(out, in0, s1, None, op0), reads, writes)
-        else:
-            op("v", lambda _: V.tensor_scalar(out, in0, s1, s2, op0, op1), reads, writes)
-
-    def tt(out, a, b, o, reads, writes):
-        op("v", lambda _: V.tensor_tensor(out, a, b, o), reads, writes)
-
-    def cp(out, in_, reads, writes):
-        op("v", lambda _: V.tensor_copy(out, in_), reads, writes)
-
-    def tr(out, in_, reads, writes):
-        op("v", lambda _: V.transpose(out, in_), reads, writes)
-
-    def times(out, in_, reads, writes, scale, q="sv"):
-        op(q, lambda e: S.activation(out, in_, Act.Copy, scale=scale) if e == "s" else V.tensor_scalar(out, in_, scale, None, Op.mult), reads, writes)
-
-    def red(out, in_, o, reads, writes, **kw):
-        op("v", lambda _: V.tensor_reduce(out, in_, AxisListType.X, o, **kw), reads, writes)
-
-    def fill(ap, val, writes):
-        op("v", lambda _: V.memset(ap, val), [], writes)
-
-    def quant(q, s, t, reads, writes):
-        op("v", lambda _: V.quantize_mx(q, s, t), reads, writes)
-
-    def mm(out, l, ls, m, ms, reads, writes, start=True, stop=True):
-        op("t", lambda _: g.tensor.matmul_mx(out, l, ls, m, ms, start, stop), reads, writes, acc=not start)
-
-    def iota(out, pattern, base, cm, writes, flt):
-        if flt:
-            op("p", lambda _: g.iota(out, pattern, base, cm, allow_small_or_imprecise_dtypes=True), [], writes)
-        else:
-            op("p", lambda _: g.iota(out, pattern, base, cm), [], writes)
-
-    def select(out, in_, pattern, cmp, fill_, base, cm, reads, writes):
-        op("p", lambda _: g.affine_select(out, in_, pattern, cmp, fill_, base, cm), reads, writes)
-
-    def col(name, k, n=1):
-        return T[name][:, k:k + n]
-
-    def sm(name, n=8):
-        return T.fs[:, SMALL[name]:SMALL[name] + n]
-
-    def sm1(name, k):
-        return T.fs[:, SMALL[name] + k:SMALL[name] + k + 1]
-
-    def blk(name, t, w=128):
-        return T[name][:, w * t:w * t + w]
-
-    PS = [T["p%d" % k] for k in range(8)]
-    M4, H4, N4, X4 = [["%s%d" % (n, t) for t in range(4)] for n in "MHNX"]
-    OX = ["ox%d" % k for k in range(8)]
-    FWALL = ["fw%d" % s for s in range(8)]
-    pf = lambda k: T.pf[:, k:k + 1]
-
-    for m in range(8):
-        for q in range(8):
-            dma("ys"[q % 2], "dm%d" % m, T.mwi[16 * q:16 * q + 16, 24 * m:24 * m + 20], T.mp[16 * m:16 * m + 16, :], [], ["mwi%d.%d" % (m, q)])
-        if m == 1:
-            dma("y", "dx", T.xi[:], T.x[:], [], ["xi"])
-    dma("y", "dw", T.wcs[:].bitcast(B8), T.wc[:], [], ["wcs"])
-    dma("y", "dw", T.wps[:], T.ws[:], [], ["wps"])
-    for i in range(16):
-        dma("y", "da", T.cwi[i:128:16, :], T.ar[:], [], ["cwi%d" % i])
-    for m in range(8):
-        dma("y", "du", T.ui[:, 8 * m:8 * m + 8], T.u[:, 64 * m:64 * m + 8], [], ["ui%d" % m])
-    dma("y", "du", T.ui[:, 64:512], T.u[:, 0:448], [], ["ui8"])
-    dma("y", "dv", T.vi[:], T.v[:], [], ["vi"])
-
-    iota(col("pi", 9), [[0, 1]], 0, 1, ["pi9"], False)
-    iota(col("cf", 0, 20), [[2, 10], [0, 2]], 0, 0, ["cf0"], True)
-    iota(col("cf", 32, 8), [[16, 4], [64, 2]], 0, 0, ["cf1"], True)
-    iota(col("cf", 64, 64), [[32, 2], [64, 2], [1, 16]], 0, 0, ["cf4"], True)
-    iota(T.nat[:], [[1, 320]], 0, 0, ["nat"], True)
-    iota(T.zt[:], [[0, 512]], 0, 0, ["zt"], True)
-    for b in range(4):
-        select(blk("ce", b, 512), T.zt[:], [[-1, 512]], Op.not_equal, 1.0, b, 4, ["zt"], ["ce%d" % b])
-    iota(col("ci", 0, 128), [[-1, 128]], 128, 1, ["cia"], False)
-    iota(col("ci", 128, 8), [[-16, 8]], 0, 1, ["cib"], False)
-    iota(col("cf", 56, 2), [[-16, 2]], 16, 0, ["cf3"], True)
-    iota(T.k20[:], [[20, 4], [0, 8]], 0, 0, ["k20"], False)
-    iota(T.nat512[:], [[512, 320]], 0, 0, ["nat512"], True)
-    select(T.idb[:], blk("zt", 0), [[-1, 128]], Op.not_equal, 1.0, 0, 1, ["zt"], ["idb"])
-    select(T.tril[:], blk("zt", 0), [[1, 128]], Op.is_ge, 1.0, 0, -1, ["zt"], ["tril"])
-    for k, sh, an in ((0, 0, 15), (1, 4, 1), (2, 5, 3), (4, 0, 1), (5, 1, 1), (6, 2, 1), (7, 0, 7), (8, 3, 1)):
-        ts(col("pi", k), col("pi", 9), sh, Op.logical_shift_right, ["pi9"], ["pi%d" % k], an, Op.bitwise_and)
-    ts(col("pi", 3), col("pi", 9), 4, Op.logical_shift_right, ["pi9"], ["pi3"])
-    cp(col("pf", 0, 10), col("pi", 0, 10), ["pi%d" % k for k in range(10)], ["pf"])
-    fill(T.b2[:], 0.0, ["b2"])
-    ts(T.ly[:], col("cf", 0, 20), pf(1), Op.add, ["cf0", "pf"], ["ly"])
-    ts(pf(10), pf(1), 64.0, Op.mult, ["pf"], ["pf10"], pf(0), Op.add)
-    ts(pf(11), pf(1), 16.0, Op.mult, ["pf"], ["pf11"])
-    ts(pf(12), pf(2), 128.0, Op.mult, ["pf"], ["pf12"], pf(0), Op.add)
-    tt(pf(13), pf(6), pf(4), Op.subtract, ["pf"], ["pf13"])
-    ts(pf(15), pf(5), 4.0, Op.mult, ["pf"], ["pf15"], pf(4), Op.add)
-    tt(pf(14), pf(13), pf(1), Op.mult, ["pf13", "pf"], ["pf14"])
-    tt(pf(16), pf(15), pf(6), Op.add, ["pf15", "pf"], ["pf16"])
-    ts(T.lr[:], col("cf", 32, 8), pf(12), Op.add, ["cf1", "pf12"], ["lr"])
-    ts(pf(24), pf(2), 3.0, Op.is_lt, ["pf"], ["pf24"], 64.0, Op.mult)
-    ts(pf(25), pf(24), pf(12), Op.add, ["pf24", "pf12"], ["pf25"])
-    ts(T.lr7[:, 0:8:2], T.cf[:, 32:40:2], pf(12), Op.add, ["cf1", "pf12"], ["lr7_"])
-    ts(T.lr7[:, 1:8:2], T.cf[:, 32:40:2], pf(25), Op.add, ["cf1", "pf25", "lr7_"], ["lr7"])
-    ts(pf(26), pf(3), 7.0, Op.is_equal, ["pf"], ["pf26"], 128.0, Op.mult)
-    ts(pf(17), pf(16), pf(4), Op.add, ["pf16", "pf14", "pf"], ["pf17"], pf(14), Op.add)
-    ts(pf(23), pf(16), pf(6), Op.add, ["pf16", "pf14", "pf"], ["pf23"], pf(14), Op.subtract)
-    ts(pf(18), pf(23), 16.0, Op.mult, ["pf23"], ["pf18"])
-    ts(col("ox", 0, 64), col("cf", 64, 64), pf(11), Op.add, ["cf4", "pf11"], ["ox0"])
-    ts(col("pk", 0), pf(17), 16.0, Op.mult, ["pf17", "pf26"], ["pk0"], pf(26), Op.add)
-    ts(col("pk", 2, 2), col("cf", 0, 2), 0.0, Op.mult, ["cf0", "pf18"], ["pk1"], pf(18), Op.add)
-    ts(T.l0[:], col("nat", 0, 4), 16.0, Op.mult, ["nat", "pf10"], ["l0"], pf(10), Op.add)
-    fill(T.b1[:], 0.0, ["b1"])
-    fill(T.ca[:], 0.0, ["ca"])
-    fill(T.cb[:], 0.0, ["cb"])
-
-    def step(s):
-        if s == 7:
-            cp(T.o7[:], col("fw", 320, 320).indirect(col("of", 24, 8)), ["fw7", "of6"], ["o7"])
-            tr(col("tl", 128, 128), T.o7[:], ["o7"], ["tl7"])
-            return
-        lst, key = (T.l0[:], "l0") if s == 0 else (blk("of", s - 1, 4), "of%d" % (s - 1))
-        cp(blk("ox", s + 1, 64), blk("fw", 8 - s, 320).indirect(lst), ["fw%d" % s, key], [OX[s + 1]])
-        tr(blk("tt", s, 64), blk("ox", s + 1, 64), [OX[s + 1]], ["tt%d" % s])
-        cp(col("of", 24, 8) if s == 6 else blk("of", s, 4), T.tt[:, 64 * s:64 * s + 64:8 if s == 6 else 16], ["tt%d" % s], ["of%d" % s])
-
-    def places():
-        cp(T.rl[:], col("ox", 64, 448).indirect(T.lr7[:]), OX[1:] + ["lr7"], ["rl"])
-        tr(col("tl", 0, 128), T.rl[:], ["rl"], ["tl"])
-        cp(T.lw[:], T.tl[:].indirect(col("pk", 0)), ["tl", "tl7", "pk0"], ["lw"])
-
-    def decode(name, keys, w, q, s, key, scale, view=None):
-        for t in range(4):
-            mm(PS[t][:, 0:w], blk("qe", t), blk("se", t), q, s, ["qe", key], ["#%d" % t])
-        for t in range(4):
-            times(T[name][:, t:4 * w:4] if view else blk(name, t, w), PS[t][:, 0:w], ["#%d" % t], [keys[t]], scale)
-
-    FH4, DH4 = ["fh%d" % t for t in range(4)], ["dh%d" % t for t in range(4)]
+    pf = lambda k: col("pf", k)
     LW = col("lw", 0, 8)
+    L0, LWP, LC, LL, LE, LA, LB, LF = [col("ls_", a, n) for a, n in ((0, 4), (4, 1), (6, 2), (8, 2), (10, 2), (12, 2), (14, 2), (16, 1))]
 
+    def rawv(a, b, c0=0, c1=C):
+        return (T.raw[:, a:b, c0:c1], [("raw", sum(bits(C * m + c0, C * m + c1) for m in range(a, b)))], (b - a) * (c1 - c0), False, False)
+
+    fill(rawv(0, 5), 0)
+    for k in range(6):
+        dma("ys"[k % 2], "d0", hbm(T.tb[k:k + 1, :], "tb"), hbm(T.mp[:] if k % 5 == 0 else T.ar[:, 20 * k - 20:20 * k]), 1500)
+    dma("s", "d1", u8(R("wcs", 0, 256)), hbm(T.wc[:, 0:1024]), 1900)
+    dma("s", "d1", R("wps"), hbm(T.ws[:]), 1900)
+    dma("s", "d2", u8(R("wcs", 256, 512)), hbm(T.wc[:, 1024:2048]), 2300)
+    iota(col("pi", 11), [[0, 1]], 0, 1)
+    iota(R("dm"), [[-1, 128]], 0, 1)
+    iota(rawv(5, 8), [[0, 3 * C]], 0, 0)
+    last = []
+    for q in range(8):
+        p0 = 16 * q + (11 if q % 2 == 0 else 0)
+        last = [dma("y", "d3", (T.raw[p0:p0 + 5, :, :],) + rawv(0, 8)[1:], hbm(T.tb[1 - q % 2:6 - q % 2, :], "tb"), 2800, last)]
+    last = [dma("y", "d4", R("xi"), hbm(T.x[:]), 3500, last)]
     for m in range(8):
-        cp(col("mwf", 24 * m, 20), col("mwi", 24 * m, 20), ["mwi%d.%d" % (m, q) for q in range(8)], ["mwf%d" % m])
-        times(blk("yb", m, 320), col("mwf", 24 * m, 20).indirect(T.ly[:]), ["mwf%d" % m, "ly"], ["yb%d" % m], 1.0)
-        tr(blk("fw", 8 - m, 320), blk("yb", m, 320), ["yb%d" % m], ["fw%d" % m])
-        step(m)
-    quant(T.qx[:], T.sx[:], T.xi[:], ["xi"], ["qx"])
-    quant(T.qe[:], T.se[:], T.ce[:], ["ce%d" % t for t in range(4)], ["qe"])
-    decode("fh", FH4, 320, T.qx[:], T.sx[:], "qx", 0.5)
-    places()
+        last = [dma("y", "d5", col("ui", 8 * m, 8), hbm(T.u[:, 64 * m:64 * m + 8]), 3500, last)]
+    last = [dma("y", "d5", R("ui", 64, 512), hbm(T.u[:, 0:448]), 3500, last)]
+    dma("y", "d6", R("vi"), hbm(T.v[:]), 3500, last)
+    heir, giver = T.cores[(r - STEP[0]) % N], T.cores[(r + STEP[0]) % N]
+    send([(u8(R("wdc", 0, 256)), u8(R("wcs", 0, 256))), (R("wdp"), R("wps")), (u8(R("wdc", 256, 512)), u8(R("wcs", 256, 512)))], heir, "aw", 4500)
+    arrives("aw", giver, [R("wdc", 0, 256), R("wdp"), R("wdc", 256, 512)])
 
-    for t in range(5):
-        fill(sm1("sc", t), 32.0 ** -t, ["sc%d" % t])
-    fill(sm1("sc", 5), 0.0, ["sc5"])
-    ts(col("cj", 0, 128), col("ci", 0, 128), 15, Op.bitwise_and, ["cia"], ["cja"])
-    ts(col("cj", 128, 8), col("ci", 128, 8), 4, Op.arith_shift_right, ["cib"], ["cjb"])
-    ts(T.mod[:], col("cj", 0, 128), 0.0, Op.is_equal, ["cja"], ["mod"])
-    ts(T.m8[:], col("cj", 128, 8), 0.0, Op.is_equal, ["cjb"], ["m8"])
+    for k, sh, an in ((0, 0, 15), (1, 4, 1), (2, 5, 1), (3, 6, 1), (4, 0, 1), (5, 1, 1), (6, 2, 1), (7, 0, 7), (8, 3, 1), (9, 4, 7), (10, 0, 31)):
+        ts(col("pi", k), col("pi", 11), sh, Op.logical_shift_right, an, Op.bitwise_and)
+    cp(col("pf", 0, 12), col("pi", 0, 12))
+    i_, h_, y_, b_, x0, x1, x2, g8, x3, g_, p31, p_ = [pf(k) for k in range(12)]
+    iota(R("nat"), [[1, 320]], 0, 0)
+    iota(col("cf", 0, 32), [[0, 4], [1, 8]], 0, 0)
+    iota(R("ci"), [[-1, 128]], 128, 1)
+    iota(col("wf", 0, 160), [[0, 160]], 0, 1)
+    ts(L0, col("nat", 0, 4), 32.0, Op.mult, p31, Op.add)
+    fill(R("ze"), 0.0)
+    ts(R("ze", 3, 515, 4), R("dm"), 0.0, Op.is_equal, 0.5, Op.mult)
+    for t in range(4):
+        quant(blk("qe", t), blk("se", t), col("ze", 3 - t, 512))
+    for s in range(9):
+        fill(col("oxf", 80 * s, 16), 0.0)
+    fill(col("fw", 8 * C, J), 0.0)
+    fma(pf(12), x0, -65.0, 64.0)
+    fma(pf(13), x1, -95.0, pf(12))
+    fma(pf(14), pf(13), h_, x0)
+    fma(pf(15), x2, 32.0, 175.0)
+    fma(pf(16), x1, 96.0, pf(15))
+    fma(pf(17), g_, 160.0, pf(16))
+    ts(LWP, pf(14), pf(17), Op.add)
+    ts(pf(18), y_, h_, Op.not_equal)
+    fma(pf(19), y_, 32.0, 64.0)
+    fma(pf(20), b_, 32.0, 15.0)
+    fma(pf(21), pf(18), pf(19), pf(20))
+    fma(pf(22), h_, 1.0, pf(21))
+    fma(pf(23), y_, 1.0, pf(20))
+    fma(pf(24), h_, 6.0, pf(21))
+    fma(pf(25), y_, 6.0, pf(20))
+    fma(pf(26), pf(22), -1.0, pf(23))
+    fma(pf(27), pf(24), -1.0, pf(25))
+    fma(pf(28), g8, 160.0, pf(22))
+    fma(pf(29), g8, 160.0, pf(23))
+    fma(pf(30), g8, 160.0, pf(24))
+    fma(pf(31), pf(26), x0, pf(28))
+    fma(pf(32), pf(26), x0, 0.0)
+    fma(pf(33), pf(27), x0, pf(30))
+    fma(pf(34), x3, 1.0, pf(33))
+    fma(pf(35), pf(32), -1.0, pf(29))
+    ts(LL, col("cf", 0, 16)[:1] and R("cf", 0, 16, 8), pf(31), Op.add, 160.0, Op.add)
+    ts(LE, R("cf", 0, 16, 8), pf(35), Op.add)
+    ts(LC, R("nat", 156, 160, 2), pf(34), Op.add)
+    fma(pf(36), g8, 2.0, 16.0)
+    ts(LA, col("nat", 0, 2), -16.0, Op.mult, pf(36), Op.add)
+    fma(pf(37), x3, -16.0, pf(36))
+    ts(LB, R("cf", 1, 17, 8), pf(37), Op.add)
+    fma(pf(38), g8, 8.0, 8.0)
+    fma(pf(39), g8, 1.0, 2.0)
+    ts(LF, pf(38), pf(39), Op.mult, -1.0, Op.add)
+    ts(pf(40), p31, 15.0, Op.is_ge)
+    ts(pf(41), p31, 16.0, Op.is_le, pf(40), Op.mult)
+    fma(R("kb"), col("cf", 0, 32), -1024.0 * C, 1024.0 * (8 * C + J))
+    fma(col("yy", 32), p_, -1024.0, 1024.0 * J)
+    fma(col("cf", 32, 16), col("nat", 0, 16), 16.0, i_)
+    times(sm("jw"), col("cf", 32, 16), 1.0 / 256)
+    fma(sm("jc", 0, 8), col("cf", 32, 8), 1.0, -1.0 * J)
+    fma(sm("xj", 1, 16, 2), col("cf", 32, 8), 4.0, 4.0 * C)
+    fill(R("fs", SMALL["wn"], SMALL["wn"] + 32), 0.0)
+    fill(R("stp"), 1.0 / 256)
+    for k, t in enumerate((3, 2, 4, 3, None, 4, 1, 0, 2, 1)):
+        fill(sm("sc", k, k + 1), 0.0 if t is None else 32.0 ** -t)
+    fill(sm("sd", 0, 10), 0.0)
+    ts(sm("sd", 1, 10, 2), sm("sd", 0, 10, 2), -32.0, Op.add)
+    ts(R("idb"), R("dm"), 0.0, Op.is_equal)
+    ts(R("tril"), R("dm"), 0.0, Op.is_gt)
+    ts(R("cj"), R("ci"), 15, Op.bitwise_and)
+    ts(R("mod"), R("cj"), 0.0, Op.is_equal)
+    ts(R("m8"), col("nat", 0, 8), g_, Op.is_equal)
+    for n, w in (("za", 516), ("zb", 516), ("ba", 516), ("bb", 512), ("b2", 512)):
+        times(col(n, 0, w), col("ze", 0, w), 0.0)
+    fill(col("ba", 516, 28), 0.0)
     for t in range(3):
-        ts(T.ca[:, 512 * t + t:512 * t + 512:4], T.mod[:], 0.0, Op.mult, ["mod", "ca"], ["ca.%d" % t], 32.0 ** t, Op.add)
-        ts(T.cb[:, 512 * t + t:512 * t + 512:4], T.mod[:], 32.0 ** t, Op.mult, ["mod", "cb"], ["cb.%d" % t])
-    quant(T.qa[:], T.sa[:], T.ca[:], ["ca"] + ["ca.%d" % t for t in range(3)], ["qa"])
-    quant(T.qb[:], T.sb[:], T.cb[:], ["cb"] + ["cb.%d" % t for t in range(3)], ["qb"])
-    quant(T.qu[:], T.su[:], T.ui[:], ["ui%d" % m for m in range(9)], ["qu"])
-    quant(T.qv[:], T.sv[:], T.vi[:], ["vi"], ["qv"])
-    ts(sm("jw"), col("nat", 0, 8), 16.0, Op.mult, ["nat", "pf"], ["jw"], pf(0), Op.add)
-    ts(pf(19), pf(7), 2.0, Op.mult, ["pf"], ["pf19"])
-    ts(pf(20), pf(8), -16.0, Op.mult, ["pf"], ["pf20"], 17.0, Op.add)
-    ts(sm("jd"), sm("jw"), 4.0, Op.mult, ["jw"], ["jd"], 1280.0, Op.add)
-    ts(col("yy", 32), pf(9), 1024.0, Op.mult, ["pf"], ["yyc"])
-    ts(col("la", 0, 2), col("cf", 56, 2), pf(19), Op.add, ["cf3", "pf19"], ["la0"])
-    tt(pf(21), pf(20), pf(19), Op.add, ["pf20", "pf19"], ["pf21"])
-    ts(col("la", 2, 2), col("nat", 0, 2), 0.0, Op.mult, ["nat", "pf21"], ["la1"], pf(21), Op.add)
-    cp(T.cwf[:], T.cwi[:], ["cwi%d" % i for i in range(16)], ["cwf"])
-    ts(pf(22), pf(3), -327680.0, Op.mult, ["pf"], ["pf22"], 2621440.0, Op.add)
+        fma(R("za", 3, 515, 4), R("mod"), 0.0, 32.0 ** t)
+        quant(blk("qa", t), blk("sa", t), col("za", 3 - t, 512))
+        times(R("zb", 3, 515, 4), R("mod"), 32.0 ** t)
+        quant(blk("qb", t), blk("sb", t), col("zb", 3 - t, 512))
+    quant(R("qu"), R("su"), R("ui"))
+    quant(R("qv"), R("sv"), R("vi"))
 
-    heir = T.cores[(r - STEP[2]) % N]
-    send([(T.wdp[:], T.wps[:])], heir, "aw", ["wps"])
+    for a in (0, 4):
+        for i in range(16):
+            o, v = R("fw", C * a + i, C * a + 4 * C, 16), rawv(a, a + 4, 20 * i, 20 * i + 20)
+            either(o, v, lambda o=o, v=v: V.tensor_copy(o[0], v[0]), lambda o=o, v=v: S.activation(o[0], v[0], Act.Copy))
+
+    def chase():
+        for s in range(8):
+            win = blk("fw", s, C)
+            lst = [col("ls_", 2 * b, 2) if s == 0 else col("ot", 66 * s - 50 + 32 * b, 2) for b in range(2)]
+            if s < 7:
+                for b in range(2):
+                    cp(col("ox", 64 * s + 32 * b, 32), by(win, lst[b]))
+                tr(col("ot", 66 * s + 1, 64), blk("ox", s, 64))
+            for b in range(2):
+                times(col("oxf", 16 + 80 * s + 32 * b, 32), by(win, lst[b]), 1.0, "vs" if s == 7 else "s")
+            tr(col("wf", 160 * s + 160, 64), col("oxf", 16 + 80 * s, 64))
+            tr(col("wf", 160 * s + 224, 96), col("oxf", 80 * s, 96))
+        cp(R("lw"), by(R("wf"), LWP))
+
+    def asks():
+        cc, d, ke, kd, v, ne, pp = [blk("pw", k, 32) for k in range(7)]
+        times(cc, by(R("wf"), LC), 1.0)
+        tt(d, by(R("wf"), LL), cc, Op.subtract)
+        times(ke, by(R("wf"), LE), -1024.0)
+        tt(kd, d, R("kb"), Op.add)
+        ts(ne, d, 0.0, Op.not_equal)
+        tt(v, ke, kd, Op.add)
+        tt(pp, v, ne, Op.mult)
+        return pp
+
+    def unpack(bank, w, q, s, planes=range(4)):
+        for t in planes:
+            mm(ps(bank + t, 0, w), blk("qe", t), blk("se", t), q, s)
+
+    def state():
+        unpack(0, C, R("qx"), R("sx"))
+        for t in range(4):
+            times(blk("fh", t, C), ps(t, 0, C), 1.0)
+        for t in range(4):
+            times(R("xt", t, 4 * C, 4), blk("fh", t, C), 2.0)
+
+    def whole():
+        for t in range(4):
+            cp(by(R("xt"), blk("xl", t, 8)), R("nt", t, 512, 4))
+        quant(R("qx"), R("sx"), col("xt", 0, 4 * C))
+
+    quant(R("qx"), R("sx"), R("xi"))
+    state()
+    chase()
     for k in range(3):
         donor, client = T.cores[(r + STEP[k]) % N], T.cores[(r - STEP[k]) % N]
-        qm, sp, qh, sh = [T["%s%d" % (n, k)] for n in ("qm", "sm", "qh", "sh")]
-        if k == 0:
-            for t in range(4):
-                times(T.mt[:, t:512:4], blk("fh", t, 320).indirect(LW), [FH4[t], "lw"], [M4[t]], 2.0)
-        else:
-            quant(T.qn[:], T.sn[:], T.nt[:], N4, ["qn"])
-            decode("mt", M4, 128, T.qn[:], T.sn[:], "qn", 1.0, True)
-        quant(qm[:], sp[:], T.mt[:], M4, ["qm%d" % k])
-        mc, mp, mkey, wc, wp, wkeys = qm, sp, "qm%d" % k, T.wdc, T.wdp, ["wd"]
-        hc, hp, hkey = qh, sh, "qh%d" % k
-        if k < 2:
-            send([(T["mc%d" % k][:].bitcast(B8), qm[:].bitcast(B8)), (T["mp_%d" % k][:], sp[:])], donor, "am%d" % k, ["qm%d" % k])
-            mc, mp, mkey, wc, wp, wkeys = T["mc%d" % k], T["mp_%d" % k], "mc%d" % k, T.wcs, T.wps, ["wcs", "wps"]
-            arrives("am%d" % k, client, [mkey])
-        for b in range(4):
-            mm(PS[b][:, 0:128], wc[:, 128 * b:128 * b + 128], wp[:, 128 * b:128 * b + 128], mc[:], mp[:], wkeys + [mkey], ["#%d" % b])
-        for b in range(4):
-            o, i = T.ht[:, b:512:4], PS[b][:, 0:128]
-            op("vs", lambda e, o=o, i=i: V.tensor_scalar(o, i, 0.0, 0.03125, Op.max, Op.mult) if e == "v" else S.activation(o, i, Act.Relu, scale=0.03125), ["#%d" % b], [H4[b]])
-        quant(qh[:], sh[:], T.ht[:], H4, ["qh%d" % k])
-        if k < 2:
-            send([(T["hc%d" % k][:].bitcast(B8), qh[:].bitcast(B8)), (T["hp%d" % k][:], sh[:])], client, "ah%d" % k, ["qh%d" % k])
-            hc, hp, hkey = T["hc%d" % k], T["hp%d" % k], "hc%d" % k
-            arrives("ah%d" % k, donor, [hkey])
-            if k == 0:
-                send([(T.wdc[:].bitcast(B8), T.wcs[:].bitcast(B8))], heir, "aw", ["wcs"])
-                arrives("aw", T.cores[(r + STEP[2]) % N], ["wd"])
-        cp(T.rle[:], T.ox[:].indirect(T.lr[:]), OX + ["lr"], ["rle"])
-        tr(T.te[:], T.rle[:], ["rle"], ["te"])
-        cp(T.ew[:], T.te[:].indirect(col("pk", 2, 2)), ["te", "pk1"], ["ew"])
-        ts(T.e1[:], T.ew[:], 15, Op.bitwise_and, ["ew"], ["e1"])
-        ts(T.e2[:], T.ew[:], 4, Op.logical_shift_right, ["ew"], ["e2"])
-        cp(T.el[:], col("ew", 0, 8), ["ew"], ["el"])
-        ts(T.e3[:], T.e1[:], 80.0, Op.mult, ["e1"], ["e3"])
-        tt(T.ec[:], T.e2[:], T.k20[:], Op.add, ["e2", "k20"], ["ec"])
-        tt(T.e1[:], T.e3[:], T.ec[:], Op.add, ["e3", "ec"], ["e1"])
-        cp(T.lc[:], T.e1[:], ["e1"], ["lc"])
-        times(T.rf[:, 4:768:6], T.nat[:].indirect(LW), ["nat", "lw"], ["rf4"], 1.0)
-        op("s", lambda _: S.activation(T.rf[:, 5:768:6], T.nat[:].indirect(T.el[:]), Act.Identity, scale=1024.0, bias=pf(22)), ["nat", "el", "pf22"], ["rf5"])
-        for q in range(4):
-            times(T.rf[:, q:768:6], T.cwf[:].indirect(blk("lc", q, 8)), ["cwf", "lc"], ["rf%d" % q], 1.0)
-        for m in range(8):
-            dma("y", "dc", blk("cp", m, 6), T.rf[16 * m:16 * m + 1, 0:768], ["rf%d" % q for q in range(6)], ["cp%d" % m], k)
-        C = ["cp%d" % m for m in range(8)]
-        for q in range(4):
-            tt(blk("ne", q, 8), T.cp[:, q:48:6], T.cp[:, 4:48:6], Op.not_equal, C, ["ne%d" % q])
-            tt(blk("sk", q, 8), T.cp[:, q:48:6], T.cp[:, 5:48:6], Op.add, C, ["sk%d" % q])
-        tt(T.pp[:], T.ne[:], T.sk[:], Op.mult, ["ne%d" % q for q in range(4)] + ["sk%d" % q for q in range(4)], ["pp"])
+        qm, sp, qh, sh = [R("%s%d" % (n, k)) for n in ("qm", "sm", "qh", "sh")]
+        pp = asks()
         if k:
+            quant(R("qn"), R("sn"), R("nt"))
+            unpack(0, J, R("qn"), R("sn"))
             for t in range(4):
-                cp(T.xt[:].indirect(blk("xl", t, 8)), T.nt[:, t:512:4], ["xl%d" % t, N4[t]], X4)
-            quant(T.qx[:], T.sx[:], col("xt", 0, 1280), X4, ["qx"])
-            decode("fh", FH4, 320, T.qx[:], T.sx[:], "qx", 0.5)
+                times(blk("dn", t), ps(t, 0, J), 1.0)
         for t in range(4):
-            times(T.xt[:, t:1280:4], blk("fh", t, 320), [FH4[t]], [X4[t]], 2.0)
-        mm(PS[4][:, 0:128], hc[:], hp[:], T.qu[:], T.su[:], [hkey, "qu"], ["#4"])
-        ts(col("sg", 0, 16), PS[4][:, 0:16], 0.0, Op.is_gt, ["#4"], ["sg0"])
-        ts(col("sg", 16, 16), PS[4][:, 0:16], 0.0, Op.is_le, ["#4"], ["sg1"])
-        tt(T.xx[:], T.sg[:].indirect(col("la", 0, 2)), T.pp[:], Op.mult, ["sg0", "sg1", "la0", "pp"], ["xx"])
-        tt(col("yy", 0, 32), T.sg[:].indirect(col("la", 2, 2)), T.xx[:], Op.mult, ["sg0", "sg1", "la1", "xx"], ["yy"])
-        red(sm("rq", 1), col("yy", 0, 33), Op.max, ["yy", "yyc"], ["rq"])
-        ts(col("qd", 0, 6), sm("sc", 6), sm("rq", 1), Op.mult, ["rq"] + ["sc%d" % t for t in range(6)], ["qd"])
-        ts(sm("nq", 5), col("qd", 1, 5), -32.0, Op.mult, ["qd"], ["nq"])
-        tt(sm("dg", 5), sm("nq", 5), col("qd", 0, 5), Op.add, ["nq", "qd"], ["dg"])
-        for t in range(3):
-            times(T.b1[:, t:512:4], T.idb[:], ["idb", "dg", "b1"], ["ba%d" % t], sm1("dg", 2 + t))
-        quant(blk("qk", 0), blk("sk1", 0), col("b1", 0, 512), ["ba%d" % t for t in range(3)] + ["b1"], ["qk0"])
-        for t in range(3):
-            mm(PS[5][:, 0:128], blk("qa", t), blk("sa", t), blk("qk", 0), blk("sk1", 0), ["qa", "qk0"], ["#5"], t == 0, t == 2)
+            times(R("mt", t, 512, 4), by(blk("dn", t), col("fl", 0, 8)) if k else by(blk("fh", t, C), LW), 2.0)
+        quant(qm, sp, R("mt"))
+        mc, mp, wc, wp, hc, hp = qm, sp, "wdc", "wdp", qh, sh
+        if k:
+            mc, mp, wc, wp, hc, hp = R("mc%d" % k), R("mp_%d" % k), "wcs", "wps", R("hc%d" % k), R("hp%d" % k)
+            send([(u8(mc), u8(qm)), (mp, sp)], donor, "am%d" % k, 2200)
+            arrives("am%d" % k, client, [mc, mp])
+            whole()
+            state()
+        for b in range(4):
+            mm(ps(4 + b, 0, J), blk(wc, b), blk(wp, b), mc, mp)
+        for b in range(4):
+            o, i = R("ht", b, 512, 4), ps(4 + b, 0, J)
+            either(o, i, lambda o=o, i=i: V.tensor_scalar(o[0], i[0], 0.0, 0.03125, Op.max, Op.mult), lambda o=o, i=i: S.activation(o[0], i[0], Act.Relu, scale=0.03125))
+        quant(qh, sh, R("ht"))
+        if k:
+            send([(u8(hc), u8(qh)), (hp, sh)], client, "ah%d" % k, 2200)
+            arrives("ah%d" % k, donor, [hc, hp])
+        mm(ps(4, 0, J), hc, hp, R("qu"), R("su"))
+        unpack(0, J, hc, hp)
         for t in range(2):
-            times(T.b1[:, 512 + t:1024:4], T.idb[:], ["idb", "dg", "b1"], ["bb%d" % t], sm1("dg", t))
+            times(blk("dh", t), ps(t, 0, J), 1.0, "s")
+        ts(col("sg", 0, 16), ps(4, 0, 16), 0.0, Op.is_gt)
+        ts(col("sg", 16, 16), ps(4, 0, 16), 0.0, Op.is_le)
+        tt(R("xx"), by(R("sg"), LA), pp, Op.mult)
+        tt(col("yy", 0, 32), by(R("sg"), LB), R("xx"), Op.mult)
+        red(sm("rq", 0, 1), col("yy", 0, 33), Op.max, negate=True)
+        ts(col("qd", 0, 10), sm("sc", 0, 10), sm("rq", 0, 1), Op.mult)
+        scan(sm("dg", 0, 10), sm("sd", 0, 10), col("qd", 0, 10), Op.mult, Op.add)
+        dg = lambda c: sm("dg", c, c + 1)
         for t in range(3):
-            times(T.b1[:, 1024 + t:1056:4], T.m8[:], ["m8", "dg", "b1"], ["bc%d" % t], sm1("dg", 2 + t))
-        ts(sm("kf", 1), col("qd", 2), 1.0, Op.add, ["qd"], ["kf"])
-        quant(blk("qk", 2), blk("sk1", 2), col("b1", 1024, 512), ["bc0", "bc1", "bc2", "b1"], ["qk2"])
+            times(R("ba", t, 512, 4), R("idb"), dg(1 + 2 * t))
+            times(R("ba", 512 + t, 544, 4), R("m8"), dg(1 + 2 * t))
+        quant(R("qk"), R("sk"), R("ba"))
         for t in range(3):
-            mm(PS[7][:, 0:128], blk("qb", t), blk("sb", t), blk("qk", 2), blk("sk1", 2), ["qb", "qk2"], ["#7"], t == 0, t == 2)
-        times(sm("kw"), PS[7][:, 0:8], ["#7"], ["kw"], 1.0)
-        ts(T.kt[:], T.tril[:], sm("kf", 1), Op.mult, ["tril", "kf"], ["kt"], -1.0, Op.add)
-        tt(T.eq[:], PS[5][:, 0:128], T.kt[:], Op.is_equal, ["#5", "kt"], ["eq"])
-        red(sm("lo", 1), T.eq[:], Op.max, ["eq"], ["lo"])
-        ts(T.b2[:, 0:32:4], T.m8[:], sm("lo", 1), Op.mult, ["m8", "lo", "b2"], ["b2a"])
-        quant(T.ql[:], T.sl[:], T.b2[:], ["b2", "b2a"], ["ql"])
-        mm(PS[4][:, 0:128], blk("qb", 0), blk("sb", 0), T.ql[:], T.sl[:], ["qb", "ql"], ["#4"])
-        quant(blk("qk", 1), blk("sk1", 1), col("b1", 512, 512), ["bb0", "bb1", "b1"], ["qk1"])
+            mm(ps(5, 0, J), blk("qa", t), blk("sa", t), col("qk", 0, J), col("sk", 0, J), t == 0, t == 2)
+        for t in range(3):
+            mm(ps(7, 0, J), blk("qb", t), blk("sb", t), col("qk", 8, J), col("sk", 8, J), t == 0, t == 2)
         for t in range(2):
-            mm(PS[6][:, 0:128], blk("qa", t), blk("sa", t), blk("qk", 1), blk("sk1", 1), ["qa", "qk1"], ["#6"], t == 0, t == 1)
-        times(T.va[:], PS[6][:, 0:128], ["#6"], ["va"], 1.0)
-        tt(sm("dj"), sm("jw"), sm("kw"), Op.subtract, ["jw", "kw"], ["dj"])
-        tt(sm("t1"), PS[4][:, 0:8], sm("dj"), Op.mult, ["#4", "dj"], ["t1"])
-        tt(sm("t2"), sm("t1"), sm("kw"), Op.add, ["t1", "kw"], ["t2"])
-        cp(T.ofs[:], sm("t2"), ["t2"], ["ofs"])
-        cp(T.fw[:].indirect(T.ofs[:]), T.va[:], ["ofs", "va"], FWALL)
-        decode("dh", DH4, 128, hc[:], hp[:], hkey, 0.5)
+            times(R("bb", t, 512, 4), R("idb"), dg(7 + 2 * t))
+        quant(R("qw"), R("sw"), R("bb"))
+        for t in range(2):
+            mm(ps(6, 0, J), blk("qa", t), blk("sa", t), R("qw"), R("sw"), t == 0, t == 1)
+        times(R("va"), ps(6, 0, J), pf(41), "s")
+        ts(R("kl"), ps(7, 120, 128), 8.0 * C + J, Op.add)
+        ts(sm("dk", 1, 16, 2), ps(7, 120, 128), 8.0 * C + J, Op.add)
+        tt(sm("dk", 0, 16, 2), sm("jc", 0, 8), ps(7, 120, 128), Op.subtract)
+        tt(R("nv"), by(R("fw"), R("kl")), R("va"), Op.add)
+        times(R("kt"), R("tril"), dg(8))
+        tt(R("eq"), ps(5, 0, J), R("kt"), Op.is_equal)
+        red(sm("lo", 0, 1), R("eq"), Op.max)
+        times(R("b2", 4, 64, 8), R("m8"), sm("lo", 0, 1), "v")
+        quant(R("ql"), R("sl"), R("b2"))
+        mm(ps(4, 0, J), blk("qb", 0), blk("sb", 0), R("ql"), R("sl"))
+        scan(sm("of"), ps(4, 0, 16), sm("dk"), Op.mult, Op.add)
+        cp(R("ofs"), sm("of", 1, 16, 2))
+        cp(by(R("fw"), R("ofs")), R("nv"))
         if k == 2:
-            for m in range(8):
-                dma("y", "do", T.fo[m:m + 1, :], T.fw[0:1, 320 * (8 - m):320 * (8 - m) + 320], ["fw%d" % m], [])
-        for s in range(8):
-            step(s)
-        places()
-        ts(sm("nl"), LW, -512.0, Op.mult, ["lw"], ["nl"])
-        tt(T.kk[:], T.nat512[:].indirect(LW), col("nat", 0, 128), Op.add, ["nat512", "lw", "nat"], ["kk"])
-        for c in range(8):
-            n = 16 * c + 16
-            d, b, i = col("dd", 128 * c, n), sm1("nl", c), col("kk", 0, n)
-            op("vs", lambda e, d=d, b=b, i=i: V.tensor_scalar(d, i, b, None, Op.add) if e == "v" else S.activation(d, i, Act.Identity, bias=b), ["kk", "nl"], ["dd%d" % c])
-        for c in range(8):
-            red(sm1("fi", c), col("dd", 128 * c, 16 * c + 16), Op.min, ["dd%d" % c], ["fi%d" % c], apply_absolute_value=True)
+            dma("y", "d7", hbm(T.fo[:]), (T.fw[15:16, 0:8 * C],) + col("fw", 0, 8 * C)[1:], 1500)
+        chase()
         for t in range(4):
-            times(blk("fg", t), blk("fh", t, 320).indirect(LW), [FH4[t], "lw"], ["fg%d" % t], 1.0)
-        cp(T.fl[:], sm("fi"), ["fi%d" % c for c in range(8)], ["fl"])
-        tt(sm("wn"), sm("fi"), sm("jw"), Op.is_equal, ["fi%d" % c for c in range(8)] + ["jw"], ["wn"])
-        ts(sm("xd"), LW, 4.0, Op.mult, ["lw"], ["xd"])
-        tt(sm("xe"), sm("xd"), sm("jd"), Op.subtract, ["xd", "jd"], ["xe"])
-        tt(sm("xd"), sm("xe"), sm("wn"), Op.mult, ["xe", "wn"], ["xd"])
-        tt(sm("xe"), sm("xd"), sm("jd"), Op.add, ["xd", "jd"], ["xe"])
+            if t < 2:
+                tt(R("nt", t, 512, 4), by(blk("fh", t, C), LW), blk("dh", t), Op.add)
+            else:
+                times(blk("fg", t - 2), by(blk("fh", t, C), LW), 1.0)
+                tt(R("nt", t, 512, 4), ps(t, 0, J), blk("fg", t - 2), Op.add)
+        times(sm("nl"), by(R("wf"), LWP), -1.0)
+        times((T.lrow[:, ::-1],) + R("lrow")[1:], by(R("nat"), LW), 1.0)
+        for c in range(7, -1, -1):
+            o, i, b = col("ne", 8 * c * (c + 1), 16 * c + 16), R("lrow", 112 - 16 * c), sm("nl", c, c + 1)
+            either(o, i, lambda o=o, i=i, b=b: V.tensor_scalar(o[0], i[0], b[0], 0.0, Op.add, Op.not_equal), lambda o=o, i=i, b=b: S.activation(o[0], i[0], Act.Abs, bias=b[0]), [b])
+        scan(R("so"), R("stp"), R("ne"), Op.add, Op.min)
+        if k < 2:
+            ts(R("fl"), by(R("so"), LF), 256.0, Op.mult)
+        times(sm("xm", 0, 8), sm("nl", 0, 8), -4.0)
+        tt(sm("xj", 0, 16, 2), sm("xm", 0, 8), sm("xj", 1, 16, 2), Op.subtract)
+        tt(R("fs", SMALL["wn"] + 1, SMALL["wn"] + 32, 2), by(R("so"), LF), sm("jw"), Op.is_equal)
+        scan(sm("xe"), sm("wn"), sm("xj"), Op.mult, Op.add)
         for t in range(4):
-            ts(blk("xl", t, 8), sm("xe"), float(t), Op.add, ["xe"], ["xl%d" % t])
-        for t in range(4):
-            tt(T.nt[:, t:512:4], blk("dh", t).indirect(T.fl[:]), blk("fg", t), Op.add, [DH4[t], "fl", "fg%d" % t], [N4[t]])
-    for t in range(4):
-        cp(T.xt[:].indirect(blk("xl", t, 8)), T.nt[:, t:512:4], ["xl%d" % t, N4[t]], X4)
-    quant(T.qx[:], T.sx[:], col("xt", 0, 1280), X4, ["qx"])
-    mm(PS[4][:, 0:320], T.qv[:], T.sv[:], T.qx[:], T.sx[:], ["qv", "qx"], ["#4"])
-    dma("y", "do", T.oc[:], T.qx[:].bitcast(B8), ["qx"], [])
+            ts(blk("xl", t, 8), sm("xe", 1, 16, 2), float(t), Op.add)
+    whole()
+    dma("y", "d8", hbm(T.oc[:]), u8(R("qx")), 1800)
+    for a in range(2):
+        mm(ps(4 + a, 0, 160), R("qv"), R("sv"), blk("qx", a, 160), blk("sx", a, 160))
+        times(blk("yo", a, 160), ps(4 + a, 0, 160), 1.0, "vs"[a])
+        dma("ys"[a], "d%d" % (9 + a), hbm(T.y[:, 160 * a:160 * a + 160]), blk("yo", a, 160), 1600)
     for i in range(4):
-        dma("y", "do", T.osc[4 * i:4 * i + 4, :], T.sx[32 * i:32 * i + 4, :], ["qx"], [])
-    times(T.yo[:], PS[4][:, 0:320], ["#4"], ["yo"], 1.0)
-    dma("s", "do", T.y[:], T.yo[:], ["yo"], [])
+        dma("y", "d11", hbm(T.osc[4 * i:4 * i + 4, :]), (T.sx[32 * i:32 * i + 4, :],) + R("sx")[1:], 1400)
     return ops
 
 
 def orders(ops):
-    wr, rd, out = {}, {}, []
-    for i, (q, _, reads, writes, kind, _, _) in enumerate(ops):
+    seen, out, group = {}, [], {}
+    for i, o in enumerate(ops):
+        if o["kind"] == "dma":
+            group.setdefault(o["sem"], []).append(i)
+    for i, o in enumerate(ops):
         p = set()
-        for k in reads:
-            p.update(wr.get(k, []))
-            if k[0] == "#":
-                p.update(j for j in rd.get(k, []) if len(q + ops[j][0]) > 2 or ops[j][0] != q)
-        for k in writes:
-            if kind != "send":
-                p.update(wr.get(k, []) + rd.get(k, []))
-        for k in reads:
-            rd.setdefault(k, []).append(i)
-        for k in writes:
-            wr[k] = wr[k] + [i] if kind == "send" and k in wr else [i]
-            rd[k] = []
-        out.append(p)
+        for writes, keys in ((False, o["r"]), (True, o["w"])):
+            for name, m in keys:
+                for j, m2, w2 in seen.get(name, []):
+                    if m & m2 and (writes or w2 or (name[0] == "#" and (len(o["q"]) > 1 or o["q"] != ops[j]["q"]))):
+                        if not (o["kind"] in ("dma", "send") and ops[j].get("sem") == o["sem"]):
+                            p.add(j)
+        for name, m in o["w"]:
+            keep = o["kind"] in ("dma", "send")
+            seen[name] = [x for x in seen.get(name, []) if x[1] & ~m or (keep and ops[x[0]].get("sem") == o["sem"])] + [(i, m, True)]
+        for name, m in o["r"]:
+            seen.setdefault(name, []).append((i, m, False))
+        p.discard(i)
+        out.append({k for j in p for k in (group[ops[j]["sem"]] if ops[j]["kind"] == "dma" else [j])})
     return out
 
 
-def listed(text, ops):
-    out = []
-    for w in text.split():
-        a, e = w.rstrip("*"), 1 if w[-1] == "*" else 0
-        lo, hi = (a.split("-") + [a])[:2] if "-" in a else (a, a)
-        out += [(k, ops[k][0][e]) for k in range(int(lo), int(hi) + 1)]
-    return out
+def plan(ops, before):
+    cost = lambda x, e: x[e] if isinstance(x, dict) else x
+    n = len(ops)
+    rest, after = [0.0] * n, [[] for _ in ops]
+    for i in range(n):
+        for j in list(before[i]) + ops[i].get("after", []):
+            after[j].append(i)
+    for i in range(n - 1, -1, -1):
+        rest[i] = cost(ops[i]["done"], ops[i]["q"][0]) + max([rest[j] + WAKE for j in after[i]] or [0.0])
+    busy, start, end, eng = {}, {}, {}, {}
+    for i in sorted(range(n), key=lambda k: (-rest[k], k)):
+        o, best = ops[i], None
+        ready = max([end[j] + (0 if o["kind"] == "acc" and ops[j]["q"] == "t" or o["kind"] == "arrival" else WAKE) for j in before[i]]
+                    + [start[j] + 1 for j in o.get("after", [])] + [0.0])
+        for e in o["q"]:
+            t, d = ready, cost(o["hold"], e)
+            for a, b in busy.get(e, []):
+                if t + d <= a:
+                    break
+                t = max(t, b)
+            if best is None or t + d < best[0] + best[1]:
+                best = (t, d, e)
+        t, d, e = best
+        start[i], end[i], eng[i] = t, t + cost(o["done"], e), e
+        if d:
+            busy[e] = sorted(busy.get(e, []) + [(t, t + d)])
+    return [(i, eng[i]) for i in sorted(range(n), key=lambda k: (start[k], k))]
 
 
 def rank_program(g, core, T, topo):
@@ -422,23 +457,22 @@ def rank_program(g, core, T, topo):
     ops = program(g, core, T, topo)
     before = orders(ops)
     Q = {"v": g.vector, "s": g.scalar, "t": g.tensor, "p": g, "y": g.sync}
-    known, tot, end, token = {q: {} for q in Q}, {}, {}, {}
-    for q, _, _, _, kind, sem, batch in ops:
-        if kind == "dma":
-            tot[sem] = tot.get(sem, 0) + 16
-            end[sem, batch] = tot[sem]
-        elif kind == "arrival":
-            tot[sem] = batch
-        elif kind == "send":
-            tot["ls"] = tot.get("ls", 0) + batch
-    for i, e in listed(ORDER_TEXT, ops) or [(k, ops[k][0][0]) for k in range(len(ops))]:
-        q, call, reads, writes, kind, sem, batch = ops[i]
-        if kind == "arrival":
-            token[i] = (sem, batch, {})
+    known, tot, token = {q: {} for q in Q}, {}, {}
+    for o in ops:
+        if o["kind"] == "dma":
+            tot[o["sem"]] = tot.get(o["sem"], 0) + 16
+        elif o["kind"] == "arrival":
+            tot[o["sem"]] = o["n"]
+        elif o["kind"] == "send":
+            tot["ls"] = tot.get("ls", 0) + o["n"]
+    for i, e in plan(ops, before):
+        o = ops[i]
+        if o["kind"] == "arrival":
+            token[i] = (o["sem"], o["n"], {})
             continue
         want = {}
         for j in before[i]:
-            if j not in token or (kind == "acc" and ops[j][0] == "t" and set(ops[j][3]) & set(writes)):
+            if j not in token or (o["kind"] == "acc" and ops[j]["q"] == "t" and ops[j]["w"] == o["w"]):
                 continue
             s, val, snap = token[j]
             if val > want.get(s, (0, None))[0]:
@@ -450,11 +484,11 @@ def rank_program(g, core, T, topo):
                 known[e][s] = val
                 for a, b in snap.items():
                     known[e][a] = max(known[e].get(a, 0), b)
-        ins = call(e)
-        if kind == "dma":
-            ins.then_inc(T.sem[sem], 16)
-            token[i] = (sem, end[sem, batch], dict(known[e]))
-        elif kind != "send":
+        ins = o["f"](e)
+        if o["kind"] == "dma":
+            ins.then_inc(T.sem[o["sem"]], 16)
+            token[i] = (o["sem"], tot[o["sem"]], dict(known[e]))
+        elif o["kind"] != "send":
             tot[e] = tot.get(e, 0) + 1
             ins.then_inc(T.sem[e], 1)
             token[i] = (e, tot[e], dict(known[e]))

@@ -24,9 +24,11 @@ for _n, _w, _t in (
 for _n in range(8):
     SCRATCH["p%d" % _n] = ("psum", [128, 512], F32)
 SMALL = {n: 16 * k for k, n in enumerate(("sc", "sd", "dg", "rq", "lo", "dk", "of", "jc", "nl", "jw", "xm", "xj", "xe", "wn", "wn_"))}
-SEMAPHORES = ["v", "s", "t", "p", "ls", "aw", "am1", "am2", "ah1", "ah2"] + ["d%d" % _n for _n in range(16)]
+SEMAPHORES = ["v", "s", "t", "p", "ls", "aw", "ac", "am1", "am2", "ah1", "ah2"] + ["d%d" % _n for _n in range(16)]
 STEP = [1, 2, 3]
-CYC, WAKE = 1.0, 130.0
+HOME = 2
+PASSES = 3
+CYC, WAKE = 1.0, 150.0
 
 
 def program(g, core, T, topo):
@@ -124,17 +126,17 @@ def program(g, core, T, topo):
         f = (lambda e: g.iota(out[0], pattern, base, cm, allow_small_or_imprecise_dtypes=True)) if flt else (lambda e: g.iota(out[0], pattern, base, cm))
         op("p", f, [out], [], 130 + 2 * out[2] * CYC)
 
-    def dma(q, sem, out, in_, done, after=()):
-        return op(q, lambda e: Q[e].dma_start(out[0], in_[0]), [out], [in_], 60, "dma", sem=sem, done=done, after=list(after))
+    def dma(q, sem, out, in_, done, after=(), behind=()):
+        return op(q, lambda e: Q[e].dma_start(out[0], in_[0]), [out], [in_] + list(behind), 60, "dma", sem=sem, done=done, after=list(after))
 
     def hbm(a, name="hbm"):
         return (a, [(name, 0 if name == "hbm" else 1)], 0, False, False)
 
-    def send(pairs, dst, sem, done):
+    def send(pairs, dst, sem, done, behind=()):
         rid, pid, _ = topo.addr(dst)
         mask, n = topo.mask(core, dst), len(topo.engines(core, dst))
         for out, in_ in pairs:
-            op("p", lambda e, out=out, in_=in_: g.remote_dma(out[0], in_[0], T.sem[sem], T.sem.ls, pid, rid, mask), [(0, [("sent" + sem, 1)])], [in_], 250, "send", sem=sem, n=n, done=done)
+            op("p", lambda e, out=out, in_=in_: g.remote_dma(out[0], in_[0], T.sem[sem], T.sem.ls, pid, rid, mask), [(0, [("sent" + sem, 1)])], [in_] + list(behind), 250 if any(o["kind"] == "send" for o in ops) else 1700, "send", sem=sem, n=n, done=done)
 
     def arrives(sem, src, outs):
         op("-", None, outs, [(0, [("sent" + sem, 1)])], 0, "arrival", sem=sem, n=len(outs) * len(topo.engines(src, core)))
@@ -146,27 +148,25 @@ def program(g, core, T, topo):
     def rawv(a, b, c0=0, c1=C):
         return (T.raw[:, a:b, c0:c1], [("raw", sum(bits(C * m + c0, C * m + c1) for m in range(a, b)))], (b - a) * (c1 - c0), False, False)
 
-    fill(rawv(0, 5), 0)
-    for k in range(6):
-        dma("ys"[k % 2], "d0", hbm(T.tb[k:k + 1, :], "tb"), hbm(T.mp[:] if k % 5 == 0 else T.ar[:, 20 * k - 20:20 * k]), 1500)
-    dma("s", "d1", u8(R("wcs", 0, 256)), hbm(T.wc[:, 0:1024]), 1900)
-    dma("s", "d1", R("wps"), hbm(T.ws[:]), 1900)
-    dma("s", "d2", u8(R("wcs", 256, 512)), hbm(T.wc[:, 1024:2048]), 2300)
+    fill(rawv(7, 8), 0)
+    fill(rawv(0, 1), 0)
+    for m in range(1, 7):
+        op("s", lambda e, m=m: S.activation(rawv(m, m + 1)[0], rawv(7, 8)[0], Act.Copy), [rawv(m, m + 1)], [rawv(7, 8)], C * CYC)
+    first = [dma("ys"[k % 2], "d0", hbm(T.tb[k:k + 1, :], "tb"), hbm(T.mp[:] if k % 5 == 0 else T.ar[:, 20 * k - 20:20 * k]), 1500) for k in range(6)]
+    dma("s", "d4", R("xi"), hbm(T.x[:]), 3000, first)
     iota(col("pi", 11), [[0, 1]], 0, 1)
     iota(R("dm"), [[-1, 128]], 0, 1)
-    iota(rawv(5, 8), [[0, 3 * C]], 0, 0)
     last = []
-    for q in range(8):
-        p0 = 16 * q + (11 if q % 2 == 0 else 0)
-        last = [dma("y", "d3", (T.raw[p0:p0 + 5, :, :],) + rawv(0, 8)[1:], hbm(T.tb[1 - q % 2:6 - q % 2, :], "tb"), 2800, last)]
-    last = [dma("y", "d4", R("xi"), hbm(T.x[:]), 3500, last)]
-    for m in range(8):
-        last = [dma("y", "d5", col("ui", 8 * m, 8), hbm(T.u[:, 64 * m:64 * m + 8]), 3500, last)]
-    last = [dma("y", "d5", R("ui", 64, 512), hbm(T.u[:, 0:448]), 3500, last)]
-    dma("y", "d6", R("vi"), hbm(T.v[:]), 3500, last)
-    heir, giver = T.cores[(r - STEP[0]) % N], T.cores[(r + STEP[0]) % N]
-    send([(u8(R("wdc", 0, 256)), u8(R("wcs", 0, 256))), (R("wdp"), R("wps")), (u8(R("wdc", 256, 512)), u8(R("wcs", 256, 512)))], heir, "aw", 4500)
-    arrives("aw", giver, [R("wdc", 0, 256), R("wdp"), R("wdc", 256, 512)])
+    for a in (0, 4):
+        for q in range(8):
+            p0 = 16 * q + (11 if q % 2 == 0 else 0)
+            last = [dma("y", "d%d" % (3 + 3 * a), (T.raw[p0:p0 + 5, a:a + 4, :],) + rawv(a, a + 4)[1:], hbm(T.tb[1 - q % 2:6 - q % 2, C * a:C * a + 4 * C], "tb"), 2200 + 150 * a, last)]
+    last = [dma("y", "d1", R("wps"), hbm(T.ws[:]), 3200, last)]
+    last = [dma("y", "d2", u8(R("wcs")), hbm(T.wc[:]), 4500, last)]
+    heir, giver = T.cores[(r - STEP[HOME]) % N], T.cores[(r + STEP[HOME]) % N]
+    send([(R("wdp"), R("wps"))], heir, "aw", 3000)
+    ops[-1]["early"] = 6000.0
+    arrives("aw", giver, [R("wdp")])
 
     for k, sh, an in ((0, 0, 15), (1, 4, 1), (2, 5, 1), (3, 6, 1), (4, 0, 1), (5, 1, 1), (6, 2, 1), (7, 0, 7), (8, 3, 1), (9, 4, 7), (10, 0, 31)):
         ts(col("pi", k), col("pi", 11), sh, Op.logical_shift_right, an, Op.bitwise_and)
@@ -174,16 +174,15 @@ def program(g, core, T, topo):
     i_, h_, y_, b_, x0, x1, x2, g8, x3, g_, p31, p_ = [pf(k) for k in range(12)]
     iota(R("nat"), [[1, 320]], 0, 0)
     iota(col("cf", 0, 32), [[0, 4], [1, 8]], 0, 0)
-    iota(R("ci"), [[-1, 128]], 128, 1)
-    iota(col("wf", 0, 160), [[0, 160]], 0, 1)
+    ts(R("ci"), R("dm"), 128.0, Op.add)
+    fma(col("wf", 0, 160), col("nat", 0, 160), 0.0, p_)
     ts(L0, col("nat", 0, 4), 32.0, Op.mult, p31, Op.add)
     fill(R("ze"), 0.0)
     ts(R("ze", 3, 515, 4), R("dm"), 0.0, Op.is_equal, 0.5, Op.mult)
     for t in range(4):
         quant(blk("qe", t), blk("se", t), col("ze", 3 - t, 512))
-    for s in range(9):
-        fill(col("oxf", 80 * s, 16), 0.0)
-    fill(col("fw", 8 * C, J), 0.0)
+    iota(R("oxf"), [[0, 656]], 0, 0)
+    iota(col("fw", 8 * C, J), [[0, J]], 0, 0)
     fma(pf(12), x0, -65.0, 64.0)
     fma(pf(13), x1, -95.0, pf(12))
     fma(pf(14), pf(13), h_, x0)
@@ -238,16 +237,13 @@ def program(g, core, T, topo):
     ts(R("cj"), R("ci"), 15, Op.bitwise_and)
     ts(R("mod"), R("cj"), 0.0, Op.is_equal)
     ts(R("m8"), col("nat", 0, 8), g_, Op.is_equal)
-    for n, w in (("za", 516), ("zb", 516), ("ba", 516), ("bb", 512), ("b2", 512)):
-        times(col(n, 0, w), col("ze", 0, w), 0.0)
-    fill(col("ba", 516, 28), 0.0)
+    for n in ("za", "zb", "ba", "bb", "b2"):
+        iota(R(n), [[0, R(n)[2]]], 0, 0)
     for t in range(3):
         fma(R("za", 3, 515, 4), R("mod"), 0.0, 32.0 ** t)
         quant(blk("qa", t), blk("sa", t), col("za", 3 - t, 512))
         times(R("zb", 3, 515, 4), R("mod"), 32.0 ** t)
         quant(blk("qb", t), blk("sb", t), col("zb", 3 - t, 512))
-    quant(R("qu"), R("su"), R("ui"))
-    quant(R("qv"), R("sv"), R("vi"))
 
     for a in (0, 4):
         for i in range(16):
@@ -260,7 +256,7 @@ def program(g, core, T, topo):
             lst = [col("ls_", 2 * b, 2) if s == 0 else col("ot", 66 * s - 50 + 32 * b, 2) for b in range(2)]
             if s < 7:
                 for b in range(2):
-                    cp(col("ox", 64 * s + 32 * b, 32), by(win, lst[b]))
+                    times(col("ox", 64 * s + 32 * b, 32), by(win, lst[b]), 1.0, "vs"[b])
                 tr(col("ot", 66 * s + 1, 64), blk("ox", s, 64))
             for b in range(2):
                 times(col("oxf", 16 + 80 * s + 32 * b, 32), by(win, lst[b]), 1.0, "vs" if s == 7 else "s")
@@ -290,14 +286,20 @@ def program(g, core, T, topo):
         for t in range(4):
             times(R("xt", t, 4 * C, 4), blk("fh", t, C), 2.0)
 
-    def whole():
-        for t in range(4):
+    def whole(last=False):
+        if last:
+            cp(by(R("xt"), R("xl")), R("nt"))
+        for t in range(0 if last else 4):
             cp(by(R("xt"), blk("xl", t, 8)), R("nt", t, 512, 4))
         quant(R("qx"), R("sx"), col("xt", 0, 4 * C))
 
     quant(R("qx"), R("sx"), R("xi"))
     state()
     chase()
+    for m in range(8):
+        dma("y", "d5", col("ui", 8 * m, 8), hbm(T.u[:, 64 * m:64 * m + 8]), 5500, last)
+    dma("y", "d5", R("ui", 64, 512), hbm(T.u[:, 0:448]), 5500, last)
+    quant(R("qu"), R("su"), R("ui"))
     for k in range(3):
         donor, client = T.cores[(r + STEP[k]) % N], T.cores[(r - STEP[k]) % N]
         qm, sp, qh, sh = [R("%s%d" % (n, k)) for n in ("qm", "sm", "qh", "sh")]
@@ -311,10 +313,12 @@ def program(g, core, T, topo):
             times(R("mt", t, 512, 4), by(blk("dn", t), col("fl", 0, 8)) if k else by(blk("fh", t, C), LW), 2.0)
         quant(qm, sp, R("mt"))
         mc, mp, wc, wp, hc, hp = qm, sp, "wdc", "wdp", qh, sh
+        x = 1 + k - (k > HOME)
+        if k != HOME:
+            mc, mp, wc, wp, hc, hp = R("mc%d" % x), R("mp_%d" % x), "wcs", "wps", R("hc%d" % x), R("hp%d" % x)
+            send([(u8(mc), u8(qm)), (mp, sp)], donor, "am%d" % x, 2800)
+            arrives("am%d" % x, client, [mc, mp])
         if k:
-            mc, mp, wc, wp, hc, hp = R("mc%d" % k), R("mp_%d" % k), "wcs", "wps", R("hc%d" % k), R("hp%d" % k)
-            send([(u8(mc), u8(qm)), (mp, sp)], donor, "am%d" % k, 2200)
-            arrives("am%d" % k, client, [mc, mp])
             whole()
             state()
         for b in range(4):
@@ -323,9 +327,14 @@ def program(g, core, T, topo):
             o, i = R("ht", b, 512, 4), ps(4 + b, 0, J)
             either(o, i, lambda o=o, i=i: V.tensor_scalar(o[0], i[0], 0.0, 0.03125, Op.max, Op.mult), lambda o=o, i=i: S.activation(o[0], i[0], Act.Relu, scale=0.03125))
         quant(qh, sh, R("ht"))
-        if k:
-            send([(u8(hc), u8(qh)), (hp, sh)], client, "ah%d" % k, 2200)
-            arrives("ah%d" % k, donor, [hc, hp])
+        if k != HOME:
+            send([(u8(hc), u8(qh)), (hp, sh)], client, "ah%d" % x, 2800)
+            arrives("ah%d" % x, donor, [hc, hp])
+        if k == 0:
+            send([(u8(R("wdc")), u8(R("wcs")))], heir, "ac", 6000, [hc])
+            arrives("ac", giver, [R("wdc")])
+            dma("y", "d6", R("vi"), hbm(T.v[:]), 2500, (), [R("wdc")])
+            quant(R("qv"), R("sv"), R("vi"))
         mm(ps(4, 0, J), hc, hp, R("qu"), R("su"))
         unpack(0, J, hc, hp)
         for t in range(2):
@@ -369,11 +378,12 @@ def program(g, core, T, topo):
             dma("y", "d7", hbm(T.fo[:]), (T.fw[15:16, 0:8 * C],) + col("fw", 0, 8 * C)[1:], 1500)
         chase()
         for t in range(4):
+            nt = blk("nt", t) if k == 2 else R("nt", t, 512, 4)
             if t < 2:
-                tt(R("nt", t, 512, 4), by(blk("fh", t, C), LW), blk("dh", t), Op.add)
+                tt(nt, by(blk("fh", t, C), LW), blk("dh", t), Op.add)
             else:
-                times(blk("fg", t - 2), by(blk("fh", t, C), LW), 1.0)
-                tt(R("nt", t, 512, 4), ps(t, 0, J), blk("fg", t - 2), Op.add)
+                times(blk("fg", t - 2), by(blk("fh", t, C), LW), 1.0, "s")
+                tt(nt, ps(t, 0, J), blk("fg", t - 2), Op.add)
         times(sm("nl"), by(R("wf"), LWP), -1.0)
         times((T.lrow[:, ::-1],) + R("lrow")[1:], by(R("nat"), LW), 1.0)
         for c in range(7, -1, -1):
@@ -388,7 +398,7 @@ def program(g, core, T, topo):
         scan(sm("xe"), sm("wn"), sm("xj"), Op.mult, Op.add)
         for t in range(4):
             ts(blk("xl", t, 8), sm("xe", 1, 16, 2), float(t), Op.add)
-    whole()
+    whole(True)
     dma("y", "d8", hbm(T.oc[:]), u8(R("qx")), 1800)
     for a in range(2):
         mm(ps(4 + a, 0, 160), R("qv"), R("sv"), blk("qx", a, 160), blk("sx", a, 160))
@@ -423,31 +433,54 @@ def orders(ops):
 
 
 def plan(ops, before):
-    cost = lambda x, e: x[e] if isinstance(x, dict) else x
     n = len(ops)
-    rest, after = [0.0] * n, [[] for _ in ops]
-    for i in range(n):
-        for j in list(before[i]) + ops[i].get("after", []):
-            after[j].append(i)
+    cost = lambda x, e: x[e] if isinstance(x, dict) else x
+    pre, post = [[] for _ in ops], [[] for _ in ops]
+    for i, o in enumerate(ops):
+        for j in before[i]:
+            pre[i].append((j, 0.0 if o["kind"] == "arrival" or (o["kind"] == "acc" and ops[j]["q"] == "t") else WAKE))
+        pre[i] += [(j, None) for j in o.get("after", [])]
+        for j, w in pre[i]:
+            post[j].append((i, w))
+
+    def lay(order, back):
+        busy, start, eng = {}, {}, {}
+        for i in order:
+            o, best = ops[i], None
+            for e in o["q"]:
+                d, full = cost(o["hold"], e), cost(o["done"], e)
+                if back:
+                    t = max([start[j] + cost(ops[j]["hold"], eng[j]) + (1 if w is None else w + full) - d for j, w in post[i]] + [full - d])
+                else:
+                    t = max([start[j] + (1 if w is None else w + cost(ops[j]["done"], eng[j])) for j, w in pre[i]] + [0.0])
+                for a, b in busy.get(e, []):
+                    if t + d <= a:
+                        break
+                    t = max(t, b)
+                if best is None or t + d < best[0] + best[1]:
+                    best = (t, d, e)
+            start[i], d, eng[i] = best
+            if d:
+                busy[eng[i]] = sorted(busy.get(eng[i], []) + [(start[i], start[i] + d)])
+        return start, eng
+
+    rest = [0.0] * n
     for i in range(n - 1, -1, -1):
-        rest[i] = cost(ops[i]["done"], ops[i]["q"][0]) + max([rest[j] + WAKE for j in after[i]] or [0.0])
-    busy, start, end, eng = {}, {}, {}, {}
-    for i in sorted(range(n), key=lambda k: (-rest[k], k)):
-        o, best = ops[i], None
-        ready = max([end[j] + (0 if o["kind"] == "acc" and ops[j]["q"] == "t" or o["kind"] == "arrival" else WAKE) for j in before[i]]
-                    + [start[j] + 1 for j in o.get("after", [])] + [0.0])
-        for e in o["q"]:
-            t, d = ready, cost(o["hold"], e)
-            for a, b in busy.get(e, []):
-                if t + d <= a:
-                    break
-                t = max(t, b)
-            if best is None or t + d < best[0] + best[1]:
-                best = (t, d, e)
-        t, d, e = best
-        start[i], end[i], eng[i] = t, t + cost(o["done"], e), e
-        if d:
-            busy[e] = sorted(busy.get(e, []) + [(t, t + d)])
+        rest[i] = cost(ops[i]["done"], ops[i]["q"][0]) + max([rest[j] + WAKE for j, _ in post[i]] + [0.0])
+    key, best = [max(rest) - x for x in rest], None
+    for _ in range(PASSES):
+        for i in range(n - 1, -1, -1):
+            key[i] = min([key[i], ops[i].get("early", key[i])] + [key[j] - 1e-3 for j, _ in post[i]])
+        start, eng = lay(sorted(range(n), key=lambda k: (key[k], k)), False)
+        end = [start[i] + cost(ops[i]["done"], eng[i]) for i in range(n)]
+        if best is None or max(end) < best[0]:
+            best = (max(end), start, eng)
+        for i in range(n - 1, -1, -1):
+            key[i] = max([-end[i]] + [key[j] + 1e-3 for j, _ in post[i]])
+        back, beng = lay(sorted(range(n), key=lambda k: (key[k], -k)), True)
+        last = [back[i] + cost(ops[i]["hold"], beng[i]) for i in range(n)]
+        key = [max(last) - x for x in last]
+    _, start, eng = best
     return [(i, eng[i]) for i in sorted(range(n), key=lambda k: (start[k], k))]
 
 

@@ -4,7 +4,7 @@ F32, BF, I32, U16, MXC, U8 = "float32", "bfloat16", "int32", "uint16", "float8_e
 C, J = 320, 128
 SCRATCH = {"tb": ("dram", [6, 8 * C], I32), "raw": ("sbuf", [128, 8, C], I32)}
 for _n, _w, _t in (
-        ("xi", 1280, BF), ("ui", 512, BF), ("vi", 512, BF), ("wcs", 512, MXC), ("wps", 512, U8), ("wdc", 512, MXC), ("wdp", 512, U8),
+        ("xi", 1280, BF), ("ui", 512, BF), ("vi", 512, BF), ("wcs", 512, MXC), ("wps", 512, U8), ("wdc", 512, MXC), ("wh", 512, MXC), ("wdp", 512, U8),
         ("pi", 16, I32), ("pf", 48, F32), ("nat", 320, F32), ("dm", 128, F32), ("ci", 128, I32), ("cj", 128, I32), ("cf", 96, F32), ("kb", 32, F32),
         ("tril", 128, BF), ("idb", 128, BF), ("mod", 128, BF), ("m8", 8, BF), ("stp", 576, BF), ("ls_", 24, U16),
         ("ze", 516, BF), ("za", 516, BF), ("zb", 516, BF),
@@ -12,22 +12,26 @@ for _n, _w, _t in (
         ("qu", 128, MXC), ("su", 128, U8), ("qv", 128, MXC), ("sv", 128, U8), ("fs", 320, F32),
         ("fw", 2688, F32), ("ox", 448, U16), ("ot", 464, U16), ("oxf", 656, F32), ("wf", 1440, F32), ("lw", 16, U16),
         ("pw", 224, F32), ("lrow", 128, F32), ("ne", 576, BF), ("so", 576, BF), ("fl", 16, U16),
-        ("sg", 32, F32), ("xx", 32, F32), ("yy", 36, F32), ("qd", 16, I32), ("ba", 544, BF), ("bb", 512, BF), ("b2", 512, BF),
-        ("qk", 136, MXC), ("sk", 136, U8), ("qw", 128, MXC), ("sw", 128, U8), ("ql", 128, MXC), ("sl", 128, U8),
+        ("sg", 96, F32), ("pp", 96, F32), ("yy", 100, F32), ("lu", 8, U16), ("qu0", 128, MXC), ("su0", 128, U8), ("qd", 16, I32), ("ba", 544, BF), ("bb", 544, BF), ("b2", 512, BF),
+        ("z0", 64, F32), ("m0", 8, I32), ("l1", 16, U16), ("qk", 136, MXC), ("sk", 136, U8), ("qw", 136, MXC), ("sw", 136, U8), ("ql", 128, MXC), ("sl", 128, U8),
         ("kt", 128, F32), ("eq", 128, F32), ("kl", 8, U16), ("ofs", 8, U16), ("va", 128, F32), ("nv", 128, F32),
-        ("fh", 1280, BF), ("dh", 256, BF), ("fg", 256, BF), ("nt", 512, BF), ("qn", 128, MXC), ("sn", 128, U8), ("dn", 512, BF), ("mt", 512, BF), ("ht", 512, BF),
-        ("xt", 1792, BF), ("qx", 320, MXC), ("sx", 320, U8), ("xl", 32, U16), ("yo", 320, F32),
+        ("fh", 3584, BF), ("dh", 256, BF), ("fg", 256, BF), ("nt", 512, BF), ("qn", 128, MXC), ("sn", 128, U8), ("dn", 512, BF), ("mt", 512, BF), ("ht", 512, BF),
+        ("xt", 1792, BF), ("qx", 320, MXC), ("sx", 320, U8), ("xl", 32, U16), ("xw", 256, F32), ("yo", 320, F32),
         ("qm0", 128, MXC), ("sm0", 128, U8), ("qm1", 128, MXC), ("sm1", 128, U8), ("qm2", 128, MXC), ("sm2", 128, U8),
         ("qh0", 128, MXC), ("sh0", 128, U8), ("qh1", 128, MXC), ("sh1", 128, U8), ("qh2", 128, MXC), ("sh2", 128, U8),
         ("mc1", 128, MXC), ("mp_1", 128, U8), ("mc2", 128, MXC), ("mp_2", 128, U8), ("hc1", 128, MXC), ("hp1", 128, U8), ("hc2", 128, MXC), ("hp2", 128, U8)):
     SCRATCH[_n] = ("sbuf", [128, _w], _t)
 for _n in range(8):
     SCRATCH["p%d" % _n] = ("psum", [128, 512], F32)
-SMALL = {n: 16 * k for k, n in enumerate(("sc", "sd", "dg", "rq", "lo", "dk", "of", "jc", "nl", "jw", "xm", "xj", "xe", "wn", "wn_"))}
-SEMAPHORES = ["v", "s", "t", "p", "ls", "aw", "ac", "am1", "am2", "ah1", "ah2"] + ["d%d" % _n for _n in range(16)]
+SMALL = {n: 16 * k for k, n in enumerate(("sc", "sd", "dg", "rq", "lo", "jc", "nl", "lf", "kw", "of"))}
+SEMAPHORES = ["v", "s", "t", "p", "ls", "aw", "ac", "am1", "am2", "ah1", "ah2"] + ["d%d" % _n for _n in range(20)]
 STEP = [1, 2, 3]
-HOME = 2
+HOME = 0
+FAR = 2048.0
+PARTS = [(0, 256)]
+ORDER = []
 PASSES = 3
+PIECE = (1, 1, 4, 2)
 CYC, WAKE = 1.0, 150.0
 
 
@@ -119,7 +123,7 @@ def program(g, core, T, topo):
         op("v", lambda e: V.quantize_mx(q[0], s[0], t[0]), [q, s], [t], (15 + 0.27 * t[2]) * CYC)
 
     def mm(out, l, ls, m, ms, start=True, stop=True):
-        op("t", lambda e: g.tensor.matmul_mx(out[0], l[0], ls[0], m[0], ms[0], start, stop), [out], [l, ls, m, ms], 0.6 * (m[2] + 16), "op" if start else "acc")
+        op("t", lambda e: g.tensor.matmul_mx(out[0], l[0], ls[0], m[0], ms[0], start, stop), [out], [l, ls, m, ms], 0.8 * (m[2] + 16), "op" if start else "acc")
 
     def iota(out, pattern, base, cm):
         flt = SCRATCH[out[1][0][0]][2] != I32
@@ -132,9 +136,10 @@ def program(g, core, T, topo):
     def hbm(a, name="hbm"):
         return (a, [(name, 0 if name == "hbm" else 1)], 0, False, False)
 
-    def send(pairs, dst, sem, done, behind=()):
+    def send(pairs, dst, sem, done, behind=(), spare=0):
         rid, pid, _ = topo.addr(dst)
-        mask, n = topo.mask(core, dst), len(topo.engines(core, dst))
+        mask = topo.mask(core, dst) & ~spare
+        n = bin(mask).count("1")
         for out, in_ in pairs:
             op("p", lambda e, out=out, in_=in_: g.remote_dma(out[0], in_[0], T.sem[sem], T.sem.ls, pid, rid, mask), [(0, [("sent" + sem, 1)])], [in_] + list(behind), 250 if any(o["kind"] == "send" for o in ops) else 1700, "send", sem=sem, n=n, done=done)
 
@@ -142,18 +147,24 @@ def program(g, core, T, topo):
         op("-", None, outs, [(0, [("sent" + sem, 1)])], 0, "arrival", sem=sem, n=len(outs) * len(topo.engines(src, core)))
 
     pf = lambda k: col("pf", k)
+    at = lambda m: J + C * (7 - m)
     LW = col("lw", 0, 8)
-    L0, LWP, LC, LL, LE, LA, LB, LF = [col("ls_", a, n) for a, n in ((0, 4), (4, 1), (6, 2), (8, 2), (10, 2), (12, 2), (14, 2), (16, 1))]
+    L0, LWP, LC, LL, LE, LA, LB, LF = [col("ls_", a, n) for a, n in ((0, 4), (4, 2), (6, 2), (8, 2), (10, 2), (12, 2), (14, 2), (16, 2))]
 
     def rawv(a, b, c0=0, c1=C):
         return (T.raw[:, a:b, c0:c1], [("raw", sum(bits(C * m + c0, C * m + c1) for m in range(a, b)))], (b - a) * (c1 - c0), False, False)
 
     fill(rawv(7, 8), 0)
     fill(rawv(0, 1), 0)
-    for m in range(1, 7):
+    fill(rawv(4, 6), 0)
+    ops[-1]["early"] = 0.0
+    for m in (1, 2, 3, 6):
         op("s", lambda e, m=m: S.activation(rawv(m, m + 1)[0], rawv(7, 8)[0], Act.Copy), [rawv(m, m + 1)], [rawv(7, 8)], C * CYC)
     first = [dma("ys"[k % 2], "d0", hbm(T.tb[k:k + 1, :], "tb"), hbm(T.mp[:] if k % 5 == 0 else T.ar[:, 20 * k - 20:20 * k]), 1500) for k in range(6)]
-    dma("s", "d4", R("xi"), hbm(T.x[:]), 3000, first)
+    first = [dma("y", "d12", (T.m0[16 * q:16 * q + 16, :],) + R("m0")[1:], hbm(T.mp[0:16, 0:8]), 1500, first) for q in range(8)]
+    own = PARTS[-1][1] if PARTS else 0
+    for n, (a, b) in enumerate(PARTS):
+        first = [dma("s", "d%d" % (16 + n), u8(R("wcs", a, b)), hbm(T.wc[:, 4 * a:4 * b]), 2000, first[:1])]
     iota(col("pi", 11), [[0, 1]], 0, 1)
     iota(R("dm"), [[-1, 128]], 0, 1)
     last = []
@@ -161,17 +172,22 @@ def program(g, core, T, topo):
         for q in range(8):
             p0 = 16 * q + (11 if q % 2 == 0 else 0)
             last = [dma("y", "d%d" % (3 + 3 * a), (T.raw[p0:p0 + 5, a:a + 4, :],) + rawv(a, a + 4)[1:], hbm(T.tb[1 - q % 2:6 - q % 2, C * a:C * a + 4 * C], "tb"), 2200 + 150 * a, last)]
-    last = [dma("y", "d1", R("wps"), hbm(T.ws[:]), 3200, last)]
-    last = [dma("y", "d2", u8(R("wcs")), hbm(T.wc[:]), 4500, last)]
+    last = [dma("y", "d4", R("xi"), hbm(T.x[:]), 3500, last)]
+    last = [dma("y", "d2", u8(R("wcs", own, 512)), hbm(T.wc[:, 4 * own:2048]), 4000, last)]
+    last = [dma("y", "d1", R("wps"), hbm(T.ws[:]), 4300, last)]
     heir, giver = T.cores[(r - STEP[HOME]) % N], T.cores[(r + STEP[HOME]) % N]
-    send([(R("wdp"), R("wps"))], heir, "aw", 3000)
-    ops[-1]["early"] = 6000.0
-    arrives("aw", giver, [R("wdp")])
+    for (a, b), mate in zip(PARTS, helpers(core, T, topo)[1]):
+        send([(u8(R("wh", a, b)), u8(R("wcs", a, b)))], mate, "aw", 7500)
+        ops[-1]["early"] = 2000.0
+        ops[-1]["w"] = [("sentac", 1)]
+    send([(u8(R("wdc", own, 512)), u8(R("wcs", own, 512))), (R("wdp"), R("wps"))], heir, "ac", 3000)
+    ops[-1]["early"] = ops[-2]["early"] = 3000.0
+    arrives("ac", giver, [R("wdp"), R("wdc", own, 512)] + [R("wdc", a, b) for a, b in PARTS])
 
-    for k, sh, an in ((0, 0, 15), (1, 4, 1), (2, 5, 1), (3, 6, 1), (4, 0, 1), (5, 1, 1), (6, 2, 1), (7, 0, 7), (8, 3, 1), (9, 4, 7), (10, 0, 31)):
+    for k, sh, an in ((0, 0, 15), (1, 4, 1), (2, 5, 1), (3, 6, 1), (4, 0, 1), (5, 1, 1), (6, 2, 1), (7, 0, 7), (8, 1, 7), (9, 4, 7), (10, 0, 31)):
         ts(col("pi", k), col("pi", 11), sh, Op.logical_shift_right, an, Op.bitwise_and)
     cp(col("pf", 0, 12), col("pi", 0, 12))
-    i_, h_, y_, b_, x0, x1, x2, g8, x3, g_, p31, p_ = [pf(k) for k in range(12)]
+    i_, h_, y_, b_, x0, x1, x2, g8, i2, g_, p31, p_ = [pf(k) for k in range(12)]
     iota(R("nat"), [[1, 320]], 0, 0)
     iota(col("cf", 0, 32), [[0, 4], [1, 8]], 0, 0)
     ts(R("ci"), R("dm"), 128.0, Op.add)
@@ -181,15 +197,18 @@ def program(g, core, T, topo):
     ts(R("ze", 3, 515, 4), R("dm"), 0.0, Op.is_equal, 0.5, Op.mult)
     for t in range(4):
         quant(blk("qe", t), blk("se", t), col("ze", 3 - t, 512))
-    iota(R("oxf"), [[0, 656]], 0, 0)
-    iota(col("fw", 8 * C, J), [[0, J]], 0, 0)
+    for s in range(9):
+        times(col("oxf", 80 * s, 16), col("dm", 0, 16), 0.0)
+    for s in range(1, 8, 2):
+        times(col("wf", 160 * s + 288, 32), col("dm", 0, 32), 0.0)
+    times(col("fw", 0, J), R("dm"), 0.0)
     fma(pf(12), x0, -65.0, 64.0)
     fma(pf(13), x1, -95.0, pf(12))
     fma(pf(14), pf(13), h_, x0)
     fma(pf(15), x2, 32.0, 175.0)
     fma(pf(16), x1, 96.0, pf(15))
     fma(pf(17), g_, 160.0, pf(16))
-    ts(LWP, pf(14), pf(17), Op.add)
+    ts(LWP, R("cf", 0, 16, 8), pf(14), Op.add, pf(17), Op.add)
     ts(pf(18), y_, h_, Op.not_equal)
     fma(pf(19), y_, 32.0, 64.0)
     fma(pf(20), b_, 32.0, 15.0)
@@ -200,36 +219,54 @@ def program(g, core, T, topo):
     fma(pf(25), y_, 6.0, pf(20))
     fma(pf(26), pf(22), -1.0, pf(23))
     fma(pf(27), pf(24), -1.0, pf(25))
-    fma(pf(28), g8, 160.0, pf(22))
-    fma(pf(29), g8, 160.0, pf(23))
-    fma(pf(30), g8, 160.0, pf(24))
-    fma(pf(31), pf(26), x0, pf(28))
-    fma(pf(32), pf(26), x0, 0.0)
-    fma(pf(33), pf(27), x0, pf(30))
-    fma(pf(34), x3, 1.0, pf(33))
+    fma(pf(28), i2, 160.0, pf(22))
+    fma(pf(29), i2, 160.0, pf(23))
+    fma(pf(30), i2, 160.0, pf(24))
+    fma(pf(31), pf(26), x1, pf(28))
+    fma(pf(32), pf(26), x1, 0.0)
+    fma(pf(33), pf(27), x1, pf(30))
+    fma(pf(34), x0, 1.0, pf(33))
     fma(pf(35), pf(32), -1.0, pf(29))
-    ts(LL, col("cf", 0, 16)[:1] and R("cf", 0, 16, 8), pf(31), Op.add, 160.0, Op.add)
+    ts(LL, R("cf", 0, 16, 8), pf(31), Op.add, 160.0, Op.add)
     ts(LE, R("cf", 0, 16, 8), pf(35), Op.add)
     ts(LC, R("nat", 156, 160, 2), pf(34), Op.add)
-    fma(pf(36), g8, 2.0, 16.0)
-    ts(LA, col("nat", 0, 2), -16.0, Op.mult, pf(36), Op.add)
-    fma(pf(37), x3, -16.0, pf(36))
-    ts(LB, R("cf", 1, 17, 8), pf(37), Op.add)
+    fill(R("lu"), 0)
+    times(col("lu", 0), i2, 16.0, "v")
+    fma(col("lu", 1), g8, 16.0, 1.0, "v")
     fma(pf(38), g8, 8.0, 8.0)
     fma(pf(39), g8, 1.0, 2.0)
-    ts(LF, pf(38), pf(39), Op.mult, -1.0, Op.add)
+    ts(pf(42), pf(38), pf(39), Op.mult, -1.0, Op.add)
+    ts(LF, R("cf", 0, 16, 8), pf(42), Op.add)
+    fma(pf(43), x1, -160.0, 64.0)
+    fma(pf(44), pf(43), h_, x0)
+    ts(col("ls_", 18), pf(44), pf(16), Op.add)
+    fma(pf(45), x1, 8.0, 1.0)
+    fma(pf(46), h_, 4.0, pf(45))
+    ts(col("ls_", 20), x0, 2.0, Op.mult, pf(46), Op.add)
+    fma(pf(47), pf(46), 0.5, x0)
+    ts(col("ls_", 22), pf(47), -0.5, Op.add)
+    fill(col("z0", 0, 16), 0.0)
     ts(pf(40), p31, 15.0, Op.is_ge)
     ts(pf(41), p31, 16.0, Op.is_le, pf(40), Op.mult)
-    fma(R("kb"), col("cf", 0, 32), -1024.0 * C, 1024.0 * (8 * C + J))
-    fma(col("yy", 32), p_, -1024.0, 1024.0 * J)
-    fma(col("cf", 32, 16), col("nat", 0, 16), 16.0, i_)
-    times(sm("jw"), col("cf", 32, 16), 1.0 / 256)
-    fma(sm("jc", 0, 8), col("cf", 32, 8), 1.0, -1.0 * J)
-    fma(sm("xj", 1, 16, 2), col("cf", 32, 8), 4.0, 4.0 * C)
-    fill(R("fs", SMALL["wn"], SMALL["wn"] + 32), 0.0)
-    fill(R("stp"), 1.0 / 256)
-    for k, t in enumerate((3, 2, 4, 3, None, 4, 1, 0, 2, 1)):
-        fill(sm("sc", k, k + 1), 0.0 if t is None else 32.0 ** -t)
+    iota(col("cf", 32, 32), [[0, 2], [1, 8], [0, 2]], 0, 0)
+    fma(R("kb"), col("cf", 32, 32), -1024.0 * C, 1024.0 * at(0))
+    times(R("pp"), col("dm", 0, 96), 0.0)
+    times(R("sg", 0, 96, 3), col("dm", 0, 32), 0.0)
+    times(col("yy", 98), p_, 1024.0)
+    xw = lambda k: blk("xw", k, 32)
+    fma(xw(0), col("cf", 0, 32), 16.0, i_)
+    ts(sm("jc", 0, 8), col("xw", 0, 8), 1.0 * at(0), Op.add)
+    iota(col("cf", 64, 32), [[1, 4], [0, 8]], 0, 0)
+    fma(xw(1), xw(0), -FAR, 1.0 * J)
+    times(xw(2), xw(0), 4.0)
+    tt(xw(2), xw(2), col("cf", 64, 32), Op.add)
+    fma(xw(3), xw(0), -FAR, 4.0 * J)
+    tt(xw(3), xw(3), col("cf", 64, 32), Op.add)
+    fill(R("stp"), FAR)
+    for a, b, t in ((0, 3, 3), (1, 8, 2), (2, 5, 4), (6, 9, 1)):
+        fill(sm("sc", a, b + 1, b - a), 32.0 ** -t)
+    fill(sm("sc", 4, 5), 0.0)
+    fill(sm("sc", 7, 8), 1.0)
     fill(sm("sd", 0, 10), 0.0)
     ts(sm("sd", 1, 10, 2), sm("sd", 0, 10, 2), -32.0, Op.add)
     ts(R("idb"), R("dm"), 0.0, Op.is_equal)
@@ -237,90 +274,97 @@ def program(g, core, T, topo):
     ts(R("cj"), R("ci"), 15, Op.bitwise_and)
     ts(R("mod"), R("cj"), 0.0, Op.is_equal)
     ts(R("m8"), col("nat", 0, 8), g_, Op.is_equal)
-    for n in ("za", "zb", "ba", "bb", "b2"):
+    for n in ("ba", "bb", "b2"):
         iota(R(n), [[0, R(n)[2]]], 0, 0)
+    fill(R("za"), 0.0)
+    times(R("zb"), R("za"), 1.0, "s")
     for t in range(3):
         fma(R("za", 3, 515, 4), R("mod"), 0.0, 32.0 ** t)
         quant(blk("qa", t), blk("sa", t), col("za", 3 - t, 512))
         times(R("zb", 3, 515, 4), R("mod"), 32.0 ** t)
         quant(blk("qb", t), blk("sb", t), col("zb", 3 - t, 512))
+        ops[-1]["early"] = ops[-3]["early"] = 4500.0
 
     for a in (0, 4):
         for i in range(16):
-            o, v = R("fw", C * a + i, C * a + 4 * C, 16), rawv(a, a + 4, 20 * i, 20 * i + 20)
+            o, v = R("fw", at(a + 3) + i, at(a) + C, 16), rawv(a, a + 4, 20 * i, 20 * i + 20)
+            v = (T.raw[:, a + 3:a - 1 if a else None:-1, 20 * i:20 * i + 20],) + v[1:]
             either(o, v, lambda o=o, v=v: V.tensor_copy(o[0], v[0]), lambda o=o, v=v: S.activation(o[0], v[0], Act.Copy))
 
-    def chase():
+    def chase(known=False):
         for s in range(8):
-            win = blk("fw", s, C)
-            lst = [col("ls_", 2 * b, 2) if s == 0 else col("ot", 66 * s - 50 + 32 * b, 2) for b in range(2)]
-            if s < 7:
+            win = col("fw", at(s), C)
+            lst = [col("ls_", 2 * b, 2) if s == 0 else col("l1", 2 * b, 2) if s == 1 and known else col("ot", 66 * s - 50 + 32 * b, 2) for b in range(2)]
+            if s < 7 and (s or not known):
                 for b in range(2):
                     times(col("ox", 64 * s + 32 * b, 32), by(win, lst[b]), 1.0, "vs"[b])
                 tr(col("ot", 66 * s + 1, 64), blk("ox", s, 64))
             for b in range(2):
                 times(col("oxf", 16 + 80 * s + 32 * b, 32), by(win, lst[b]), 1.0, "vs" if s == 7 else "s")
             tr(col("wf", 160 * s + 160, 64), col("oxf", 16 + 80 * s, 64))
-            tr(col("wf", 160 * s + 224, 96), col("oxf", 80 * s, 96))
-        cp(R("lw"), by(R("wf"), LWP))
+            tr(col("wf", 160 * s + 224, 96 - 32 * (s % 2)), col("oxf", 80 * s, 96 - 32 * (s % 2)))
+        cp(R("lw"), by(R("wf"), col("ls_", 4)))
 
     def asks():
-        cc, d, ke, kd, v, ne, pp = [blk("pw", k, 32) for k in range(7)]
+        cc, d, ke, kd, v, ne = [blk("pw", k, 32) for k in range(6)]
+        times(R("z0", 17, 48, 2), by(R("wf"), col("ls_", 18)), 1.0)
         times(cc, by(R("wf"), LC), 1.0)
         tt(d, by(R("wf"), LL), cc, Op.subtract)
-        times(ke, by(R("wf"), LE), -1024.0)
-        tt(kd, d, R("kb"), Op.add)
+        times(ke, by(R("wf"), LE), 1024.0)
+        tt(kd, R("kb"), d, Op.subtract)
         ts(ne, d, 0.0, Op.not_equal)
         tt(v, ke, kd, Op.add)
-        tt(pp, v, ne, Op.mult)
-        return pp
+        tt(R("pp", 0, 96, 3), v, ne, Op.mult)
 
     def unpack(bank, w, q, s, planes=range(4)):
         for t in planes:
             mm(ps(bank + t, 0, w), blk("qe", t), blk("se", t), q, s)
 
-    def state():
+    def fh(k, t, w=C):
+        return col("fh", (C + J) * (4 * (k % 2) + t + 1) - w, w)
+
+    def state(k, tile):
+        quant(R("qx"), R("sx"), tile)
         unpack(0, C, R("qx"), R("sx"))
         for t in range(4):
-            times(blk("fh", t, C), ps(t, 0, C), 1.0)
-        for t in range(4):
-            times(R("xt", t, 4 * C, 4), blk("fh", t, C), 2.0)
+            times(fh(k, t), ps(t, 0, C), 1.0)
 
-    def whole(last=False):
-        if last:
-            cp(by(R("xt"), R("xl")), R("nt"))
-        for t in range(0 if last else 4):
-            cp(by(R("xt"), blk("xl", t, 8)), R("nt", t, 512, 4))
-        quant(R("qx"), R("sx"), col("xt", 0, 4 * C))
-
-    quant(R("qx"), R("sx"), R("xi"))
-    state()
-    chase()
-    for m in range(8):
-        dma("y", "d5", col("ui", 8 * m, 8), hbm(T.u[:, 64 * m:64 * m + 8]), 5500, last)
-    dma("y", "d5", R("ui", 64, 512), hbm(T.u[:, 0:448]), 5500, last)
-    quant(R("qu"), R("su"), R("ui"))
+    state(0, R("xi"))
+    cp(R("l1"), by(R("m0"), col("ls_", 22)))
+    chase(True)
+    dma("y", "d5", R("ui"), hbm(T.u[:]), 5500, last)
+    quant(R("qu0"), R("su0"), R("ui"))
+    word = lambda v: (v[0].bitcast(dt.uint32),) + v[1:]
+    cp(word(R("qu")), by(word(R("qu0")), R("lu")))
+    op("s", lambda e: S.activation(T.su[:], T.su0[:].indirect(T.lu[:]), Act.Copy), [R("su")], [R("su0"), R("lu")], 270.0)
     for k in range(3):
         donor, client = T.cores[(r + STEP[k]) % N], T.cores[(r - STEP[k]) % N]
         qm, sp, qh, sh = [R("%s%d" % (n, k)) for n in ("qm", "sm", "qh", "sh")]
-        pp = asks()
+        asks()
         if k:
             quant(R("qn"), R("sn"), R("nt"))
             unpack(0, J, R("qn"), R("sn"))
             for t in range(4):
                 times(blk("dn", t), ps(t, 0, J), 1.0)
         for t in range(4):
-            times(R("mt", t, 512, 4), by(blk("dn", t), col("fl", 0, 8)) if k else by(blk("fh", t, C), LW), 2.0)
+            times(R("mt", t, 512, 4), by(blk("dn", t), col("fl", 0, 8)) if k else by(fh(0, t), LW), 2.0)
         quant(qm, sp, R("mt"))
         mc, mp, wc, wp, hc, hp = qm, sp, "wdc", "wdp", qh, sh
         x = 1 + k - (k > HOME)
         if k != HOME:
             mc, mp, wc, wp, hc, hp = R("mc%d" % x), R("mp_%d" % x), "wcs", "wps", R("hc%d" % x), R("hp%d" % x)
-            send([(u8(mc), u8(qm)), (mp, sp)], donor, "am%d" % x, 2800)
+            send([(u8(mc), u8(qm)), (mp, sp)], donor, "am%d" % x, 2100)
             arrives("am%d" % x, client, [mc, mp])
-        if k:
-            whole()
-            state()
+        if k and k != HOME:
+            state(k, col("xt", 4 * J, 4 * C))
+        for t in range(4 if k else 0):
+            n = 8 if k != HOME else PIECE[t]
+            for c in range(0, 8, n):
+                cp(by(fh(k, t, C + J), col("xl", c, n) if n > 1 else col("xl", 8 + 2 * c)), col("dn", J * t + 16 * c, 16 * n))
+        for t in range(4):
+            times(R("xt", 4 * J + t, 4 * (J + C), 4), fh(k, t), 2.0)
+        if k + 1 == HOME:
+            state(k + 1, col("xt", 4 * J, 4 * C))
         for b in range(4):
             mm(ps(4 + b, 0, J), blk(wc, b), blk(wp, b), mc, mp)
         for b in range(4):
@@ -328,22 +372,19 @@ def program(g, core, T, topo):
             either(o, i, lambda o=o, i=i: V.tensor_scalar(o[0], i[0], 0.0, 0.03125, Op.max, Op.mult), lambda o=o, i=i: S.activation(o[0], i[0], Act.Relu, scale=0.03125))
         quant(qh, sh, R("ht"))
         if k != HOME:
-            send([(u8(hc), u8(qh)), (hp, sh)], client, "ah%d" % x, 2800)
+            send([(u8(hc), u8(qh)), (hp, sh)], client, "ah%d" % x, 2100)
             arrives("ah%d" % x, donor, [hc, hp])
         if k == 0:
-            send([(u8(R("wdc")), u8(R("wcs")))], heir, "ac", 6000, [hc])
-            arrives("ac", giver, [R("wdc")])
-            dma("y", "d6", R("vi"), hbm(T.v[:]), 2500, (), [R("wdc")])
+            dma("y", "d6", R("vi"), hbm(T.v[:]), 2500, (), [hc])
             quant(R("qv"), R("sv"), R("vi"))
         mm(ps(4, 0, J), hc, hp, R("qu"), R("su"))
         unpack(0, J, hc, hp)
         for t in range(2):
             times(blk("dh", t), ps(t, 0, J), 1.0, "s")
-        ts(col("sg", 0, 16), ps(4, 0, 16), 0.0, Op.is_gt)
-        ts(col("sg", 16, 16), ps(4, 0, 16), 0.0, Op.is_le)
-        tt(R("xx"), by(R("sg"), LA), pp, Op.mult)
-        tt(col("yy", 0, 32), by(R("sg"), LB), R("xx"), Op.mult)
-        red(sm("rq", 0, 1), col("yy", 0, 33), Op.max, negate=True)
+        for a, b, st, c, o in ((1, 48, 3, 0, Op.is_le), (49, 96, 3, 0, Op.is_gt), (2, 96, 6, 16, Op.is_le), (5, 96, 6, 16, Op.is_gt)):
+            ts(R("sg", a, b, st), ps(4, c, c + 16), 0.0, o)
+        scan(col("yy", 0, 96), R("sg"), R("pp"), Op.mult, Op.add)
+        red(sm("rq", 0, 1), R("yy", 2, 99, 3), Op.max)
         ts(col("qd", 0, 10), sm("sc", 0, 10), sm("rq", 0, 1), Op.mult)
         scan(sm("dg", 0, 10), sm("sd", 0, 10), col("qd", 0, 10), Op.mult, Op.add)
         dg = lambda c: sm("dg", c, c + 1)
@@ -357,48 +398,60 @@ def program(g, core, T, topo):
             mm(ps(7, 0, J), blk("qb", t), blk("sb", t), col("qk", 8, J), col("sk", 8, J), t == 0, t == 2)
         for t in range(2):
             times(R("bb", t, 512, 4), R("idb"), dg(7 + 2 * t))
+            times(R("bb", 512 + t, 544, 4), R("m8"), dg(7 + 2 * t))
         quant(R("qw"), R("sw"), R("bb"))
         for t in range(2):
-            mm(ps(6, 0, J), blk("qa", t), blk("sa", t), R("qw"), R("sw"), t == 0, t == 1)
+            mm(ps(6, 0, J), blk("qa", t), blk("sa", t), col("qw", 0, J), col("sw", 0, J), t == 0, t == 1)
+        for t in range(2):
+            mm(ps(0, 0, J), blk("qb", t), blk("sb", t), col("qw", 8, J), col("sw", 8, J), t == 0, t == 1)
         times(R("va"), ps(6, 0, J), pf(41), "s")
-        ts(R("kl"), ps(7, 120, 128), 8.0 * C + J, Op.add)
-        ts(sm("dk", 1, 16, 2), ps(7, 120, 128), 8.0 * C + J, Op.add)
-        tt(sm("dk", 0, 16, 2), sm("jc", 0, 8), ps(7, 120, 128), Op.subtract)
+        times(R("z0", 16, 32, 2), ps(0, 120, 128), 1.0)
+        cp(R("kl"), ps(7, 120, 128))
+        times(sm("kw", 0, 8), ps(7, 120, 128), 1.0)
         tt(R("nv"), by(R("fw"), R("kl")), R("va"), Op.add)
+        tt(R("z0", 1, 16, 2), sm("kw", 0, 8), sm("jc", 0, 8), Op.is_equal)
+        scan(col("z0", 48, 16), col("z0", 0, 16), col("z0", 16, 16), Op.mult, Op.add)
+        cp(R("l1"), by(col("z0", 48, 16), col("ls_", 20)))
         times(R("kt"), R("tril"), dg(8))
         tt(R("eq"), ps(5, 0, J), R("kt"), Op.is_equal)
         red(sm("lo", 0, 1), R("eq"), Op.max)
-        times(R("b2", 4, 64, 8), R("m8"), sm("lo", 0, 1), "v")
+        ts(R("b2", 482, 512, 4), R("m8"), sm("lo", 0, 1), Op.mult, -4.0, Op.mult)
         quant(R("ql"), R("sl"), R("b2"))
-        mm(ps(4, 0, J), blk("qb", 0), blk("sb", 0), R("ql"), R("sl"))
-        scan(sm("of"), ps(4, 0, 16), sm("dk"), Op.mult, Op.add)
-        cp(R("ofs"), sm("of", 1, 16, 2))
+        mm(ps(4, 0, J), blk("qb", 2), blk("sb", 2), R("ql"), R("sl"))
+        tt(sm("of", 0, 8), ps(4, 120, 128), sm("kw", 0, 8), Op.add)
+        tt(R("ofs"), sm("of", 0, 8), col("xw", 0, 8), Op.max)
         cp(by(R("fw"), R("ofs")), R("nv"))
-        if k == 2:
-            dma("y", "d7", hbm(T.fo[:]), (T.fw[15:16, 0:8 * C],) + col("fw", 0, 8 * C)[1:], 1500)
-        chase()
+        for m in range(8 if k == 2 else 0):
+            dma("y", "d7", hbm(T.fo[m:m + 1, :]), (T.fw[15:16, at(m):at(m) + C],) + col("fw", at(m), C)[1:], 1500)
+        chase(True)
         for t in range(4):
             nt = blk("nt", t) if k == 2 else R("nt", t, 512, 4)
             if t < 2:
-                tt(nt, by(blk("fh", t, C), LW), blk("dh", t), Op.add)
+                tt(nt, by(fh(k, t), LW), blk("dh", t), Op.add)
             else:
-                times(blk("fg", t - 2), by(blk("fh", t, C), LW), 1.0, "s")
+                times(blk("fg", t - 2), by(fh(k, t), LW), 1.0, "s")
                 tt(nt, ps(t, 0, J), blk("fg", t - 2), Op.add)
-        times(sm("nl"), by(R("wf"), LWP), -1.0)
+        times(sm("nl"), by(R("wf"), col("ls_", 4)), -256 * FAR)
+        times(sm("lf"), by(R("wf"), col("ls_", 4)), 1.0)
         times((T.lrow[:, ::-1],) + R("lrow")[1:], by(R("nat"), LW), 1.0)
         for c in range(7, -1, -1):
-            o, i, b = col("ne", 8 * c * (c + 1), 16 * c + 16), R("lrow", 112 - 16 * c), sm("nl", c, c + 1)
-            either(o, i, lambda o=o, i=i, b=b: V.tensor_scalar(o[0], i[0], b[0], 0.0, Op.add, Op.not_equal), lambda o=o, i=i, b=b: S.activation(o[0], i[0], Act.Abs, bias=b[0]), [b])
+            o, i, a, b = col("ne", 8 * c * (c + 1), 16 * c + 16), R("lrow", 112 - 16 * c), sm("lf", c, c + 1), sm("nl", c, c + 1)
+            either(o, i, lambda o=o, i=i, a=a: V.tensor_scalar(o[0], i[0], a[0], 256 * FAR, Op.not_equal, Op.mult),
+                   lambda o=o, i=i, b=b: S.activation(o[0], i[0], Act.Abs, bias=b[0], scale=256 * FAR), [a, b])
         scan(R("so"), R("stp"), R("ne"), Op.add, Op.min)
         if k < 2:
-            ts(R("fl"), by(R("so"), LF), 256.0, Op.mult)
-        times(sm("xm", 0, 8), sm("nl", 0, 8), -4.0)
-        tt(sm("xj", 0, 16, 2), sm("xm", 0, 8), sm("xj", 1, 16, 2), Op.subtract)
-        tt(R("fs", SMALL["wn"] + 1, SMALL["wn"] + 32, 2), by(R("so"), LF), sm("jw"), Op.is_equal)
-        scan(sm("xe"), sm("wn"), sm("xj"), Op.mult, Op.add)
-        for t in range(4):
-            ts(blk("xl", t, 8), sm("xe", 1, 16, 2), float(t), Op.add)
-    whole(True)
+            ts(R("fl"), by(R("so"), col("ls_", 16)), 1 / FAR, Op.mult)
+        times(xw(4), by(R("wf"), LWP), 4.0 if k == 2 else 1.0)
+        tt(xw(5), xw(4), xw(3 if k == 2 else 1), Op.add)
+        tt(xw(6), by(R("so"), LF), xw(5), Op.add)
+        if k == 2:
+            tt(R("xl"), xw(6), xw(2), Op.max)
+        else:
+            tt(col("xl", 0, 8), col("xw", 192, 8), col("xw", 0, 8), Op.max)
+            if k + 1 == HOME:
+                tt(R("xl", 8, 24, 2), col("xw", 192, 8), col("xw", 0, 8), Op.max)
+    cp(by(R("xt"), R("xl")), R("nt"))
+    quant(R("qx"), R("sx"), col("xt", 4 * J, 4 * C))
     dma("y", "d8", hbm(T.oc[:]), u8(R("qx")), 1800)
     for a in range(2):
         mm(ps(4 + a, 0, 160), R("qv"), R("sv"), blk("qx", a, 160), blk("sx", a, 160))
@@ -411,6 +464,7 @@ def program(g, core, T, topo):
 
 def orders(ops):
     seen, out, group = {}, [], {}
+    alike = lambda a, b: a["kind"] == b["kind"] and (a["kind"] == "send" or (a["kind"] == "dma" and a["sem"] == b["sem"]))
     for i, o in enumerate(ops):
         if o["kind"] == "dma":
             group.setdefault(o["sem"], []).append(i)
@@ -420,11 +474,10 @@ def orders(ops):
             for name, m in keys:
                 for j, m2, w2 in seen.get(name, []):
                     if m & m2 and (writes or w2 or (name[0] == "#" and (len(o["q"]) > 1 or o["q"] != ops[j]["q"]))):
-                        if not (o["kind"] in ("dma", "send") and ops[j].get("sem") == o["sem"]):
+                        if not alike(o, ops[j]):
                             p.add(j)
         for name, m in o["w"]:
-            keep = o["kind"] in ("dma", "send")
-            seen[name] = [x for x in seen.get(name, []) if x[1] & ~m or (keep and ops[x[0]].get("sem") == o["sem"])] + [(i, m, True)]
+            seen[name] = [x for x in seen.get(name, []) if x[1] & ~m or alike(o, ops[x[0]])] + [(i, m, True)]
         for name, m in o["r"]:
             seen.setdefault(name, []).append((i, m, False))
         p.discard(i)
@@ -484,9 +537,26 @@ def plan(ops, before):
     return [(i, eng[i]) for i in sorted(range(n), key=lambda k: (start[k], k))]
 
 
+def helpers(core, T, topo):
+    heir = T.cores[(T.rank_of(core) - STEP[HOME]) % len(T.cores)]
+    free = [c for c in topo.cores_of(core) if T.rank_of(c) is None and topo.may_write(c, heir)]
+    return heir, sorted(free, key=lambda c: (topo.die(c) == topo.die(core), c))[:len(PARTS)]
+
+
+def hand_on(g, core, T, topo):
+    for home in T.cores:
+        heir, mates = helpers(home, T, topo)
+        if core in mates:
+            a, b = PARTS[mates.index(core)]
+            rid, pid, _ = topo.addr(heir)
+            g.wait_ge(T.sem.aw, len(topo.engines(home, core)))
+            g.remote_dma(T.wdc[:, a:b].bitcast(dt.uint8), T.wh[:, a:b].bitcast(dt.uint8), T.sem.ac, T.sem.ls, pid, rid, topo.mask(core, heir))
+            g.wait_ge(T.sem.ls, len(topo.engines(core, heir)))
+
+
 def rank_program(g, core, T, topo):
     if T.rank_of(core) is None:
-        return
+        return hand_on(g, core, T, topo)
     ops = program(g, core, T, topo)
     before = orders(ops)
     Q = {"v": g.vector, "s": g.scalar, "t": g.tensor, "p": g, "y": g.sync}
@@ -498,7 +568,9 @@ def rank_program(g, core, T, topo):
             tot[o["sem"]] = o["n"]
         elif o["kind"] == "send":
             tot["ls"] = tot.get("ls", 0) + o["n"]
-    for i, e in plan(ops, before):
+    if not ORDER:
+        ORDER.extend(plan(ops, before))
+    for i, e in ORDER:
         o = ops[i]
         if o["kind"] == "arrival":
             token[i] = (o["sem"], o["n"], {})

@@ -5,15 +5,15 @@ C, J = 320, 128
 SCRATCH = {"tb": ("dram", [6, 8 * C], I32), "raw": ("sbuf", [128, 8, C], I32)}
 for _n, _w, _t in (
         ("xi", 1280, BF), ("ui", 512, BF), ("vi", 512, BF), ("wcs", 512, MXC), ("wps", 512, U8), ("wdc", 512, MXC), ("wh", 512, MXC), ("wdp", 512, U8),
-        ("pi", 16, I32), ("pf", 48, F32), ("nat", 320, F32), ("dm", 128, F32), ("ci", 128, I32), ("cj", 128, I32), ("cf", 96, F32), ("kb", 32, F32),
+        ("pi", 16, I32), ("pf", 48, F32), ("nat", 320, F32), ("dm", 128, F32), ("ci", 128, BF), ("cf", 96, F32), ("kb", 32, F32),
         ("tril", 128, BF), ("idb", 128, BF), ("mod", 128, BF), ("m8", 8, BF), ("stp", 576, BF), ("ls_", 24, U16),
         ("ze", 516, BF), ("za", 516, BF), ("zb", 516, BF),
         ("qe", 512, MXC), ("se", 512, U8), ("qa", 384, MXC), ("sa", 384, U8), ("qb", 384, MXC), ("sb", 384, U8),
         ("qu", 128, MXC), ("su", 128, U8), ("qv", 128, MXC), ("sv", 128, U8), ("fs", 320, F32),
-        ("fw", 2688, F32), ("ox", 448, U16), ("ot", 464, U16), ("oxf", 656, F32), ("wf", 1440, F32), ("lw", 16, U16),
+        ("fw", 2688, F32), ("ox", 576, U16), ("o7", 80, F32), ("wu", 1281, U16), ("wf", 1409, F32), ("lw", 16, U16),
         ("pw", 224, F32), ("lrow", 128, F32), ("ne", 576, BF), ("so", 576, BF), ("fl", 16, U16),
-        ("sg", 96, F32), ("pp", 96, F32), ("yy", 100, F32), ("lu", 8, U16), ("qu0", 128, MXC), ("su0", 128, U8), ("qd", 16, I32), ("ba", 544, BF), ("bb", 544, BF), ("b2", 512, BF),
-        ("z0", 64, F32), ("m0", 8, I32), ("l1", 16, U16), ("qk", 136, MXC), ("sk", 136, U8), ("qw", 136, MXC), ("sw", 136, U8), ("ql", 128, MXC), ("sl", 128, U8),
+        ("sg", 96, F32), ("pp", 96, F32), ("yy", 100, F32), ("lu", 8, U16), ("qu0", 128, MXC), ("su0", 128, U8), ("qd", 16, I32), ("ba", 512, BF), ("bb", 576, BF), ("b2", 512, BF),
+        ("z0", 64, F32), ("m0", 8, I32), ("l1", 16, U16), ("qk", 128, MXC), ("sk", 128, U8), ("qw", 144, MXC), ("sw", 144, U8), ("ql", 128, MXC), ("sl", 128, U8),
         ("kt", 128, F32), ("eq", 128, F32), ("kl", 8, U16), ("ofs", 8, U16), ("va", 128, F32), ("nv", 128, F32),
         ("fh", 3584, BF), ("dh", 256, BF), ("fg", 256, BF), ("nt", 512, BF), ("qn", 128, MXC), ("sn", 128, U8), ("dn", 512, BF), ("mt", 512, BF), ("ht", 512, BF),
         ("xt", 1792, BF), ("qx", 320, MXC), ("sx", 320, U8), ("xl", 32, U16), ("xw", 256, F32), ("yo", 320, F32),
@@ -23,7 +23,7 @@ for _n, _w, _t in (
     SCRATCH[_n] = ("sbuf", [128, _w], _t)
 for _n in range(8):
     SCRATCH["p%d" % _n] = ("psum", [128, 512], F32)
-SMALL = {n: 16 * k for k, n in enumerate(("sc", "sd", "dg", "rq", "lo", "jc", "nl", "lf", "kw", "of"))}
+SMALL = {n: 16 * k for k, n in enumerate(("sc", "sd", "dg", "rq", "lo", "jc", "nl", "lf", "mf"))}
 SEMAPHORES = ["v", "s", "t", "p", "ls", "aw", "ac", "am1", "am2", "ah1", "ah2"] + ["d%d" % _n for _n in range(20)]
 STEP = [1, 2, 3]
 HOME = 0
@@ -155,10 +155,12 @@ def program(g, core, T, topo):
         return (T.raw[:, a:b, c0:c1], [("raw", sum(bits(C * m + c0, C * m + c1) for m in range(a, b)))], (b - a) * (c1 - c0), False, False)
 
     fill(rawv(7, 8), 0)
+    ops[-1]["early"] = -2.0
     fill(rawv(0, 1), 0)
-    fill(rawv(4, 6), 0)
+    ops[-1]["early"] = -1.0
+    iota(rawv(5, 7), [[0, 2 * C]], 0, 0)
     ops[-1]["early"] = 0.0
-    for m in (1, 2, 3, 6):
+    for m in (1, 2, 3, 4):
         op("s", lambda e, m=m: S.activation(rawv(m, m + 1)[0], rawv(7, 8)[0], Act.Copy), [rawv(m, m + 1)], [rawv(7, 8)], C * CYC)
     first = [dma("ys"[k % 2], "d0", hbm(T.tb[k:k + 1, :], "tb"), hbm(T.mp[:] if k % 5 == 0 else T.ar[:, 20 * k - 20:20 * k]), 1500) for k in range(6)]
     first = [dma("y", "d12", (T.m0[16 * q:16 * q + 16, :],) + R("m0")[1:], hbm(T.mp[0:16, 0:8]), 1500, first) for q in range(8)]
@@ -171,8 +173,8 @@ def program(g, core, T, topo):
     for a in (0, 4):
         for q in range(8):
             p0 = 16 * q + (11 if q % 2 == 0 else 0)
-            last = [dma("y", "d%d" % (3 + 3 * a), (T.raw[p0:p0 + 5, a:a + 4, :],) + rawv(a, a + 4)[1:], hbm(T.tb[1 - q % 2:6 - q % 2, C * a:C * a + 4 * C], "tb"), 2200 + 150 * a, last)]
-    last = [dma("y", "d4", R("xi"), hbm(T.x[:]), 3500, last)]
+            last = [dma("y", "d%d" % (3 + 3 * a), (T.raw[p0:p0 + 5, a:a + 4, :],) + rawv(a, a + 4)[1:], hbm(T.tb[1 - q % 2:6 - q % 2, C * a:C * a + 4 * C], "tb"), 1700 + 150 * a, last)]
+    last = [dma("y", "d4", R("xi"), hbm(T.x[:]), 2800, last)]
     last = [dma("y", "d2", u8(R("wcs", own, 512)), hbm(T.wc[:, 4 * own:2048]), 4000, last)]
     last = [dma("y", "d1", R("wps"), hbm(T.ws[:]), 4300, last)]
     heir, giver = T.cores[(r - STEP[HOME]) % N], T.cores[(r + STEP[HOME]) % N]
@@ -190,46 +192,37 @@ def program(g, core, T, topo):
     i_, h_, y_, b_, x0, x1, x2, g8, i2, g_, p31, p_ = [pf(k) for k in range(12)]
     iota(R("nat"), [[1, 320]], 0, 0)
     iota(col("cf", 0, 32), [[0, 4], [1, 8]], 0, 0)
-    ts(R("ci"), R("dm"), 128.0, Op.add)
-    fma(col("wf", 0, 160), col("nat", 0, 160), 0.0, p_)
+    fma(col("wf", 0, 161), col("nat", 0, 161), 0.0, p_)
     ts(L0, col("nat", 0, 4), 32.0, Op.mult, p31, Op.add)
     fill(R("ze"), 0.0)
     ts(R("ze", 3, 515, 4), R("dm"), 0.0, Op.is_equal, 0.5, Op.mult)
     for t in range(4):
         quant(blk("qe", t), blk("se", t), col("ze", 3 - t, 512))
-    for s in range(9):
-        times(col("oxf", 80 * s, 16), col("dm", 0, 16), 0.0)
-    for s in range(1, 8, 2):
-        times(col("wf", 160 * s + 288, 32), col("dm", 0, 32), 0.0)
-    times(col("fw", 0, J), R("dm"), 0.0)
+    fill(R("ox"), 0)
+    iota(col("o7", 0, 16), [[0, 16]], 0, 0)
+    iota(col("fw", 0, J), [[0, J]], 0, 0)
     fma(pf(12), x0, -65.0, 64.0)
     fma(pf(13), x1, -95.0, pf(12))
     fma(pf(14), pf(13), h_, x0)
-    fma(pf(15), x2, 32.0, 175.0)
+    fma(pf(15), x2, 32.0, 176.0)
     fma(pf(16), x1, 96.0, pf(15))
     fma(pf(17), g_, 160.0, pf(16))
     ts(LWP, R("cf", 0, 16, 8), pf(14), Op.add, pf(17), Op.add)
     ts(pf(18), y_, h_, Op.not_equal)
     fma(pf(19), y_, 32.0, 64.0)
-    fma(pf(20), b_, 32.0, 15.0)
-    fma(pf(21), pf(18), pf(19), pf(20))
-    fma(pf(22), h_, 1.0, pf(21))
-    fma(pf(23), y_, 1.0, pf(20))
-    fma(pf(24), h_, 6.0, pf(21))
-    fma(pf(25), y_, 6.0, pf(20))
-    fma(pf(26), pf(22), -1.0, pf(23))
-    fma(pf(27), pf(24), -1.0, pf(25))
-    fma(pf(28), i2, 160.0, pf(22))
-    fma(pf(29), i2, 160.0, pf(23))
-    fma(pf(30), i2, 160.0, pf(24))
-    fma(pf(31), pf(26), x1, pf(28))
-    fma(pf(32), pf(26), x1, 0.0)
-    fma(pf(33), pf(27), x1, pf(30))
-    fma(pf(34), x0, 1.0, pf(33))
-    fma(pf(35), pf(32), -1.0, pf(29))
-    ts(LL, R("cf", 0, 16, 8), pf(31), Op.add, 160.0, Op.add)
-    ts(LE, R("cf", 0, 16, 8), pf(35), Op.add)
-    ts(LC, R("nat", 156, 160, 2), pf(34), Op.add)
+    fma(pf(20), b_, 32.0, 16.0)
+    times(pf(21), pf(18), pf(19))
+    fma(pf(22), i2, 160.0, pf(20))
+    fma(pf(23), x1, -1.0, 1.0)
+    fma(pf(24), h_, -1.0, y_)
+    fma(pf(25), pf(24), x1, h_)
+    fma(pf(26), pf(24), pf(23), h_)
+    fma(pf(27), pf(21), pf(23), pf(22))
+    fma(pf(28), pf(21), x1, pf(22))
+    fma(pf(29), pf(25), 6.0, pf(27))
+    ts(LL, R("cf", 0, 16, 8), pf(27), Op.add, pf(25), Op.add)
+    ts(LE, R("cf", 0, 16, 8), pf(28), Op.add, pf(26), Op.add)
+    ts(LC, R("nat", 156, 160, 2), pf(29), Op.add, x0, Op.add)
     fill(R("lu"), 0)
     times(col("lu", 0), i2, 16.0, "v")
     fma(col("lu", 1), g8, 16.0, 1.0, "v")
@@ -240,22 +233,17 @@ def program(g, core, T, topo):
     fma(pf(43), x1, -160.0, 64.0)
     fma(pf(44), pf(43), h_, x0)
     ts(col("ls_", 18), pf(44), pf(16), Op.add)
-    fma(pf(45), x1, 8.0, 1.0)
-    fma(pf(46), h_, 4.0, pf(45))
-    ts(col("ls_", 20), x0, 2.0, Op.mult, pf(46), Op.add)
-    fma(pf(47), pf(46), 0.5, x0)
-    ts(col("ls_", 22), pf(47), -0.5, Op.add)
-    fill(col("z0", 0, 16), 0.0)
+    fma(pf(45), x1, 4.0, x0)
+    ts(col("ls_", 22), h_, 2.0, Op.mult, pf(45), Op.add)
     ts(pf(40), p31, 15.0, Op.is_ge)
     ts(pf(41), p31, 16.0, Op.is_le, pf(40), Op.mult)
     iota(col("cf", 32, 32), [[0, 2], [1, 8], [0, 2]], 0, 0)
     fma(R("kb"), col("cf", 32, 32), -1024.0 * C, 1024.0 * at(0))
-    times(R("pp"), col("dm", 0, 96), 0.0)
-    times(R("sg", 0, 96, 3), col("dm", 0, 32), 0.0)
+    iota(R("pp"), [[0, 96]], 0, 0)
+    iota(R("sg", 0, 96, 3), [[0, 32]], 0, 0)
     times(col("yy", 98), p_, 1024.0)
     xw = lambda k: blk("xw", k, 32)
     fma(xw(0), col("cf", 0, 32), 16.0, i_)
-    ts(sm("jc", 0, 8), col("xw", 0, 8), 1.0 * at(0), Op.add)
     iota(col("cf", 64, 32), [[1, 4], [0, 8]], 0, 0)
     fma(xw(1), xw(0), -FAR, 1.0 * J)
     times(xw(2), xw(0), 4.0)
@@ -269,11 +257,12 @@ def program(g, core, T, topo):
     fill(sm("sc", 7, 8), 1.0)
     fill(sm("sd", 0, 10), 0.0)
     ts(sm("sd", 1, 10, 2), sm("sd", 0, 10, 2), -32.0, Op.add)
-    ts(R("idb"), R("dm"), 0.0, Op.is_equal)
-    ts(R("tril"), R("dm"), 0.0, Op.is_gt)
-    ts(R("cj"), R("ci"), 15, Op.bitwise_and)
-    ts(R("mod"), R("cj"), 0.0, Op.is_equal)
+    for n, o, st in (("idb", Op.not_equal, -1), ("tril", Op.is_ge, 1)):
+        op("p", lambda e, n=n, o=o, st=st: g.affine_select(T[n][:], T.ze[:, 0:512:4], [[st, J]], o, 1.0, 0, -st), [R(n)], [R("ze", 0, 512, 4)], 430.0)
+    iota(R("ci"), [[0, 8], [1, 16]], 0, 0)
+    ts(R("mod"), R("ci"), i_, Op.is_equal)
     ts(R("m8"), col("nat", 0, 8), g_, Op.is_equal)
+    fma(sm("jc", 0, 8), R("m8"), -1024.0 * C - 512, 1024.0 * (at(0) + C))
     for n in ("ba", "bb", "b2"):
         iota(R(n), [[0, R(n)[2]]], 0, 0)
     fill(R("za"), 0.0)
@@ -283,7 +272,6 @@ def program(g, core, T, topo):
         quant(blk("qa", t), blk("sa", t), col("za", 3 - t, 512))
         times(R("zb", 3, 515, 4), R("mod"), 32.0 ** t)
         quant(blk("qb", t), blk("sb", t), col("zb", 3 - t, 512))
-        ops[-1]["early"] = ops[-3]["early"] = 4500.0
 
     for a in (0, 4):
         for i in range(16):
@@ -294,22 +282,21 @@ def program(g, core, T, topo):
     def chase(known=False):
         for s in range(8):
             win = col("fw", at(s), C)
-            lst = [col("ls_", 2 * b, 2) if s == 0 else col("l1", 2 * b, 2) if s == 1 and known else col("ot", 66 * s - 50 + 32 * b, 2) for b in range(2)]
-            if s < 7 and (s or not known):
-                for b in range(2):
-                    times(col("ox", 64 * s + 32 * b, 32), by(win, lst[b]), 1.0, "vs"[b])
-                tr(col("ot", 66 * s + 1, 64), blk("ox", s, 64))
+            lst = [col("ls_", 2 * b, 2) if s == 0 else col("l1", 2 * b, 2) if s == 1 and known else col("wu", 160 * s + 16 + 32 * b, 2) for b in range(2)]
+            rows, at0, turned = ("ox", 80 * s, "wu") if s < 7 else ("o7", 0, "wf")
             for b in range(2):
-                times(col("oxf", 16 + 80 * s + 32 * b, 32), by(win, lst[b]), 1.0, "vs" if s == 7 else "s")
-            tr(col("wf", 160 * s + 160, 64), col("oxf", 16 + 80 * s, 64))
-            tr(col("wf", 160 * s + 224, 96 - 32 * (s % 2)), col("oxf", 80 * s, 96 - 32 * (s % 2)))
+                times(col(rows, at0 + 16 + 32 * b, 32), by(win, lst[b]), 1.0)
+            tr(col(turned, 160 * s + 161, 64), col(rows, at0 + 16, 64))
+            tr(col(turned, 160 * s + 225, 96 if s < 7 else 64), col(rows, at0, 96 if s < 7 else 64))
+            if s < 7:
+                times(col("wf", 160 * s + 161, 160), col("wu", 160 * s + 161, 160), 1.0, "s")
         cp(R("lw"), by(R("wf"), col("ls_", 4)))
 
     def asks():
         cc, d, ke, kd, v, ne = [blk("pw", k, 32) for k in range(6)]
-        times(R("z0", 17, 48, 2), by(R("wf"), col("ls_", 18)), 1.0)
+        times(col("z0", 0, 16), by(R("wf"), col("ls_", 18)), 1.0)
         times(cc, by(R("wf"), LC), 1.0)
-        tt(d, by(R("wf"), LL), cc, Op.subtract)
+        tt(d, by(R("wf", 160), LL), cc, Op.subtract)
         times(ke, by(R("wf"), LE), 1024.0)
         tt(kd, R("kb"), d, Op.subtract)
         ts(ne, d, 0.0, Op.not_equal)
@@ -387,39 +374,37 @@ def program(g, core, T, topo):
         red(sm("rq", 0, 1), R("yy", 2, 99, 3), Op.max)
         ts(col("qd", 0, 10), sm("sc", 0, 10), sm("rq", 0, 1), Op.mult)
         scan(sm("dg", 0, 10), sm("sd", 0, 10), col("qd", 0, 10), Op.mult, Op.add)
+        ts(sm("mf", 0, 8), sm("jc", 0, 8), sm("rq", 0, 1), Op.is_lt)
         dg = lambda c: sm("dg", c, c + 1)
         for t in range(3):
             times(R("ba", t, 512, 4), R("idb"), dg(1 + 2 * t))
-            times(R("ba", 512 + t, 544, 4), R("m8"), dg(1 + 2 * t))
         quant(R("qk"), R("sk"), R("ba"))
         for t in range(3):
-            mm(ps(5, 0, J), blk("qa", t), blk("sa", t), col("qk", 0, J), col("sk", 0, J), t == 0, t == 2)
+            mm(ps(5, 0, J), blk("qa", t), blk("sa", t), R("qk"), R("sk"), t == 0, t == 2)
         for t in range(3):
-            mm(ps(7, 0, J), blk("qb", t), blk("sb", t), col("qk", 8, J), col("sk", 8, J), t == 0, t == 2)
+            times(R("bb", 544 + t, 576, 4), R("m8"), dg(1 + 2 * t))
         for t in range(2):
             times(R("bb", t, 512, 4), R("idb"), dg(7 + 2 * t))
-            times(R("bb", 512 + t, 544, 4), R("m8"), dg(7 + 2 * t))
+            times(R("bb", 512 + t, 544, 4), sm("mf", 0, 8), dg(7 + 2 * t))
         quant(R("qw"), R("sw"), R("bb"))
+        for t in range(3):
+            mm(ps(7, 0, J), blk("qb", t), blk("sb", t), col("qw", 16, J), col("sw", 16, J), t == 0, t == 2)
         for t in range(2):
             mm(ps(6, 0, J), blk("qa", t), blk("sa", t), col("qw", 0, J), col("sw", 0, J), t == 0, t == 1)
-        for t in range(2):
-            mm(ps(0, 0, J), blk("qb", t), blk("sb", t), col("qw", 8, J), col("sw", 8, J), t == 0, t == 1)
         times(R("va"), ps(6, 0, J), pf(41), "s")
-        times(R("z0", 16, 32, 2), ps(0, 120, 128), 1.0)
         cp(R("kl"), ps(7, 120, 128))
-        times(sm("kw", 0, 8), ps(7, 120, 128), 1.0)
         tt(R("nv"), by(R("fw"), R("kl")), R("va"), Op.add)
-        tt(R("z0", 1, 16, 2), sm("kw", 0, 8), sm("jc", 0, 8), Op.is_equal)
-        scan(col("z0", 48, 16), col("z0", 0, 16), col("z0", 16, 16), Op.mult, Op.add)
-        cp(R("l1"), by(col("z0", 48, 16), col("ls_", 20)))
+        tt(col("z0", 16, 8), ps(7, 112, 120), col("z0", 0, 8), Op.add)
+        cp(R("l1"), by(col("z0", 16, 8), col("ls_", 22)))
         times(R("kt"), R("tril"), dg(8))
         tt(R("eq"), ps(5, 0, J), R("kt"), Op.is_equal)
         red(sm("lo", 0, 1), R("eq"), Op.max)
         ts(R("b2", 482, 512, 4), R("m8"), sm("lo", 0, 1), Op.mult, -4.0, Op.mult)
         quant(R("ql"), R("sl"), R("b2"))
-        mm(ps(4, 0, J), blk("qb", 2), blk("sb", 2), R("ql"), R("sl"))
-        tt(sm("of", 0, 8), ps(4, 120, 128), sm("kw", 0, 8), Op.add)
-        tt(R("ofs"), sm("of", 0, 8), col("xw", 0, 8), Op.max)
+        for t in range(3):
+            mm(ps(4, 0, J), blk("qb", t), blk("sb", t), col("qw", 16, J), col("sw", 16, J), t == 0, False)
+        mm(ps(4, 0, J), blk("qb", 2), blk("sb", 2), R("ql"), R("sl"), False, True)
+        tt(R("ofs"), ps(4, 120, 128), col("xw", 0, 8), Op.max)
         cp(by(R("fw"), R("ofs")), R("nv"))
         for m in range(8 if k == 2 else 0):
             dma("y", "d7", hbm(T.fo[m:m + 1, :]), (T.fw[15:16, at(m):at(m) + C],) + col("fw", at(m), C)[1:], 1500)

@@ -1,38 +1,44 @@
+import numpy as np
 from concourse.mybir import dt, AluOpType as Op, AxisListType, ActivationFunctionType as Act
 
 F32, BF, I32, U16, MXC, U8 = "float32", "bfloat16", "int32", "uint16", "float8_e4m3fn_x4", "uint8"
 C, J = 320, 128
-SCRATCH = {"tb": ("dram", [6, 8 * C], I32), "raw": ("sbuf", [128, 8, C], I32)}
+XO = 1024
+SCRATCH = {"tb": ("dram", [4, 8 * C], I32), "raw": ("sbuf", [128, 8, C], I32)}
 for _n, _w, _t in (
         ("xi", 1280, BF), ("ui", 512, BF), ("vi", 512, BF), ("wcs", 512, MXC), ("wps", 512, U8), ("wdc", 512, MXC), ("wh", 512, MXC), ("wdp", 512, U8),
-        ("pi", 16, I32), ("pf", 48, F32), ("nat", 320, F32), ("dm", 128, F32), ("ci", 128, BF), ("cf", 96, F32), ("kb", 32, F32),
-        ("tril", 128, BF), ("idb", 128, BF), ("mod", 128, BF), ("m8", 8, BF), ("stp", 576, BF), ("ls_", 24, U16),
-        ("ze", 516, BF), ("za", 516, BF), ("zb", 516, BF),
-        ("qe", 512, MXC), ("se", 512, U8), ("qa", 384, MXC), ("sa", 384, U8), ("qb", 384, MXC), ("sb", 384, U8),
+        ("pi", 16, I32), ("pf", 48, F32), ("nat", 320, F32), ("ci", 128, BF), ("cf", 98, F32),
+        ("idb", 128, BF), ("mod", 128, BF), ("m8", 8, BF), ("stp", 576, BF), ("ls_", 24, U16),
+        ("ze", 516, BF), ("za", 512, BF), ("zb", 516, BF), ("ad", 128, BF), ("zs", 136, BF), ("gt", 72, BF), ("lp", 2, U16),
+        ("qe", 512, MXC), ("se", 512, U8), ("qa", 256, MXC), ("sa", 256, U8), ("qb", 256, MXC), ("sb", 256, U8),
         ("qu", 128, MXC), ("su", 128, U8), ("qv", 128, MXC), ("sv", 128, U8), ("fs", 320, F32),
         ("fw", 2688, F32), ("ox", 576, U16), ("o7", 80, F32), ("wu", 1281, U16), ("wf", 1409, F32), ("lw", 16, U16),
-        ("pw", 224, F32), ("lrow", 128, F32), ("ne", 576, BF), ("so", 576, BF), ("fl", 16, U16),
-        ("sg", 96, F32), ("pp", 96, F32), ("yy", 100, F32), ("lu", 8, U16), ("qu0", 128, MXC), ("su0", 128, U8), ("qd", 16, I32), ("ba", 512, BF), ("bb", 576, BF), ("b2", 512, BF),
-        ("z0", 64, F32), ("m0", 8, I32), ("l1", 16, U16), ("qk", 128, MXC), ("sk", 128, U8), ("qw", 144, MXC), ("sw", 144, U8), ("ql", 128, MXC), ("sl", 128, U8),
-        ("kt", 128, F32), ("eq", 128, F32), ("kl", 8, U16), ("ofs", 8, U16), ("va", 128, F32), ("nv", 128, F32),
+        ("pw", 64, F32), ("lrow", 128, F32), ("ne", 576, BF), ("so", 616, BF), ("fl", 16, U16), ("ne2", 616, BF), ("st2", 616, BF),
+        ("le", 16, U16), ("hi", 8, I32), ("cg", 160, F32), ("ct", 288, F32),
+        ("thr", 128, F32), ("sg", 128, BF), ("nw", 132, BF), ("zi", 136, I32), ("zd", 136, BF), ("dd", 136, BF), ("hs", 528, F32),
+        ("lu", 8, U16), ("qu0", 128, MXC), ("su0", 128, U8), ("ba", 512, BF), ("bb", 640, BF),
+        ("z0", 64, F32), ("m0", 8, I32), ("l1", 16, U16), ("qk", 128, MXC), ("sk", 128, U8), ("qw", 160, MXC), ("sw", 160, U8), ("ql", 128, MXC), ("sl", 128, U8),
+        ("ofs", 8, U16), ("nv", 128, F32),
         ("fh", 3584, BF), ("dh", 256, BF), ("fg", 256, BF), ("nt", 512, BF), ("qn", 128, MXC), ("sn", 128, U8), ("dn", 512, BF), ("mt", 512, BF), ("ht", 512, BF),
-        ("xt", 1792, BF), ("qx", 320, MXC), ("sx", 320, U8), ("xl", 32, U16), ("xw", 256, F32), ("yo", 320, F32),
+        ("xt", XO + 1280, BF), ("qx", 320, MXC), ("sx", 320, U8), ("xl", 32, U16), ("xw", 256, F32), ("yo", 320, F32),
         ("qm0", 128, MXC), ("sm0", 128, U8), ("qm1", 128, MXC), ("sm1", 128, U8), ("qm2", 128, MXC), ("sm2", 128, U8),
         ("qh0", 128, MXC), ("sh0", 128, U8), ("qh1", 128, MXC), ("sh1", 128, U8), ("qh2", 128, MXC), ("sh2", 128, U8),
         ("mc1", 128, MXC), ("mp_1", 128, U8), ("mc2", 128, MXC), ("mp_2", 128, U8), ("hc1", 128, MXC), ("hp1", 128, U8), ("hc2", 128, MXC), ("hp2", 128, U8)):
     SCRATCH[_n] = ("sbuf", [128, _w], _t)
 for _n in range(8):
     SCRATCH["p%d" % _n] = ("psum", [128, 512], F32)
-SMALL = {n: 16 * k for k, n in enumerate(("sc", "sd", "dg", "rq", "lo", "jc", "nl", "lf", "mf"))}
+SMALL = {n: 16 * k for k, n in enumerate(("lo", "nl", "lf"))}
 SEMAPHORES = ["v", "s", "t", "p", "ls", "aw", "ac", "am1", "am2", "ah1", "ah2"] + ["d%d" % _n for _n in range(20)]
 STEP = [1, 2, 3]
 HOME = 0
 FAR = 2048.0
-PARTS = [(0, 256)]
+BIG = 1e29
+PARTS = [(0, 192)]
 ORDER = []
 PASSES = 3
-PIECE = (1, 1, 4, 2)
-CYC, WAKE = 1.0, 150.0
+EARLY = 9000.0
+CYC, WAKE = 1.0, 200.0
+PACES, MOVES, HEAT = [(0.85, 200.0), (1.15, 230.0)], 45000, 100.0
 
 
 def program(g, core, T, topo):
@@ -110,14 +116,21 @@ def program(g, core, T, topo):
         either(out, in_, lambda: V.tensor_scalar(out[0], in_[0], ap(s), ap(b), Op.mult, Op.add),
                lambda: S.activation(out[0], in_[0], Act.Identity, bias=ap(b), scale=ap(s)), [s, b], q)
 
-    def scan(out, d0, d1, op0, op1):
-        op("v", lambda e: V.tensor_tensor_scan(out[0], d0[0], d1[0], 0.0, op0, op1), [out], [d0, d1], ew(out, d0, half(out, d0, d1)))
+    def scan(out, d0, d1, op0, op1, first=0.0):
+        op("v", lambda e: V.tensor_tensor_scan(out[0], d0[0], d1[0], ap(first), op0, op1), [out], [d0, d1, first], ew(out, d0, half(out, d0, d1)))
 
     def red(out, in_, o, **kw):
         op("v", lambda e: V.tensor_reduce(out[0], in_[0], AxisListType.X, o, **kw), [out], [in_], ew(out, in_))
 
     def fill(out, val):
         op("v", lambda e: V.memset(out[0], val), [out], [], ew(out, out, half(out)))
+
+    def zero(out):
+        z = col("ox", 0, out[2])
+        op("vs", lambda e: V.memset(out[0], 0) if e == "v" else S.activation(out[0], z[0], Act.Copy), [out], [z], {"v": ew(out, out, half(out)), "s": ew(out, z) + 10})
+
+    def flat(out, val):
+        iota(out, [[0, out[2]]], int(val), 0)
 
     def quant(q, s, t):
         op("v", lambda e: V.quantize_mx(q[0], s[0], t[0]), [q, s], [t], (15 + 0.27 * t[2]) * CYC)
@@ -147,60 +160,58 @@ def program(g, core, T, topo):
         op("-", None, outs, [(0, [("sent" + sem, 1)])], 0, "arrival", sem=sem, n=len(outs) * len(topo.engines(src, core)))
 
     pf = lambda k: col("pf", k)
-    at = lambda m: J + C * (7 - m)
+    at = lambda m: C * m
     LW = col("lw", 0, 8)
-    L0, LWP, LC, LL, LE, LA, LB, LF = [col("ls_", a, n) for a, n in ((0, 4), (4, 2), (6, 2), (8, 2), (10, 2), (12, 2), (14, 2), (16, 2))]
+    L0, LWP, LC, LL, LE, LK, LG, LF = [col("ls_", a, n) for a, n in ((0, 4), (4, 2), (6, 2), (8, 2), (10, 2), (12, 2), (14, 2), (16, 2))]
 
     def rawv(a, b, c0=0, c1=C):
         return (T.raw[:, a:b, c0:c1], [("raw", sum(bits(C * m + c0, C * m + c1) for m in range(a, b)))], (b - a) * (c1 - c0), False, False)
 
-    fill(rawv(7, 8), 0)
-    ops[-1]["early"] = -2.0
-    fill(rawv(0, 1), 0)
-    ops[-1]["early"] = -1.0
-    iota(rawv(5, 7), [[0, 2 * C]], 0, 0)
-    ops[-1]["early"] = 0.0
-    for m in (1, 2, 3, 4):
-        op("s", lambda e, m=m: S.activation(rawv(m, m + 1)[0], rawv(7, 8)[0], Act.Copy), [rawv(m, m + 1)], [rawv(7, 8)], C * CYC)
-    first = [dma("ys"[k % 2], "d0", hbm(T.tb[k:k + 1, :], "tb"), hbm(T.mp[:] if k % 5 == 0 else T.ar[:, 20 * k - 20:20 * k]), 1500) for k in range(6)]
-    first = [dma("y", "d12", (T.m0[16 * q:16 * q + 16, :],) + R("m0")[1:], hbm(T.mp[0:16, 0:8]), 1500, first) for q in range(8)]
-    own = PARTS[-1][1] if PARTS else 0
-    for n, (a, b) in enumerate(PARTS):
-        first = [dma("s", "d%d" % (16 + n), u8(R("wcs", a, b)), hbm(T.wc[:, 4 * a:4 * b]), 2000, first[:1])]
     iota(col("pi", 11), [[0, 1]], 0, 1)
-    iota(R("dm"), [[-1, 128]], 0, 1)
-    last = []
+    ops[-1]["early"] = -3.0
+    fill(R("ox"), 0)
+    for m in range(8):
+        (fill if m == 0 else flat if m == 2 else lambda o, _: zero(o))(rawv(m, m + 1), 0)
+        ops[-1]["early"] = m / 32 - 2.9
+    own = PARTS[-1][1]
+    first = [dma("s", "d16", u8(R("wcs", 0, own)), hbm(T.wc[:, 0:4 * own]), 1800)]
+    first = [dma("ys"[k % 2], "d0", hbm(T.tb[k:k + 1, :], "tb"), hbm(T.ar[:, 20 * k:20 * k + 20]), 1800, first) for k in range(4)]
+    last = [dma("y", "d12", (T.m0[16 * q:16 * q + 16, :],) + R("m0")[1:], hbm(T.mp[0:16, 0:8]), 1500, first) for q in range(8)]
+    last = [dma("y", "d18", col("xi", 0, 640), hbm(T.x[:, 0:640]), 2300, last)]
     for a in (0, 4):
         for q in range(8):
-            p0 = 16 * q + (11 if q % 2 == 0 else 0)
-            last = [dma("y", "d%d" % (3 + 3 * a), (T.raw[p0:p0 + 5, a:a + 4, :],) + rawv(a, a + 4)[1:], hbm(T.tb[1 - q % 2:6 - q % 2, C * a:C * a + 4 * C], "tb"), 1700 + 150 * a, last)]
-    last = [dma("y", "d4", R("xi"), hbm(T.x[:]), 2800, last)]
-    last = [dma("y", "d2", u8(R("wcs", own, 512)), hbm(T.wc[:, 4 * own:2048]), 4000, last)]
-    last = [dma("y", "d1", R("wps"), hbm(T.ws[:]), 4300, last)]
+            p0 = 16 * q + (15 if q % 2 == 0 else 0)
+            last = [dma("y", "d%d" % (3 + 3 * a), (T.raw[p0:p0 + 1, a:a + 4, :],) + rawv(a, a + 4)[1:], hbm(T.mp[16 * a:16 * a + 64, :]), 1500, last)]
+    last = [dma("y", "d2", u8(R("wcs", own, 512)), hbm(T.wc[:, 4 * own:2048]), 2200, last)]
+    last = [dma("y", "d1", R("wps"), hbm(T.ws[:]), 2400, last)]
+    last = [dma("y", "d4", col("xi", 640, 640), hbm(T.x[:, 640:1280]), 2900, last)]
     heir, giver = T.cores[(r - STEP[HOME]) % N], T.cores[(r + STEP[HOME]) % N]
     for (a, b), mate in zip(PARTS, helpers(core, T, topo)[1]):
-        send([(u8(R("wh", a, b)), u8(R("wcs", a, b)))], mate, "aw", 7500)
+        send([(u8(R("wh", a, b)), u8(R("wcs", a, b)))], mate, "aw", 6600)
         ops[-1]["early"] = 2000.0
-        ops[-1]["w"] = [("sentac", 1)]
-    send([(u8(R("wdc", own, 512)), u8(R("wcs", own, 512))), (R("wdp"), R("wps"))], heir, "ac", 3000)
+        ops[-1]["w"], ops[-1]["soon"] = [("sentac", 1)], True
+    send([(u8(R("wdc", own, 512)), u8(R("wcs", own, 512))), (R("wdp"), R("wps"))], heir, "ac", 4000)
     ops[-1]["early"] = ops[-2]["early"] = 3000.0
+    ops[-1]["soon"] = True
     arrives("ac", giver, [R("wdp"), R("wdc", own, 512)] + [R("wdc", a, b) for a, b in PARTS])
 
-    for k, sh, an in ((0, 0, 15), (1, 4, 1), (2, 5, 1), (3, 6, 1), (4, 0, 1), (5, 1, 1), (6, 2, 1), (7, 0, 7), (8, 1, 7), (9, 4, 7), (10, 0, 31)):
+    for k, sh, an in ((0, 0, 15), (1, 4, 1), (2, 5, 1), (3, 6, 1), (4, 0, 1), (5, 1, 1), (6, 2, 1), (7, 0, 7), (8, 2, 3), (9, 4, 7), (10, 0, 31)):
         ts(col("pi", k), col("pi", 11), sh, Op.logical_shift_right, an, Op.bitwise_and)
     cp(col("pf", 0, 12), col("pi", 0, 12))
-    i_, h_, y_, b_, x0, x1, x2, g8, i2, g_, p31, p_ = [pf(k) for k in range(12)]
+    i_, h_, y_, b_, x0, x1, x2, g8, i4, g_, p31, p_ = [pf(k) for k in range(12)]
     iota(R("nat"), [[1, 320]], 0, 0)
+    ops[-1]["early"] = -2.5
     iota(col("cf", 0, 32), [[0, 4], [1, 8]], 0, 0)
     fma(col("wf", 0, 161), col("nat", 0, 161), 0.0, p_)
     ts(L0, col("nat", 0, 4), 32.0, Op.mult, p31, Op.add)
-    fill(R("ze"), 0.0)
-    ts(R("ze", 3, 515, 4), R("dm"), 0.0, Op.is_equal, 0.5, Op.mult)
+    for a in range(2):
+        zero(blk("ze", a, 258))
+    ts(R("ze", 3, 515, 4), col("nat", 0, J), p_, Op.is_equal, 0.5, Op.mult)
     for t in range(4):
         quant(blk("qe", t), blk("se", t), col("ze", 3 - t, 512))
-    fill(R("ox"), 0)
+        ops[-1]["early"] = 2500.0
     iota(col("o7", 0, 16), [[0, 16]], 0, 0)
-    iota(col("fw", 0, J), [[0, J]], 0, 0)
+    iota(col("fw", at(8), J), [[0, J]], 0, 0)
     fma(pf(12), x0, -65.0, 64.0)
     fma(pf(13), x1, -95.0, pf(12))
     fma(pf(14), pf(13), h_, x0)
@@ -210,74 +221,99 @@ def program(g, core, T, topo):
     ts(LWP, R("cf", 0, 16, 8), pf(14), Op.add, pf(17), Op.add)
     ts(pf(18), y_, h_, Op.not_equal)
     fma(pf(19), y_, 32.0, 64.0)
-    fma(pf(20), b_, 32.0, 16.0)
+    fma(pf(20), b_, 32.0, 16.0 + 7 * 160)
     times(pf(21), pf(18), pf(19))
-    fma(pf(22), i2, 160.0, pf(20))
-    fma(pf(23), x1, -1.0, 1.0)
+    fma(pf(22), i4, -160.0, pf(20))
+    fma(pf(23), x2, -1.0, 1.0)
     fma(pf(24), h_, -1.0, y_)
-    fma(pf(25), pf(24), x1, h_)
-    fma(pf(26), pf(24), pf(23), h_)
-    fma(pf(27), pf(21), pf(23), pf(22))
-    fma(pf(28), pf(21), x1, pf(22))
-    fma(pf(29), pf(25), 6.0, pf(27))
-    ts(LL, R("cf", 0, 16, 8), pf(27), Op.add, pf(25), Op.add)
-    ts(LE, R("cf", 0, 16, 8), pf(28), Op.add, pf(26), Op.add)
-    ts(LC, R("nat", 156, 160, 2), pf(29), Op.add, x0, Op.add)
-    fill(R("lu"), 0)
-    times(col("lu", 0), i2, 16.0, "v")
-    fma(col("lu", 1), g8, 16.0, 1.0, "v")
+    fma(pf(25), pf(24), pf(23), h_)
+    fma(pf(26), pf(24), x2, h_)
+    fma(pf(27), pf(21), x2, pf(22))
+    fma(pf(28), pf(21), pf(23), pf(22))
+    fma(pf(30), x0, 2.0, 156.0)
+    fma(pf(31), x1, 1.0, pf(30))
+    iota(col("cf", 96, 2), [[-640, 2]], 0, 0)
+    ts(LL, col("cf", 96, 2), pf(27), Op.add, pf(25), Op.add)
+    ts(LE, col("cf", 96, 2), pf(28), Op.add, pf(26), Op.add)
+    fma(pf(32), x1, 1.0, 112.0)
+    fma(R("lu"), col("nat", 0, 8), -16.0, pf(32), "v")
+    cp(col("lp", 0), p_)
     fma(pf(38), g8, 8.0, 8.0)
     fma(pf(39), g8, 1.0, 2.0)
     ts(pf(42), pf(38), pf(39), Op.mult, -1.0, Op.add)
     ts(LF, R("cf", 0, 16, 8), pf(42), Op.add)
-    fma(pf(43), x1, -160.0, 64.0)
-    fma(pf(44), pf(43), h_, x0)
-    ts(col("ls_", 18), pf(44), pf(16), Op.add)
     fma(pf(45), x1, 4.0, x0)
     ts(col("ls_", 22), h_, 2.0, Op.mult, pf(45), Op.add)
-    ts(pf(40), p31, 15.0, Op.is_ge)
-    ts(pf(41), p31, 16.0, Op.is_le, pf(40), Op.mult)
-    iota(col("cf", 32, 32), [[0, 2], [1, 8], [0, 2]], 0, 0)
-    fma(R("kb"), col("cf", 32, 32), -1024.0 * C, 1024.0 * at(0))
-    iota(R("pp"), [[0, 96]], 0, 0)
-    iota(R("sg", 0, 96, 3), [[0, 32]], 0, 0)
-    times(col("yy", 98), p_, 1024.0)
+    ts(pf(33), x2, h_, Op.not_equal, 144.0, Op.mult)
+    fma(pf(34), i4, 16.0, pf(31))
+    fma(pf(35), h_, -10.0, -145.0)
+    fma(pf(36), pf(35), 1.0, pf(33))
+    ts(LK, R("nat", 0, J, 64), pf(34), Op.add, pf(36), Op.add)
+    for a in (0, 144):
+        iota(col("cg", a, 16), [[0, 16]], 0, 0)
+    fma(pf(40), g8, 8.0, 29.0)
+    fma(pf(41), g8, -0.125, 17.0)
+    fma(pf(43), i_, 0.125, pf(41))
+    fma(pf(44), pf(40), g8, pf(43))
+    ts(LG, R("nat", 0, 4, 2), pf(44), Op.add)
+    for t in range(4):
+        iota(R("thr", t, J, 4), [[0, 16], [1, 2]] if t < 2 else [[0, 8], [1, 2], [0, 2]], -(t % 2), 0)
+    times(R("thr"), R("thr"), BIG)
+    iota(R("ad"), [[0, 32], [1, 4]], 0, 0)
+    iota(R("zs"), [[0, 68], [-32, 2]], 0, 0)
+    flat(R("zi"), 0)
+    flat(col("nw", 0, 4), 0)
+    flat(col("hs", 512, 16), 0)
+    flat(R("gt"), 0)
+    for a, b, st, val in ((4, 72, 4, 1.0), (0, 1, 1, -7.0), (32, 33, 1, 0.0), (36, 72, 32, -4.0), (52, 53, 1, 2.0)):
+        flat(R("gt", a, b, st), val)
     xw = lambda k: blk("xw", k, 32)
     fma(xw(0), col("cf", 0, 32), 16.0, i_)
+    fma(col("xw", 224, 8), col("xw", 0, 8), 1.0, 1.0 * at(8))
     iota(col("cf", 64, 32), [[1, 4], [0, 8]], 0, 0)
     fma(xw(1), xw(0), -FAR, 1.0 * J)
-    times(xw(2), xw(0), 4.0)
-    tt(xw(2), xw(2), col("cf", 64, 32), Op.add)
-    fma(xw(3), xw(0), -FAR, 4.0 * J)
-    tt(xw(3), xw(3), col("cf", 64, 32), Op.add)
-    fill(R("stp"), FAR)
-    for a, b, t in ((0, 3, 3), (1, 8, 2), (2, 5, 4), (6, 9, 1)):
-        fill(sm("sc", a, b + 1, b - a), 32.0 ** -t)
-    fill(sm("sc", 4, 5), 0.0)
-    fill(sm("sc", 7, 8), 1.0)
-    fill(sm("sd", 0, 10), 0.0)
-    ts(sm("sd", 1, 10, 2), sm("sd", 0, 10, 2), -32.0, Op.add)
-    for n, o, st in (("idb", Op.not_equal, -1), ("tril", Op.is_ge, 1)):
-        op("p", lambda e, n=n, o=o, st=st: g.affine_select(T[n][:], T.ze[:, 0:512:4], [[st, J]], o, 1.0, 0, -st), [R(n)], [R("ze", 0, 512, 4)], 430.0)
+    fma(xw(3), col("cf", 64, 32), 1.0, 1.0 * XO)
+    for a in range(2):
+        iota(blk("stp", a, 288), [[0, 288]], int(FAR), 0)
+    run = lambda c: 8 * c * c + 13 * c
+    for a in range(2):
+        iota(blk("ne2", a, 308), [[0, 308]], int(256 * FAR), 0)
+        iota(blk("st2", a, 308), [[0, 308]], 0, 0)
+    fma(pf(46), i_, -1.0, 15.0)
+    for c in range(8):
+        ts(col("st2", run(c) + 1, 16), col("nat", 0, 16), pf(46), Op.is_equal, 256 * FAR, Op.mult)
+    for t, (a, b) in enumerate(((2.0, 0.0), (0.0, 1.0), (0.0, 255.0), (2.0, 256.0))):
+        fma(col("xw", 64 + 8 * t, 8), col("xw", 0, 8), a, b)
+    cp(by(R("st2"), LG), xw(2))
+    ts(R("idb"), col("nat", 0, J), p_, Op.is_equal)
     iota(R("ci"), [[0, 8], [1, 16]], 0, 0)
     ts(R("mod"), R("ci"), i_, Op.is_equal)
-    ts(R("m8"), col("nat", 0, 8), g_, Op.is_equal)
-    fma(sm("jc", 0, 8), R("m8"), -1024.0 * C - 512, 1024.0 * (at(0) + C))
-    for n in ("ba", "bb", "b2"):
-        iota(R(n), [[0, R(n)[2]]], 0, 0)
-    fill(R("za"), 0.0)
-    times(R("zb"), R("za"), 1.0, "s")
-    for t in range(3):
-        fma(R("za", 3, 515, 4), R("mod"), 0.0, 32.0 ** t)
-        quant(blk("qa", t), blk("sa", t), col("za", 3 - t, 512))
-        times(R("zb", 3, 515, 4), R("mod"), 32.0 ** t)
-        quant(blk("qb", t), blk("sb", t), col("zb", 3 - t, 512))
+    ts(R("m8"), col("nat", 0, 8), g_, Op.is_equal, 0.5, Op.mult)
+    iota(R("ba", 3, 512, 4), [[0, J]], 0, 0)
+    iota(R("bb"), [[0, 640]], 0, 0)
+    for t, wt in enumerate((-1.0, -32.0, -384.0, 0.0)):
+        flat(R("za", t, 512, 4), wt)
+    quant(blk("qa", 0), blk("sa", 0), R("za"))
+    for t, wt in enumerate((1.0, 32.0, 384.0)):
+        op("p", lambda e, t=t, wt=wt: g.affine_select(T.za[:, t:512:4], T.ze[:, 0:512:4], [[-1, J]], Op.is_ge, wt, 0, 1), [R("za", t, 512, 4)], [R("ze", 0, 512, 4)], 170 + 2 * J * CYC)
+    quant(blk("qa", 1), blk("sa", 1), R("za"))
+    ops[-1]["early"] = EARLY
+    for t in range(2):
+        flat(R("zb", t, 516, 4), 0)
+    for n, wts in enumerate(((1.0, 32.0), (1.0 * C, 1.0 * C))):
+        for t in range(2):
+            times(R("zb", 2 + t, 514, 4), R("mod"), wts[t])
+        quant(blk("qb", n), blk("sb", n), col("zb", 2 - 2 * n, 512))
+        ops[-1]["early"] = EARLY
 
     for a in (0, 4):
         for i in range(16):
-            o, v = R("fw", at(a + 3) + i, at(a) + C, 16), rawv(a, a + 4, 20 * i, 20 * i + 20)
-            v = (T.raw[:, a + 3:a - 1 if a else None:-1, 20 * i:20 * i + 20],) + v[1:]
+            o, v = R("fw", at(a) + i, at(a + 4), 16), rawv(a, a + 4, 20 * i, 20 * i + 20)
             either(o, v, lambda o=o, v=v: V.tensor_copy(o[0], v[0]), lambda o=o, v=v: S.activation(o[0], v[0], Act.Copy))
+    for a in (0, 4):
+        for q in range(8):
+            p0 = 16 * q + (11 if q % 2 == 0 else 1)
+            last = [dma("y", "d%d" % (13 + a), (T.raw[p0:p0 + 4, a:a + 4, :],) + rawv(a, a + 4)[1:], hbm(T.tb[:, C * a:C * a + 4 * C], "tb"), 2500, last)]
 
     def chase(known=False):
         for s in range(8):
@@ -292,16 +328,27 @@ def program(g, core, T, topo):
                 times(col("wf", 160 * s + 161, 160), col("wu", 160 * s + 161, 160), 1.0, "s")
         cp(R("lw"), by(R("wf"), col("ls_", 4)))
 
-    def asks():
-        cc, d, ke, kd, v, ne = [blk("pw", k, 32) for k in range(6)]
-        times(col("z0", 0, 16), by(R("wf"), col("ls_", 18)), 1.0)
-        times(cc, by(R("wf"), LC), 1.0)
+    def asks(k):
+        cc, d = R("zi", 71, 135, 2), col("pw", 0, 32)
+        times(R("zi", 3, 67, 2), by(R("wf", 0, 1281), LE), 1.0, "v")
+        e, a, b = R("zi", 3, 67, 8), col("pw", 40, 8), col("pw", 48, 8)
+        ts(R("hi"), e, -7.5, Op.add, 1 / 16, Op.mult)
+        times(a, e, 20.0)
+        times(b, R("hi"), 1.0 - C)
+        tt(R("le", 0, 16, 2), a, b, Op.add)
+        for c in range(8):
+            times(col("cg", 16 + 16 * c, 16), by((T.raw[:, 7 - c, :],) + rawv(7 - c, 8 - c)[1:], col("le", 2 * c)), 1.0)
+        tr(col("ct", 0, J), col("cg", 16, J))
+        tr(col("ct", J, 160), R("cg"))
+        times(cc, by(R("ct"), LK), 1.0, "v")
         tt(d, by(R("wf", 160), LL), cc, Op.subtract)
-        times(ke, by(R("wf"), LE), 1024.0)
-        tt(kd, R("kb"), d, Op.subtract)
-        ts(ne, d, 0.0, Op.not_equal)
-        tt(v, ke, kd, Op.add)
-        tt(R("pp", 0, 96, 3), v, ne, Op.mult)
+        for a in range(2):
+            ts(R("thr", 5 * a, J, 8), R("pw", a, 32, 2), 0.0, Op.is_equal, BIG * (2 * a - 1), Op.mult)
+        ts(R("zi", 0, 136, 2), R("zi", 1, 136, 2), 1 / 32, Op.mult)
+        scan(R("zd"), R("zs"), R("zi"), Op.mult, Op.add)
+        for a in (0, 68):
+            tt(col("dd", a, 66), col("zd", a, 66), col("zd", a + 2, 66), Op.subtract)
+        tt(col("dd", 134, 2), col("zd", 56, 2), col("zd", 126, 2), Op.subtract)
 
     def unpack(bank, w, q, s, planes=range(4)):
         for t in planes:
@@ -311,15 +358,22 @@ def program(g, core, T, topo):
         return col("fh", (C + J) * (4 * (k % 2) + t + 1) - w, w)
 
     def state(k, tile):
-        quant(R("qx"), R("sx"), tile)
+        for a in range(2):
+            quant(blk("qx", a, 160), blk("sx", a, 160), col(tile[0], tile[1] + 640 * a, 640))
         unpack(0, C, R("qx"), R("sx"))
         for t in range(4):
             times(fh(k, t), ps(t, 0, C), 1.0)
 
-    state(0, R("xi"))
+    for a in range(2):
+        q, sp = blk("qx", a, 160), blk("sx", a, 160)
+        quant(q, sp, blk("xi", a, 640))
+        unpack(4 * a, 160, q, sp)
+        for t in range(4):
+            times(col("fh", (C + J) * t + J + 160 * a, 160), ps(4 * a + t, 0, 160), 1.0)
     cp(R("l1"), by(R("m0"), col("ls_", 22)))
     chase(True)
-    dma("y", "d5", R("ui"), hbm(T.u[:]), 5500, last)
+    ops[-1]["soon"] = True
+    dma("y", "d5", R("ui"), hbm(T.u[:]), 3000, last)
     quant(R("qu0"), R("su0"), R("ui"))
     word = lambda v: (v[0].bitcast(dt.uint32),) + v[1:]
     cp(word(R("qu")), by(word(R("qu0")), R("lu")))
@@ -327,7 +381,7 @@ def program(g, core, T, topo):
     for k in range(3):
         donor, client = T.cores[(r + STEP[k]) % N], T.cores[(r - STEP[k]) % N]
         qm, sp, qh, sh = [R("%s%d" % (n, k)) for n in ("qm", "sm", "qh", "sh")]
-        asks()
+        asks(k)
         if k:
             quant(R("qn"), R("sn"), R("nt"))
             unpack(0, J, R("qn"), R("sn"))
@@ -342,16 +396,12 @@ def program(g, core, T, topo):
             mc, mp, wc, wp, hc, hp = R("mc%d" % x), R("mp_%d" % x), "wcs", "wps", R("hc%d" % x), R("hp%d" % x)
             send([(u8(mc), u8(qm)), (mp, sp)], donor, "am%d" % x, 2100)
             arrives("am%d" % x, client, [mc, mp])
-        if k and k != HOME:
-            state(k, col("xt", 4 * J, 4 * C))
-        for t in range(4 if k else 0):
-            n = 8 if k != HOME else PIECE[t]
-            for c in range(0, 8, n):
-                cp(by(fh(k, t, C + J), col("xl", c, n) if n > 1 else col("xl", 8 + 2 * c)), col("dn", J * t + 16 * c, 16 * n))
+        if k:
+            state(k, ("xt", XO))
+            for t in range(4):
+                cp(by(fh(k, t, C + J), col("xl", 0, 8)), blk("dn", t))
         for t in range(4):
-            times(R("xt", 4 * J + t, 4 * (J + C), 4), fh(k, t), 2.0)
-        if k + 1 == HOME:
-            state(k + 1, col("xt", 4 * J, 4 * C))
+            times(R("xt", XO + t, XO + 4 * C, 4), fh(k, t), 2.0)
         for b in range(4):
             mm(ps(4 + b, 0, J), blk(wc, b), blk(wp, b), mc, mp)
         for b in range(4):
@@ -368,43 +418,34 @@ def program(g, core, T, topo):
         unpack(0, J, hc, hp)
         for t in range(2):
             times(blk("dh", t), ps(t, 0, J), 1.0, "s")
-        for a, b, st, c, o in ((1, 48, 3, 0, Op.is_le), (49, 96, 3, 0, Op.is_gt), (2, 96, 6, 16, Op.is_le), (5, 96, 6, 16, Op.is_gt)):
-            ts(R("sg", a, b, st), ps(4, c, c + 16), 0.0, o)
-        scan(col("yy", 0, 96), R("sg"), R("pp"), Op.mult, Op.add)
-        red(sm("rq", 0, 1), R("yy", 2, 99, 3), Op.max)
-        ts(col("qd", 0, 10), sm("sc", 0, 10), sm("rq", 0, 1), Op.mult)
-        scan(sm("dg", 0, 10), sm("sd", 0, 10), col("qd", 0, 10), Op.mult, Op.add)
-        ts(sm("mf", 0, 8), sm("jc", 0, 8), sm("rq", 0, 1), Op.is_lt)
-        dg = lambda c: sm("dg", c, c + 1)
-        for t in range(3):
-            times(R("ba", t, 512, 4), R("idb"), dg(1 + 2 * t))
+        for a, o in ((0, Op.is_gt), (1, Op.is_le)):
+            tt(R("sg", a, J, 2), ps(4, a, J, 2), R("thr", a, J, 2), o)
+        scan(col("nw", 4, J), R("ad"), R("sg"), Op.min, Op.max)
+        dg = lambda t: col("hs", 512 + t)
+        for t, d in ((4, R("dd", 1, 67, 2)), (5, R("dd", 0, 66, 2)), (8, col("gt", 36, 33)), (9, R("dd", 69, 135, 2)), (10, R("dd", 68, 134, 2)), (6, col("gt", 0, 33))):
+            scan(R("hs", t, 528, 16), R("nw", 3, 132, 4), d, Op.mult, Op.add)
+        for t in range(2):
+            scan(R("hs", 464 + t, 528, 16), R("nw", 119, 132, 4), R("dd", 127 - t, 134, 2), Op.mult, Op.add, col("dd", 135 - t))
+        for t, c in enumerate((4, 5, 8)):
+            times(R("ba", t, 512, 4), R("idb"), dg(c))
         quant(R("qk"), R("sk"), R("ba"))
-        for t in range(3):
-            mm(ps(5, 0, J), blk("qa", t), blk("sa", t), R("qk"), R("sk"), t == 0, t == 2)
-        for t in range(3):
-            times(R("bb", 544 + t, 576, 4), R("m8"), dg(1 + 2 * t))
+        mm(ps(5, 0, J), blk("qa", 1), blk("sa", 1), R("qk"), R("sk"), True, False)
+        mm(ps(5, 0, J), R("qk"), R("sk"), blk("qa", 0), blk("sa", 0), False, True)
+        red(sm("lo", 0, 1), ps(5, 0, J), Op.min, apply_absolute_value=True)
         for t in range(2):
-            times(R("bb", t, 512, 4), R("idb"), dg(7 + 2 * t))
-            times(R("bb", 512 + t, 544, 4), sm("mf", 0, 8), dg(7 + 2 * t))
+            times(R("bb", t, 512, 4), R("idb"), dg(9 + t))
+        cp(by(R("bb", 512), col("lp", 0)), col("hs", 512, 16))
         quant(R("qw"), R("sw"), R("bb"))
-        for t in range(3):
-            mm(ps(7, 0, J), blk("qb", t), blk("sb", t), col("qw", 16, J), col("sw", 16, J), t == 0, t == 2)
-        for t in range(2):
-            mm(ps(6, 0, J), blk("qa", t), blk("sa", t), col("qw", 0, J), col("sw", 0, J), t == 0, t == 1)
-        times(R("va"), ps(6, 0, J), pf(41), "s")
-        cp(R("kl"), ps(7, 120, 128))
-        tt(R("nv"), by(R("fw"), R("kl")), R("va"), Op.add)
-        tt(col("z0", 16, 8), ps(7, 112, 120), col("z0", 0, 8), Op.add)
-        cp(R("l1"), by(col("z0", 16, 8), col("ls_", 22)))
-        times(R("kt"), R("tril"), dg(8))
-        tt(R("eq"), ps(5, 0, J), R("kt"), Op.is_equal)
-        red(sm("lo", 0, 1), R("eq"), Op.max)
-        ts(R("b2", 482, 512, 4), R("m8"), sm("lo", 0, 1), Op.mult, -4.0, Op.mult)
-        quant(R("ql"), R("sl"), R("b2"))
-        for t in range(3):
-            mm(ps(4, 0, J), blk("qb", t), blk("sb", t), col("qw", 16, J), col("sw", 16, J), t == 0, False)
-        mm(ps(4, 0, J), blk("qb", 2), blk("sb", 2), R("ql"), R("sl"), False, True)
-        tt(R("ofs"), ps(4, 120, 128), col("xw", 0, 8), Op.max)
+        mm(ps(7, 0, J), blk("qb", 0), blk("sb", 0), col("qw", 32, J), col("sw", 32, J))
+        mm(ps(6, 0, J), blk("qa", 0), blk("sa", 0), col("qw", 0, J), col("sw", 0, J))
+        times(R("nv"), ps(6, 0, J), -1.0)
+        times(col("z0", 16, 8), ps(7, 96, J, 4), 1.0)
+        times(R("l1"), by(col("z0", 16, 8), col("ls_", 22)), 1.0)
+        ts(R("bb", 519, 640, 16), R("m8"), sm("lo", 0, 1), Op.is_gt, 16.0, Op.mult)
+        quant(R("ql"), R("sl"), col("bb", J, 512))
+        mm(ps(4, 0, J), blk("qb", 0), blk("sb", 0), col("qw", 32, J), col("sw", 32, J), True, False)
+        mm(ps(4, 0, J), blk("qb", 1), blk("sb", 1), R("ql"), R("sl"), False, True)
+        tt(R("ofs"), ps(4, 97, J, 4), col("xw", 224, 8), Op.min)
         cp(by(R("fw"), R("ofs")), R("nv"))
         for m in range(8 if k == 2 else 0):
             dma("y", "d7", hbm(T.fo[m:m + 1, :]), (T.fw[15:16, at(m):at(m) + C],) + col("fw", at(m), C)[1:], 1500)
@@ -421,22 +462,22 @@ def program(g, core, T, topo):
         times((T.lrow[:, ::-1],) + R("lrow")[1:], by(R("nat"), LW), 1.0)
         for c in range(7, -1, -1):
             o, i, a, b = col("ne", 8 * c * (c + 1), 16 * c + 16), R("lrow", 112 - 16 * c), sm("lf", c, c + 1), sm("nl", c, c + 1)
+            if k == 2:
+                o = col("ne2", run(c), 16 * c + 16)
             either(o, i, lambda o=o, i=i, a=a: V.tensor_scalar(o[0], i[0], a[0], 256 * FAR, Op.not_equal, Op.mult),
                    lambda o=o, i=i, b=b: S.activation(o[0], i[0], Act.Abs, bias=b[0], scale=256 * FAR), [a, b])
-        scan(R("so"), R("stp"), R("ne"), Op.add, Op.min)
-        if k < 2:
-            ts(R("fl"), by(R("so"), col("ls_", 16)), 1 / FAR, Op.mult)
         times(xw(4), by(R("wf"), LWP), 4.0 if k == 2 else 1.0)
         tt(xw(5), xw(4), xw(3 if k == 2 else 1), Op.add)
-        tt(xw(6), by(R("so"), LF), xw(5), Op.add)
-        if k == 2:
-            tt(R("xl"), xw(6), xw(2), Op.max)
-        else:
+        if k < 2:
+            scan(col("so", 0, 576), R("stp"), R("ne"), Op.add, Op.min)
+            ts(R("fl"), by(col("so", 0, 576), col("ls_", 16)), 1 / FAR, Op.mult)
+            tt(xw(6), by(col("so", 0, 576), LF), xw(5), Op.add)
             tt(col("xl", 0, 8), col("xw", 192, 8), col("xw", 0, 8), Op.max)
-            if k + 1 == HOME:
-                tt(R("xl", 8, 24, 2), col("xw", 192, 8), col("xw", 0, 8), Op.max)
+        else:
+            scan(R("so"), R("st2"), R("ne2"), Op.add, Op.min)
+            tt(R("xl"), by(R("so"), LG), xw(5), Op.min)
     cp(by(R("xt"), R("xl")), R("nt"))
-    quant(R("qx"), R("sx"), col("xt", 4 * J, 4 * C))
+    quant(R("qx"), R("sx"), col("xt", XO, 4 * C))
     dma("y", "d8", hbm(T.oc[:]), u8(R("qx")), 1800)
     for a in range(2):
         mm(ps(4 + a, 0, 160), R("qv"), R("sv"), blk("qx", a, 160), blk("sx", a, 160))
@@ -519,7 +560,66 @@ def plan(ops, before):
         last = [back[i] + cost(ops[i]["hold"], beng[i]) for i in range(n)]
         key = [max(last) - x for x in last]
     _, start, eng = best
-    return [(i, eng[i]) for i in sorted(range(n), key=lambda k: (start[k], k))]
+    return mend(ops, before, [(i, eng[i]) for i in sorted(range(n), key=lambda k: (start[k], k))])
+
+
+def mend(ops, before, seq):
+    n = len(ops)
+    cost = lambda x, e: x[e] if isinstance(x, dict) else x
+    pre = [[(j, 0.0 if o["kind"] == "arrival" or (o["kind"] == "acc" and ops[j]["q"] == "t") else 1.0) for j in before[i]] for i, o in enumerate(ops)]
+    hard = [set(before[i]) | set(o.get("after", [])) for i, o in enumerate(ops)]
+    post = [[] for _ in ops]
+    for i in range(n):
+        for j in hard[i]:
+            post[j].append(i)
+    tab = [[{e: (cost(o["hold"], e) * f, cost(o["done"], e) * f) for e in o["q"]} for o in ops for f in [s / CYC if o["kind"] in ("op", "acc") else 1.0]] for s, _ in PACES]
+
+    soon = [i for i, o in enumerate(ops) if o.get("soon")]
+
+    def run(seq, k, old=None, a=0):
+        w, tb = PACES[k][1], tab[k]
+        a -= a % 32
+        end, why, marks = (list(old[0]), list(old[1]), old[2][:a // 32 + 1]) if old else ([0.0] * n, [None] * n, [({}, {})])
+        free, last = dict(marks[-1][0]), dict(marks[-1][1])
+        for p in range(a, n):
+            if p % 32 == 0 and p > a:
+                marks.append((dict(free), dict(last)))
+            i, e = seq[p]
+            t, c = free.get(e, 0.0), last.get(e)
+            for j, f in pre[i]:
+                if end[j] + f * w > t:
+                    t, c = end[j] + f * w, j
+            h, d = tb[i][e]
+            end[i], why[i] = t + d, c
+            if h:
+                free[e], last[e] = t + h, i
+        return end, why, marks
+
+    total = lambda runs: sum(max(x[0]) + 0.3 * sum(x[0][i] for i in soon) + 1e-3 * sum(x[0]) for x in runs)
+    now = [run(seq, k) for k in range(len(PACES))]
+    rng, best, path, pos = np.random.RandomState(1), total(now), [], {}
+    for m in range(MOVES):
+        if m % 20 == 0 or not path:
+            end, why, _ = now[m // 20 % len(PACES)]
+            path = [end.index(max(end)) if m % 80 else soon[m // 80 % len(soon)]]
+            while why[path[-1]] is not None:
+                path.append(why[path[-1]])
+        pos = pos or {i: p for p, (i, _) in enumerate(seq)}
+        a = min(n - 1, max(0, pos[path[int(rng.randint(len(path)))]] + int(rng.randint(-10, 11))))
+        i, e = seq[a]
+        if ops[i]["kind"] in ("dma", "send"):
+            continue
+        if len(ops[i]["q"]) > 1 and rng.rand() < 0.4:
+            e = ops[i]["q"].replace(e, "")
+        lo, hi = max([pos[j] for j in hard[i]] + [-1]) + 1, min([pos[j] for j in post[i]] + [n]) - 1
+        b = int(rng.randint(lo, hi + 1)) if rng.rand() < 0.1 else min(hi, max(lo, a + int(rng.randint(-14, 15))))
+        new = seq[:a] + seq[a + 1:]
+        new.insert(b, (i, e))
+        runs = [run(new, k, now[k], min(a, b)) for k in range(len(PACES))]
+        t = total(runs)
+        if t <= best + max(0.0, HEAT * (1 - m / (0.8 * MOVES)) * rng.rand() ** 2):
+            seq, now, pos, best, path = new, runs, {}, t, path if t == best else []
+    return seq
 
 
 def helpers(core, T, topo):

import numpy as np
from concourse.mybir import dt, AluOpType as Op, AxisListType, ActivationFunctionType as Act

F32, BF, I32, U16, MXC, U8 = "float32", "bfloat16", "int32", "uint16", "float8_e4m3fn_x4", "uint8"
C, J = 320, 128
XO = 1024
SCRATCH = {"tb": ("dram", [4, 8 * C], I32), "raw": ("sbuf", [128, 8, C], I32)}
for _n, _w, _t in (
        ("xi", 1280, BF), ("ui", 512, BF), ("vi", 512, BF), ("wcs", 512, MXC), ("wps", 512, U8), ("wdc", 512, MXC), ("wh", 512, MXC), ("wdp", 512, U8),
        ("pi", 16, I32), ("pf", 48, F32), ("nat", 320, F32), ("ci", 128, BF), ("cf", 98, F32),
        ("idb", 128, BF), ("mod", 128, BF), ("m8", 8, BF), ("stp", 576, BF), ("ls_", 24, U16),
        ("ze", 516, BF), ("za", 512, BF), ("zb", 516, BF), ("ad", 128, BF), ("zs", 136, BF), ("gt", 72, BF), ("lp", 2, U16),
        ("qe", 512, MXC), ("se", 512, U8), ("qa", 256, MXC), ("sa", 256, U8), ("qb", 256, MXC), ("sb", 256, U8),
        ("qu", 128, MXC), ("su", 128, U8), ("qv", 128, MXC), ("sv", 128, U8), ("fs", 320, F32),
        ("fw", 2688, F32), ("ox", 576, U16), ("o7", 80, F32), ("wu", 1281, U16), ("wf", 1409, F32), ("lw", 16, U16),
        ("pw", 64, F32), ("lrow", 128, F32), ("ne", 576, BF), ("so", 616, BF), ("fl", 16, U16), ("ne2", 616, BF), ("st2", 616, BF),
        ("le", 16, U16), ("hi", 8, I32), ("cg", 160, F32), ("ct", 288, F32),
        ("thr", 128, F32), ("sg", 128, BF), ("nw", 132, BF), ("zi", 136, I32), ("zd", 136, BF), ("dd", 136, BF), ("hs", 528, F32),
        ("lu", 8, U16), ("qu0", 128, MXC), ("su0", 128, U8), ("ba", 512, BF), ("bb", 640, BF),
        ("z0", 64, F32), ("m0", 8, I32), ("l1", 16, U16), ("qk", 128, MXC), ("sk", 128, U8), ("qw", 160, MXC), ("sw", 160, U8), ("ql", 128, MXC), ("sl", 128, U8),
        ("ofs", 8, U16), ("nv", 128, F32),
        ("fh", 3584, BF), ("dh", 256, BF), ("fg", 256, BF), ("nt", 512, BF), ("qn", 128, MXC), ("sn", 128, U8), ("dn", 512, BF), ("mt", 512, BF), ("ht", 512, BF),
        ("xt", XO + 1280, BF), ("qx", 320, MXC), ("sx", 320, U8), ("xl", 32, U16), ("xw", 256, F32), ("yo", 320, F32),
        ("qm0", 128, MXC), ("sm0", 128, U8), ("qm1", 128, MXC), ("sm1", 128, U8), ("qm2", 128, MXC), ("sm2", 128, U8),
        ("qh0", 128, MXC), ("sh0", 128, U8), ("qh1", 128, MXC), ("sh1", 128, U8), ("qh2", 128, MXC), ("sh2", 128, U8),
        ("mc1", 128, MXC), ("mp_1", 128, U8), ("mc2", 128, MXC), ("mp_2", 128, U8), ("hc1", 128, MXC), ("hp1", 128, U8), ("hc2", 128, MXC), ("hp2", 128, U8)):
    SCRATCH[_n] = ("sbuf", [128, _w], _t)
for _n in range(8):
    SCRATCH["p%d" % _n] = ("psum", [128, 512], F32)
SMALL = {n: 16 * k for k, n in enumerate(("lo", "nl", "lf"))}
SEMAPHORES = ["v", "s", "t", "p", "ls", "aw", "ac", "am1", "am2", "ah1", "ah2"] + ["d%d" % _n for _n in range(20)]
STEP = [1, 2, 3]
HOME = 0
FAR = 2048.0
BIG = 1e29
PARTS = [(0, 192)]
ORDER = []
PASSES = 3
EARLY = 9000.0
CYC, WAKE = 1.0, 200.0
PACES, MOVES, HEAT = [(0.85, 200.0), (1.15, 230.0)], 45000, 100.0


def program(g, core, T, topo):
    r = T.rank_of(core)
    N = len(T.cores)
    V, S = g.vector, g.scalar
    Q = {"s": S, "y": g.sync}
    ops = []

    def bits(a, b, st=1):
        return sum(1 << c for c in range(a, b, st)) if st != 1 else (1 << b) - (1 << a)

    def R(name, a=0, b=None, st=1):
        b = T[name].shape[1] if b is None else b
        return (T[name][:, a:b:st], [(name, bits(a, b, st))], len(range(a, b, st)), SCRATCH[name][2] in (BF, U16), False)

    def col(name, k, n=1):
        return R(name, k, k + n)

    def blk(name, t, w=128):
        return R(name, w * t, w * t + w)

    def by(win, off):
        return (win[0].indirect(off[0]), win[1] + off[1], 16 * off[2], False, True)

    def sm(name, a=0, b=16, st=1):
        return R("fs", SMALL[name] + a, SMALL[name] + b, st)

    def ps(k, a, b, st=1):
        return (T["p%d" % k][:, a:b:st], [("#%d" % k, 1)], len(range(a, b, st)), False, False)

    def u8(v):
        return (v[0].bitcast(dt.uint8),) + v[1:]

    def ap(x):
        return x[0] if isinstance(x, tuple) else x

    def op(q, f, out, ins, cost, kind="op", **kw):
        ins = [x for x in ins if isinstance(x, tuple)]
        w = [k for o in out for k in o[1][:1]]
        rd = [k for x in ins for k in x[1]] + [k for o in out for k in o[1][1:]]
        ops.append(dict(q=q, f=f, r=rd, w=w, hold=cost, done=kw.pop("done", cost), kind=kind, **kw))
        return len(ops) - 1

    def ew(out, in0, per=1.0):
        if in0[4]:
            return 55 + 1.55 * in0[2] * CYC
        if out[4]:
            return 55 + 3.8 * out[2] * CYC
        return max(64, in0[2] * per) * CYC

    def half(*a):
        return 0.5 if all(x[3] for x in a) else 1.0

    def ts(out, in0, s1, op0, s2=None, op1=None):
        f = (lambda e: V.tensor_scalar(out[0], in0[0], ap(s1), None, op0)) if op1 is None else (lambda e: V.tensor_scalar(out[0], in0[0], ap(s1), ap(s2), op0, op1))
        op("v", f, [out], [in0, s1, s2], ew(out, in0, half(out, in0)))

    def tt(out, a, b, o):
        op("v", lambda e: V.tensor_tensor(out[0], a[0], b[0], o), [out], [a, b], ew(out, a, 1.0 if "#" in a[1][0][0] + b[1][0][0] else 2.0))

    def cp(out, in_):
        op("v", lambda e: V.tensor_copy(out[0], in_[0]), [out], [in_], ew(out, in_, half(out, in_)))

    def tr(out, in_):
        op("v", lambda e: V.transpose(out[0], in_[0]), [out], [in_], ew(out, in_, half(in_)))

    def either(out, in_, fv, fs, more=(), q="vs"):
        op(q, lambda e: fv() if e == "v" else fs(), [out], [in_] + list(more), {"v": ew(out, in_, half(out, in_)), "s": ew(out, in_) + 10})

    def times(out, in_, s, q="vs"):
        either(out, in_, lambda: V.tensor_scalar(out[0], in_[0], ap(s), None, Op.mult), lambda: S.activation(out[0], in_[0], Act.Copy, scale=ap(s)), [s], q)

    def fma(out, in_, s, b, q="vs"):
        either(out, in_, lambda: V.tensor_scalar(out[0], in_[0], ap(s), ap(b), Op.mult, Op.add),
               lambda: S.activation(out[0], in_[0], Act.Identity, bias=ap(b), scale=ap(s)), [s, b], q)

    def scan(out, d0, d1, op0, op1, first=0.0):
        op("v", lambda e: V.tensor_tensor_scan(out[0], d0[0], d1[0], ap(first), op0, op1), [out], [d0, d1, first], ew(out, d0, half(out, d0, d1)))

    def red(out, in_, o, **kw):
        op("v", lambda e: V.tensor_reduce(out[0], in_[0], AxisListType.X, o, **kw), [out], [in_], ew(out, in_))

    def fill(out, val):
        op("v", lambda e: V.memset(out[0], val), [out], [], ew(out, out, half(out)))

    def zero(out):
        z = col("ox", 0, out[2])
        op("vs", lambda e: V.memset(out[0], 0) if e == "v" else S.activation(out[0], z[0], Act.Copy), [out], [z], {"v": ew(out, out, half(out)), "s": ew(out, z) + 10})

    def flat(out, val):
        iota(out, [[0, out[2]]], int(val), 0)

    def quant(q, s, t):
        op("v", lambda e: V.quantize_mx(q[0], s[0], t[0]), [q, s], [t], (15 + 0.27 * t[2]) * CYC)

    def mm(out, l, ls, m, ms, start=True, stop=True):
        op("t", lambda e: g.tensor.matmul_mx(out[0], l[0], ls[0], m[0], ms[0], start, stop), [out], [l, ls, m, ms], 0.8 * (m[2] + 16), "op" if start else "acc")

    def iota(out, pattern, base, cm):
        flt = SCRATCH[out[1][0][0]][2] != I32
        f = (lambda e: g.iota(out[0], pattern, base, cm, allow_small_or_imprecise_dtypes=True)) if flt else (lambda e: g.iota(out[0], pattern, base, cm))
        op("p", f, [out], [], 130 + 2 * out[2] * CYC)

    def dma(q, sem, out, in_, done, after=(), behind=()):
        return op(q, lambda e: Q[e].dma_start(out[0], in_[0]), [out], [in_] + list(behind), 60, "dma", sem=sem, done=done, after=list(after))

    def hbm(a, name="hbm"):
        return (a, [(name, 0 if name == "hbm" else 1)], 0, False, False)

    def send(pairs, dst, sem, done, behind=(), spare=0):
        rid, pid, _ = topo.addr(dst)
        mask = topo.mask(core, dst) & ~spare
        n = bin(mask).count("1")
        for out, in_ in pairs:
            op("p", lambda e, out=out, in_=in_: g.remote_dma(out[0], in_[0], T.sem[sem], T.sem.ls, pid, rid, mask), [(0, [("sent" + sem, 1)])], [in_] + list(behind), 250 if any(o["kind"] == "send" for o in ops) else 1700, "send", sem=sem, n=n, done=done)

    def arrives(sem, src, outs):
        op("-", None, outs, [(0, [("sent" + sem, 1)])], 0, "arrival", sem=sem, n=len(outs) * len(topo.engines(src, core)))

    pf = lambda k: col("pf", k)
    at = lambda m: C * m
    LW = col("lw", 0, 8)
    L0, LWP, LC, LL, LE, LK, LG, LF = [col("ls_", a, n) for a, n in ((0, 4), (4, 2), (6, 2), (8, 2), (10, 2), (12, 2), (14, 2), (16, 2))]

    def rawv(a, b, c0=0, c1=C):
        return (T.raw[:, a:b, c0:c1], [("raw", sum(bits(C * m + c0, C * m + c1) for m in range(a, b)))], (b - a) * (c1 - c0), False, False)

    iota(col("pi", 11), [[0, 1]], 0, 1)
    ops[-1]["early"] = -3.0
    fill(R("ox"), 0)
    for m in range(8):
        (fill if m == 0 else flat if m == 2 else lambda o, _: zero(o))(rawv(m, m + 1), 0)
        ops[-1]["early"] = m / 32 - 2.9
    own = PARTS[-1][1]
    first = [dma("s", "d16", u8(R("wcs", 0, own)), hbm(T.wc[:, 0:4 * own]), 1800)]
    first = [dma("ys"[k % 2], "d0", hbm(T.tb[k:k + 1, :], "tb"), hbm(T.ar[:, 20 * k:20 * k + 20]), 1800, first) for k in range(4)]
    last = [dma("y", "d12", (T.m0[16 * q:16 * q + 16, :],) + R("m0")[1:], hbm(T.mp[0:16, 0:8]), 1500, first) for q in range(8)]
    last = [dma("y", "d18", col("xi", 0, 640), hbm(T.x[:, 0:640]), 2300, last)]
    for a in (0, 4):
        for q in range(8):
            p0 = 16 * q + (15 if q % 2 == 0 else 0)
            last = [dma("y", "d%d" % (3 + 3 * a), (T.raw[p0:p0 + 1, a:a + 4, :],) + rawv(a, a + 4)[1:], hbm(T.mp[16 * a:16 * a + 64, :]), 1500, last)]
    last = [dma("y", "d2", u8(R("wcs", own, 512)), hbm(T.wc[:, 4 * own:2048]), 2200, last)]
    last = [dma("y", "d1", R("wps"), hbm(T.ws[:]), 2400, last)]
    last = [dma("y", "d4", col("xi", 640, 640), hbm(T.x[:, 640:1280]), 2900, last)]
    heir, giver = T.cores[(r - STEP[HOME]) % N], T.cores[(r + STEP[HOME]) % N]
    for (a, b), mate in zip(PARTS, helpers(core, T, topo)[1]):
        send([(u8(R("wh", a, b)), u8(R("wcs", a, b)))], mate, "aw", 6600)
        ops[-1]["early"] = 2000.0
        ops[-1]["w"], ops[-1]["soon"] = [("sentac", 1)], True
    send([(u8(R("wdc", own, 512)), u8(R("wcs", own, 512))), (R("wdp"), R("wps"))], heir, "ac", 4000)
    ops[-1]["early"] = ops[-2]["early"] = 3000.0
    ops[-1]["soon"] = True
    arrives("ac", giver, [R("wdp"), R("wdc", own, 512)] + [R("wdc", a, b) for a, b in PARTS])

    for k, sh, an in ((0, 0, 15), (1, 4, 1), (2, 5, 1), (3, 6, 1), (4, 0, 1), (5, 1, 1), (6, 2, 1), (7, 0, 7), (8, 2, 3), (9, 4, 7), (10, 0, 31)):
        ts(col("pi", k), col("pi", 11), sh, Op.logical_shift_right, an, Op.bitwise_and)
    cp(col("pf", 0, 12), col("pi", 0, 12))
    i_, h_, y_, b_, x0, x1, x2, g8, i4, g_, p31, p_ = [pf(k) for k in range(12)]
    iota(R("nat"), [[1, 320]], 0, 0)
    ops[-1]["early"] = -2.5
    iota(col("cf", 0, 32), [[0, 4], [1, 8]], 0, 0)
    fma(col("wf", 0, 161), col("nat", 0, 161), 0.0, p_)
    ts(L0, col("nat", 0, 4), 32.0, Op.mult, p31, Op.add)
    for a in range(2):
        zero(blk("ze", a, 258))
    ts(R("ze", 3, 515, 4), col("nat", 0, J), p_, Op.is_equal, 0.5, Op.mult)
    for t in range(4):
        quant(blk("qe", t), blk("se", t), col("ze", 3 - t, 512))
        ops[-1]["early"] = 2500.0
    iota(col("o7", 0, 16), [[0, 16]], 0, 0)
    iota(col("fw", at(8), J), [[0, J]], 0, 0)
    fma(pf(12), x0, -65.0, 64.0)
    fma(pf(13), x1, -95.0, pf(12))
    fma(pf(14), pf(13), h_, x0)
    fma(pf(15), x2, 32.0, 176.0)
    fma(pf(16), x1, 96.0, pf(15))
    fma(pf(17), g_, 160.0, pf(16))
    ts(LWP, R("cf", 0, 16, 8), pf(14), Op.add, pf(17), Op.add)
    ts(pf(18), y_, h_, Op.not_equal)
    fma(pf(19), y_, 32.0, 64.0)
    fma(pf(20), b_, 32.0, 16.0 + 7 * 160)
    times(pf(21), pf(18), pf(19))
    fma(pf(22), i4, -160.0, pf(20))
    fma(pf(23), x2, -1.0, 1.0)
    fma(pf(24), h_, -1.0, y_)
    fma(pf(25), pf(24), pf(23), h_)
    fma(pf(26), pf(24), x2, h_)
    fma(pf(27), pf(21), x2, pf(22))
    fma(pf(28), pf(21), pf(23), pf(22))
    fma(pf(30), x0, 2.0, 156.0)
    fma(pf(31), x1, 1.0, pf(30))
    iota(col("cf", 96, 2), [[-640, 2]], 0, 0)
    ts(LL, col("cf", 96, 2), pf(27), Op.add, pf(25), Op.add)
    ts(LE, col("cf", 96, 2), pf(28), Op.add, pf(26), Op.add)
    fma(pf(32), x1, 1.0, 112.0)
    fma(R("lu"), col("nat", 0, 8), -16.0, pf(32), "v")
    cp(col("lp", 0), p_)
    fma(pf(38), g8, 8.0, 8.0)
    fma(pf(39), g8, 1.0, 2.0)
    ts(pf(42), pf(38), pf(39), Op.mult, -1.0, Op.add)
    ts(LF, R("cf", 0, 16, 8), pf(42), Op.add)
    fma(pf(45), x1, 4.0, x0)
    ts(col("ls_", 22), h_, 2.0, Op.mult, pf(45), Op.add)
    ts(pf(33), x2, h_, Op.not_equal, 144.0, Op.mult)
    fma(pf(34), i4, 16.0, pf(31))
    fma(pf(35), h_, -10.0, -145.0)
    fma(pf(36), pf(35), 1.0, pf(33))
    ts(LK, R("nat", 0, J, 64), pf(34), Op.add, pf(36), Op.add)
    for a in (0, 144):
        iota(col("cg", a, 16), [[0, 16]], 0, 0)
    fma(pf(40), g8, 8.0, 29.0)
    fma(pf(41), g8, -0.125, 17.0)
    fma(pf(43), i_, 0.125, pf(41))
    fma(pf(44), pf(40), g8, pf(43))
    ts(LG, R("nat", 0, 4, 2), pf(44), Op.add)
    for t in range(4):
        iota(R("thr", t, J, 4), [[0, 16], [1, 2]] if t < 2 else [[0, 8], [1, 2], [0, 2]], -(t % 2), 0)
    times(R("thr"), R("thr"), BIG)
    iota(R("ad"), [[0, 32], [1, 4]], 0, 0)
    iota(R("zs"), [[0, 68], [-32, 2]], 0, 0)
    flat(R("zi"), 0)
    flat(col("nw", 0, 4), 0)
    flat(col("hs", 512, 16), 0)
    flat(R("gt"), 0)
    for a, b, st, val in ((4, 72, 4, 1.0), (0, 1, 1, -7.0), (32, 33, 1, 0.0), (36, 72, 32, -4.0), (52, 53, 1, 2.0)):
        flat(R("gt", a, b, st), val)
    xw = lambda k: blk("xw", k, 32)
    fma(xw(0), col("cf", 0, 32), 16.0, i_)
    fma(col("xw", 224, 8), col("xw", 0, 8), 1.0, 1.0 * at(8))
    iota(col("cf", 64, 32), [[1, 4], [0, 8]], 0, 0)
    fma(xw(1), xw(0), -FAR, 1.0 * J)
    fma(xw(3), col("cf", 64, 32), 1.0, 1.0 * XO)
    for a in range(2):
        iota(blk("stp", a, 288), [[0, 288]], int(FAR), 0)
    run = lambda c: 8 * c * c + 13 * c
    for a in range(2):
        iota(blk("ne2", a, 308), [[0, 308]], int(256 * FAR), 0)
        iota(blk("st2", a, 308), [[0, 308]], 0, 0)
    fma(pf(46), i_, -1.0, 15.0)
    for c in range(8):
        ts(col("st2", run(c) + 1, 16), col("nat", 0, 16), pf(46), Op.is_equal, 256 * FAR, Op.mult)
    for t, (a, b) in enumerate(((2.0, 0.0), (0.0, 1.0), (0.0, 255.0), (2.0, 256.0))):
        fma(col("xw", 64 + 8 * t, 8), col("xw", 0, 8), a, b)
    cp(by(R("st2"), LG), xw(2))
    ts(R("idb"), col("nat", 0, J), p_, Op.is_equal)
    iota(R("ci"), [[0, 8], [1, 16]], 0, 0)
    ts(R("mod"), R("ci"), i_, Op.is_equal)
    ts(R("m8"), col("nat", 0, 8), g_, Op.is_equal, 0.5, Op.mult)
    iota(R("ba", 3, 512, 4), [[0, J]], 0, 0)
    iota(R("bb"), [[0, 640]], 0, 0)
    for t, wt in enumerate((-1.0, -32.0, -384.0, 0.0)):
        flat(R("za", t, 512, 4), wt)
    quant(blk("qa", 0), blk("sa", 0), R("za"))
    for t, wt in enumerate((1.0, 32.0, 384.0)):
        op("p", lambda e, t=t, wt=wt: g.affine_select(T.za[:, t:512:4], T.ze[:, 0:512:4], [[-1, J]], Op.is_ge, wt, 0, 1), [R("za", t, 512, 4)], [R("ze", 0, 512, 4)], 170 + 2 * J * CYC)
    quant(blk("qa", 1), blk("sa", 1), R("za"))
    ops[-1]["early"] = EARLY
    for t in range(2):
        flat(R("zb", t, 516, 4), 0)
    for n, wts in enumerate(((1.0, 32.0), (1.0 * C, 1.0 * C))):
        for t in range(2):
            times(R("zb", 2 + t, 514, 4), R("mod"), wts[t])
        quant(blk("qb", n), blk("sb", n), col("zb", 2 - 2 * n, 512))
        ops[-1]["early"] = EARLY

    for a in (0, 4):
        for i in range(16):
            o, v = R("fw", at(a) + i, at(a + 4), 16), rawv(a, a + 4, 20 * i, 20 * i + 20)
            either(o, v, lambda o=o, v=v: V.tensor_copy(o[0], v[0]), lambda o=o, v=v: S.activation(o[0], v[0], Act.Copy))
    for a in (0, 4):
        for q in range(8):
            p0 = 16 * q + (11 if q % 2 == 0 else 1)
            last = [dma("y", "d%d" % (13 + a), (T.raw[p0:p0 + 4, a:a + 4, :],) + rawv(a, a + 4)[1:], hbm(T.tb[:, C * a:C * a + 4 * C], "tb"), 2500, last)]

    def chase(known=False):
        for s in range(8):
            win = col("fw", at(s), C)
            lst = [col("ls_", 2 * b, 2) if s == 0 else col("l1", 2 * b, 2) if s == 1 and known else col("wu", 160 * s + 16 + 32 * b, 2) for b in range(2)]
            rows, at0, turned = ("ox", 80 * s, "wu") if s < 7 else ("o7", 0, "wf")
            for b in range(2):
                times(col(rows, at0 + 16 + 32 * b, 32), by(win, lst[b]), 1.0)
            tr(col(turned, 160 * s + 161, 64), col(rows, at0 + 16, 64))
            tr(col(turned, 160 * s + 225, 96 if s < 7 else 64), col(rows, at0, 96 if s < 7 else 64))
            if s < 7:
                times(col("wf", 160 * s + 161, 160), col("wu", 160 * s + 161, 160), 1.0, "s")
        cp(R("lw"), by(R("wf"), col("ls_", 4)))

    def asks(k):
        cc, d = R("zi", 71, 135, 2), col("pw", 0, 32)
        times(R("zi", 3, 67, 2), by(R("wf", 0, 1281), LE), 1.0, "v")
        e, a, b = R("zi", 3, 67, 8), col("pw", 40, 8), col("pw", 48, 8)
        ts(R("hi"), e, -7.5, Op.add, 1 / 16, Op.mult)
        times(a, e, 20.0)
        times(b, R("hi"), 1.0 - C)
        tt(R("le", 0, 16, 2), a, b, Op.add)
        for c in range(8):
            times(col("cg", 16 + 16 * c, 16), by((T.raw[:, 7 - c, :],) + rawv(7 - c, 8 - c)[1:], col("le", 2 * c)), 1.0)
        tr(col("ct", 0, J), col("cg", 16, J))
        tr(col("ct", J, 160), R("cg"))
        times(cc, by(R("ct"), LK), 1.0, "v")
        tt(d, by(R("wf", 160), LL), cc, Op.subtract)
        for a in range(2):
            ts(R("thr", 5 * a, J, 8), R("pw", a, 32, 2), 0.0, Op.is_equal, BIG * (2 * a - 1), Op.mult)
        ts(R("zi", 0, 136, 2), R("zi", 1, 136, 2), 1 / 32, Op.mult)
        scan(R("zd"), R("zs"), R("zi"), Op.mult, Op.add)
        for a in (0, 68):
            tt(col("dd", a, 66), col("zd", a, 66), col("zd", a + 2, 66), Op.subtract)
        tt(col("dd", 134, 2), col("zd", 56, 2), col("zd", 126, 2), Op.subtract)

    def unpack(bank, w, q, s, planes=range(4)):
        for t in planes:
            mm(ps(bank + t, 0, w), blk("qe", t), blk("se", t), q, s)

    def fh(k, t, w=C):
        return col("fh", (C + J) * (4 * (k % 2) + t + 1) - w, w)

    def state(k, tile):
        for a in range(2):
            quant(blk("qx", a, 160), blk("sx", a, 160), col(tile[0], tile[1] + 640 * a, 640))
        unpack(0, C, R("qx"), R("sx"))
        for t in range(4):
            times(fh(k, t), ps(t, 0, C), 1.0)

    for a in range(2):
        q, sp = blk("qx", a, 160), blk("sx", a, 160)
        quant(q, sp, blk("xi", a, 640))
        unpack(4 * a, 160, q, sp)
        for t in range(4):
            times(col("fh", (C + J) * t + J + 160 * a, 160), ps(4 * a + t, 0, 160), 1.0)
    cp(R("l1"), by(R("m0"), col("ls_", 22)))
    chase(True)
    ops[-1]["soon"] = True
    dma("y", "d5", R("ui"), hbm(T.u[:]), 3000, last)
    quant(R("qu0"), R("su0"), R("ui"))
    word = lambda v: (v[0].bitcast(dt.uint32),) + v[1:]
    cp(word(R("qu")), by(word(R("qu0")), R("lu")))
    op("s", lambda e: S.activation(T.su[:], T.su0[:].indirect(T.lu[:]), Act.Copy), [R("su")], [R("su0"), R("lu")], 270.0)
    for k in range(3):
        donor, client = T.cores[(r + STEP[k]) % N], T.cores[(r - STEP[k]) % N]
        qm, sp, qh, sh = [R("%s%d" % (n, k)) for n in ("qm", "sm", "qh", "sh")]
        asks(k)
        if k:
            quant(R("qn"), R("sn"), R("nt"))
            unpack(0, J, R("qn"), R("sn"))
            for t in range(4):
                times(blk("dn", t), ps(t, 0, J), 1.0)
        for t in range(4):
            times(R("mt", t, 512, 4), by(blk("dn", t), col("fl", 0, 8)) if k else by(fh(0, t), LW), 2.0)
        quant(qm, sp, R("mt"))
        mc, mp, wc, wp, hc, hp = qm, sp, "wdc", "wdp", qh, sh
        x = 1 + k - (k > HOME)
        if k != HOME:
            mc, mp, wc, wp, hc, hp = R("mc%d" % x), R("mp_%d" % x), "wcs", "wps", R("hc%d" % x), R("hp%d" % x)
            send([(u8(mc), u8(qm)), (mp, sp)], donor, "am%d" % x, 2100)
            arrives("am%d" % x, client, [mc, mp])
        if k:
            state(k, ("xt", XO))
            for t in range(4):
                cp(by(fh(k, t, C + J), col("xl", 0, 8)), blk("dn", t))
        for t in range(4):
            times(R("xt", XO + t, XO + 4 * C, 4), fh(k, t), 2.0)
        for b in range(4):
            mm(ps(4 + b, 0, J), blk(wc, b), blk(wp, b), mc, mp)
        for b in range(4):
            o, i = R("ht", b, 512, 4), ps(4 + b, 0, J)
            either(o, i, lambda o=o, i=i: V.tensor_scalar(o[0], i[0], 0.0, 0.03125, Op.max, Op.mult), lambda o=o, i=i: S.activation(o[0], i[0], Act.Relu, scale=0.03125))
        quant(qh, sh, R("ht"))
        if k != HOME:
            send([(u8(hc), u8(qh)), (hp, sh)], client, "ah%d" % x, 2100)
            arrives("ah%d" % x, donor, [hc, hp])
        if k == 0:
            dma("y", "d6", R("vi"), hbm(T.v[:]), 2500, (), [hc])
            quant(R("qv"), R("sv"), R("vi"))
        mm(ps(4, 0, J), hc, hp, R("qu"), R("su"))
        unpack(0, J, hc, hp)
        for t in range(2):
            times(blk("dh", t), ps(t, 0, J), 1.0, "s")
        for a, o in ((0, Op.is_gt), (1, Op.is_le)):
            tt(R("sg", a, J, 2), ps(4, a, J, 2), R("thr", a, J, 2), o)
        scan(col("nw", 4, J), R("ad"), R("sg"), Op.min, Op.max)
        dg = lambda t: col("hs", 512 + t)
        for t, d in ((4, R("dd", 1, 67, 2)), (5, R("dd", 0, 66, 2)), (8, col("gt", 36, 33)), (9, R("dd", 69, 135, 2)), (10, R("dd", 68, 134, 2)), (6, col("gt", 0, 33))):
            scan(R("hs", t, 528, 16), R("nw", 3, 132, 4), d, Op.mult, Op.add)
        for t in range(2):
            scan(R("hs", 464 + t, 528, 16), R("nw", 119, 132, 4), R("dd", 127 - t, 134, 2), Op.mult, Op.add, col("dd", 135 - t))
        for t, c in enumerate((4, 5, 8)):
            times(R("ba", t, 512, 4), R("idb"), dg(c))
        quant(R("qk"), R("sk"), R("ba"))
        mm(ps(5, 0, J), blk("qa", 1), blk("sa", 1), R("qk"), R("sk"), True, False)
        mm(ps(5, 0, J), R("qk"), R("sk"), blk("qa", 0), blk("sa", 0), False, True)
        red(sm("lo", 0, 1), ps(5, 0, J), Op.min, apply_absolute_value=True)
        for t in range(2):
            times(R("bb", t, 512, 4), R("idb"), dg(9 + t))
        cp(by(R("bb", 512), col("lp", 0)), col("hs", 512, 16))
        quant(R("qw"), R("sw"), R("bb"))
        mm(ps(7, 0, J), blk("qb", 0), blk("sb", 0), col("qw", 32, J), col("sw", 32, J))
        mm(ps(6, 0, J), blk("qa", 0), blk("sa", 0), col("qw", 0, J), col("sw", 0, J))
        times(R("nv"), ps(6, 0, J), -1.0)
        times(col("z0", 16, 8), ps(7, 96, J, 4), 1.0)
        times(R("l1"), by(col("z0", 16, 8), col("ls_", 22)), 1.0)
        ts(R("bb", 519, 640, 16), R("m8"), sm("lo", 0, 1), Op.is_gt, 16.0, Op.mult)
        quant(R("ql"), R("sl"), col("bb", J, 512))
        mm(ps(4, 0, J), blk("qb", 0), blk("sb", 0), col("qw", 32, J), col("sw", 32, J), True, False)
        mm(ps(4, 0, J), blk("qb", 1), blk("sb", 1), R("ql"), R("sl"), False, True)
        tt(R("ofs"), ps(4, 97, J, 4), col("xw", 224, 8), Op.min)
        cp(by(R("fw"), R("ofs")), R("nv"))
        for m in range(8 if k == 2 else 0):
            dma("y", "d7", hbm(T.fo[m:m + 1, :]), (T.fw[15:16, at(m):at(m) + C],) + col("fw", at(m), C)[1:], 1500)
        chase(True)
        for t in range(4):
            nt = blk("nt", t) if k == 2 else R("nt", t, 512, 4)
            if t < 2:
                tt(nt, by(fh(k, t), LW), blk("dh", t), Op.add)
            else:
                times(blk("fg", t - 2), by(fh(k, t), LW), 1.0, "s")
                tt(nt, ps(t, 0, J), blk("fg", t - 2), Op.add)
        times(sm("nl"), by(R("wf"), col("ls_", 4)), -256 * FAR)
        times(sm("lf"), by(R("wf"), col("ls_", 4)), 1.0)
        times((T.lrow[:, ::-1],) + R("lrow")[1:], by(R("nat"), LW), 1.0)
        for c in range(7, -1, -1):
            o, i, a, b = col("ne", 8 * c * (c + 1), 16 * c + 16), R("lrow", 112 - 16 * c), sm("lf", c, c + 1), sm("nl", c, c + 1)
            if k == 2:
                o = col("ne2", run(c), 16 * c + 16)
            either(o, i, lambda o=o, i=i, a=a: V.tensor_scalar(o[0], i[0], a[0], 256 * FAR, Op.not_equal, Op.mult),
                   lambda o=o, i=i, b=b: S.activation(o[0], i[0], Act.Abs, bias=b[0], scale=256 * FAR), [a, b])
        times(xw(4), by(R("wf"), LWP), 4.0 if k == 2 else 1.0)
        tt(xw(5), xw(4), xw(3 if k == 2 else 1), Op.add)
        if k < 2:
            scan(col("so", 0, 576), R("stp"), R("ne"), Op.add, Op.min)
            ts(R("fl"), by(col("so", 0, 576), col("ls_", 16)), 1 / FAR, Op.mult)
            tt(xw(6), by(col("so", 0, 576), LF), xw(5), Op.add)
            tt(col("xl", 0, 8), col("xw", 192, 8), col("xw", 0, 8), Op.max)
        else:
            scan(R("so"), R("st2"), R("ne2"), Op.add, Op.min)
            tt(R("xl"), by(R("so"), LG), xw(5), Op.min)
    cp(by(R("xt"), R("xl")), R("nt"))
    quant(R("qx"), R("sx"), col("xt", XO, 4 * C))
    dma("y", "d8", hbm(T.oc[:]), u8(R("qx")), 1800)
    for a in range(2):
        mm(ps(4 + a, 0, 160), R("qv"), R("sv"), blk("qx", a, 160), blk("sx", a, 160))
        times(blk("yo", a, 160), ps(4 + a, 0, 160), 1.0, "vs"[a])
        dma("ys"[a], "d%d" % (9 + a), hbm(T.y[:, 160 * a:160 * a + 160]), blk("yo", a, 160), 1600)
    for i in range(4):
        dma("y", "d11", hbm(T.osc[4 * i:4 * i + 4, :]), (T.sx[32 * i:32 * i + 4, :],) + R("sx")[1:], 1400)
    return ops


def orders(ops):
    seen, out, group = {}, [], {}
    alike = lambda a, b: a["kind"] == b["kind"] and (a["kind"] == "send" or (a["kind"] == "dma" and a["sem"] == b["sem"]))
    for i, o in enumerate(ops):
        if o["kind"] == "dma":
            group.setdefault(o["sem"], []).append(i)
    for i, o in enumerate(ops):
        p = set()
        for writes, keys in ((False, o["r"]), (True, o["w"])):
            for name, m in keys:
                for j, m2, w2 in seen.get(name, []):
                    if m & m2 and (writes or w2 or (name[0] == "#" and (len(o["q"]) > 1 or o["q"] != ops[j]["q"]))):
                        if not alike(o, ops[j]):
                            p.add(j)
        for name, m in o["w"]:
            seen[name] = [x for x in seen.get(name, []) if x[1] & ~m or alike(o, ops[x[0]])] + [(i, m, True)]
        for name, m in o["r"]:
            seen.setdefault(name, []).append((i, m, False))
        p.discard(i)
        out.append({k for j in p for k in (group[ops[j]["sem"]] if ops[j]["kind"] == "dma" else [j])})
    return out


def plan(ops, before):
    n = len(ops)
    cost = lambda x, e: x[e] if isinstance(x, dict) else x
    pre, post = [[] for _ in ops], [[] for _ in ops]
    for i, o in enumerate(ops):
        for j in before[i]:
            pre[i].append((j, 0.0 if o["kind"] == "arrival" or (o["kind"] == "acc" and ops[j]["q"] == "t") else WAKE))
        pre[i] += [(j, None) for j in o.get("after", [])]
        for j, w in pre[i]:
            post[j].append((i, w))

    def lay(order, back):
        busy, start, eng = {}, {}, {}
        for i in order:
            o, best = ops[i], None
            for e in o["q"]:
                d, full = cost(o["hold"], e), cost(o["done"], e)
                if back:
                    t = max([start[j] + cost(ops[j]["hold"], eng[j]) + (1 if w is None else w + full) - d for j, w in post[i]] + [full - d])
                else:
                    t = max([start[j] + (1 if w is None else w + cost(ops[j]["done"], eng[j])) for j, w in pre[i]] + [0.0])
                for a, b in busy.get(e, []):
                    if t + d <= a:
                        break
                    t = max(t, b)
                if best is None or t + d < best[0] + best[1]:
                    best = (t, d, e)
            start[i], d, eng[i] = best
            if d:
                busy[eng[i]] = sorted(busy.get(eng[i], []) + [(start[i], start[i] + d)])
        return start, eng

    rest = [0.0] * n
    for i in range(n - 1, -1, -1):
        rest[i] = cost(ops[i]["done"], ops[i]["q"][0]) + max([rest[j] + WAKE for j, _ in post[i]] + [0.0])
    key, best = [max(rest) - x for x in rest], None
    for _ in range(PASSES):
        for i in range(n - 1, -1, -1):
            key[i] = min([key[i], ops[i].get("early", key[i])] + [key[j] - 1e-3 for j, _ in post[i]])
        start, eng = lay(sorted(range(n), key=lambda k: (key[k], k)), False)
        end = [start[i] + cost(ops[i]["done"], eng[i]) for i in range(n)]
        if best is None or max(end) < best[0]:
            best = (max(end), start, eng)
        for i in range(n - 1, -1, -1):
            key[i] = max([-end[i]] + [key[j] + 1e-3 for j, _ in post[i]])
        back, beng = lay(sorted(range(n), key=lambda k: (key[k], -k)), True)
        last = [back[i] + cost(ops[i]["hold"], beng[i]) for i in range(n)]
        key = [max(last) - x for x in last]
    _, start, eng = best
    return mend(ops, before, [(i, eng[i]) for i in sorted(range(n), key=lambda k: (start[k], k))])


def mend(ops, before, seq):
    n = len(ops)
    cost = lambda x, e: x[e] if isinstance(x, dict) else x
    pre = [[(j, 0.0 if o["kind"] == "arrival" or (o["kind"] == "acc" and ops[j]["q"] == "t") else 1.0) for j in before[i]] for i, o in enumerate(ops)]
    hard = [set(before[i]) | set(o.get("after", [])) for i, o in enumerate(ops)]
    post = [[] for _ in ops]
    for i in range(n):
        for j in hard[i]:
            post[j].append(i)
    tab = [[{e: (cost(o["hold"], e) * f, cost(o["done"], e) * f) for e in o["q"]} for o in ops for f in [s / CYC if o["kind"] in ("op", "acc") else 1.0]] for s, _ in PACES]

    soon = [i for i, o in enumerate(ops) if o.get("soon")]

    def run(seq, k, old=None, a=0):
        w, tb = PACES[k][1], tab[k]
        a -= a % 32
        end, why, marks = (list(old[0]), list(old[1]), old[2][:a // 32 + 1]) if old else ([0.0] * n, [None] * n, [({}, {})])
        free, last = dict(marks[-1][0]), dict(marks[-1][1])
        for p in range(a, n):
            if p % 32 == 0 and p > a:
                marks.append((dict(free), dict(last)))
            i, e = seq[p]
            t, c = free.get(e, 0.0), last.get(e)
            for j, f in pre[i]:
                if end[j] + f * w > t:
                    t, c = end[j] + f * w, j
            h, d = tb[i][e]
            end[i], why[i] = t + d, c
            if h:
                free[e], last[e] = t + h, i
        return end, why, marks

    total = lambda runs: sum(max(x[0]) + 0.3 * sum(x[0][i] for i in soon) + 1e-3 * sum(x[0]) for x in runs)
    now = [run(seq, k) for k in range(len(PACES))]
    rng, best, path, pos = np.random.RandomState(1), total(now), [], {}
    for m in range(MOVES):
        if m % 20 == 0 or not path:
            end, why, _ = now[m // 20 % len(PACES)]
            path = [end.index(max(end)) if m % 80 else soon[m // 80 % len(soon)]]
            while why[path[-1]] is not None:
                path.append(why[path[-1]])
        pos = pos or {i: p for p, (i, _) in enumerate(seq)}
        a = min(n - 1, max(0, pos[path[int(rng.randint(len(path)))]] + int(rng.randint(-10, 11))))
        i, e = seq[a]
        if ops[i]["kind"] in ("dma", "send"):
            continue
        if len(ops[i]["q"]) > 1 and rng.rand() < 0.4:
            e = ops[i]["q"].replace(e, "")
        lo, hi = max([pos[j] for j in hard[i]] + [-1]) + 1, min([pos[j] for j in post[i]] + [n]) - 1
        b = int(rng.randint(lo, hi + 1)) if rng.rand() < 0.1 else min(hi, max(lo, a + int(rng.randint(-14, 15))))
        new = seq[:a] + seq[a + 1:]
        new.insert(b, (i, e))
        runs = [run(new, k, now[k], min(a, b)) for k in range(len(PACES))]
        t = total(runs)
        if t <= best + max(0.0, HEAT * (1 - m / (0.8 * MOVES)) * rng.rand() ** 2):
            seq, now, pos, best, path = new, runs, {}, t, path if t == best else []
    return seq


def helpers(core, T, topo):
    heir = T.cores[(T.rank_of(core) - STEP[HOME]) % len(T.cores)]
    free = [c for c in topo.cores_of(core) if T.rank_of(c) is None and topo.may_write(c, heir)]
    return heir, sorted(free, key=lambda c: (topo.die(c) == topo.die(core), c))[:len(PARTS)]


def hand_on(g, core, T, topo):
    for home in T.cores:
        heir, mates = helpers(home, T, topo)
        if core in mates:
            a, b = PARTS[mates.index(core)]
            rid, pid, _ = topo.addr(heir)
            g.wait_ge(T.sem.aw, len(topo.engines(home, core)))
            g.remote_dma(T.wdc[:, a:b].bitcast(dt.uint8), T.wh[:, a:b].bitcast(dt.uint8), T.sem.ac, T.sem.ls, pid, rid, topo.mask(core, heir))
            g.wait_ge(T.sem.ls, len(topo.engines(core, heir)))


def rank_program(g, core, T, topo):
    if T.rank_of(core) is None:
        return hand_on(g, core, T, topo)
    ops = program(g, core, T, topo)
    before = orders(ops)
    Q = {"v": g.vector, "s": g.scalar, "t": g.tensor, "p": g, "y": g.sync}
    known, tot, token = {q: {} for q in Q}, {}, {}
    for o in ops:
        if o["kind"] == "dma":
            tot[o["sem"]] = tot.get(o["sem"], 0) + 16
        elif o["kind"] == "arrival":
            tot[o["sem"]] = o["n"]
        elif o["kind"] == "send":
            tot["ls"] = tot.get("ls", 0) + o["n"]
    if not ORDER:
        ORDER.extend(plan(ops, before))
    for i, e in ORDER:
        o = ops[i]
        if o["kind"] == "arrival":
            token[i] = (o["sem"], o["n"], {})
            continue
        want = {}
        for j in before[i]:
            if j not in token or (o["kind"] == "acc" and ops[j]["q"] == "t" and ops[j]["w"] == o["w"]):
                continue
            s, val, snap = token[j]
            if val > want.get(s, (0, None))[0]:
                want[s] = (val, snap)
        for s in sorted(want, key=lambda m: (-len(want[m][1]), m)):
            val, snap = want[s]
            if known[e].get(s, 0) < val:
                Q[e].wait_ge(T.sem[s], val)
                known[e][s] = val
                for a, b in snap.items():
                    known[e][a] = max(known[e].get(a, 0), b)
        ins = o["f"](e)
        if o["kind"] == "dma":
            ins.then_inc(T.sem[o["sem"]], 16)
            token[i] = (o["sem"], tot[o["sem"]], dict(known[e]))
        elif o["kind"] != "send":
            tot[e] = tot.get(e, 0) + 1
            ins.then_inc(T.sem[e], 1)
            token[i] = (e, tot[e], dict(known[e]))
    for sem in sorted(tot):
        if known["p"].get(sem, 0) < tot[sem]:
            g.wait_ge(T.sem[sem], tot[sem])
